import numpy as np, ml_dtypes
CORES = [40,41,42,43,44,45,46,47]
N = 8
import mx_ref
BF = ml_dtypes.bfloat16
def gentries(a):
    return np.ascontiguousarray(a.reshape(8, 16, -1).transpose(0, 2, 1)).reshape(8, -1)
def gtable(e):
    e = np.asarray(e); return np.ascontiguousarray(e.reshape(8, -1, 16).transpose(0, 2, 1)).reshape(128, -1).astype(np.int32)
def gcols(t, e):
    v = np.concatenate([t.reshape(8, 16, -1, 4), np.zeros((8, 16, 1, 4), BF)], axis=2)
    return np.ascontiguousarray(np.stack([v[g][:, e[g]] for g in range(8)])).reshape(128, -1)
def tile(rs):
    return np.stack(rs, axis=2).reshape(128, -1).astype(BF)
def pick(q, e):
    c = np.concatenate([q[0].reshape(128, -1, 4), np.zeros((128, 1, 4), np.uint8)], axis=1); s = np.concatenate([q[1], np.ones((16, 1), np.uint8)], axis=1)
    return (np.ascontiguousarray(c[:, e].reshape(128, -1)), np.ascontiguousarray(s[:, e]))
def join(*qs):
    return (np.concatenate([q[0] for q in qs], axis=1), np.concatenate([q[1] for q in qs], axis=1))
def put(q, e, v):
    c, s = q[0].reshape(128, -1, 4).copy(), q[1].copy(); c[:, e] = v[0].reshape(128, -1, 4); s[:, e] = v[1]
    return (c.reshape(128, -1), s)
def pk(c, s):
    return (np.ascontiguousarray(c), mx_ref.live(s))
def emit(q):
    return q[0], q[1]
def packed(v, rng):
    q = [mx_ref.quantize(np.ascontiguousarray(v[r])) for r in range(N)]
    return np.stack([a for a, b in q]), np.stack([mx_ref.plane(b, rng) for a, b in q])
def values_of_codes():
    e, c = np.zeros((128, 128, 4), np.float32), np.zeros((128, 2, 4), np.uint8)
    e[np.arange(128), np.arange(128), 0] = 1
    c[:127, :, 0] = np.arange(256).reshape(2, 128).T[:127]
    return mx_ref.matmul(mx_ref.quantize(e.reshape(128, 512).astype(BF)), (c.reshape(128, 8), np.full((16, 2), 127, np.uint8))).T.reshape(-1).astype(np.float64)
CODE_VALUE, SCALE_VALUE = values_of_codes(), 2.0 ** (np.arange(256) - 127.0)
def decode(q):
    return (CODE_VALUE[q[0]].reshape(16, 8, -1, 4) * SCALE_VALUE[q[1]][:, None, :, None] + 0.0).reshape(128, -1).astype(np.float32)
def f(rng, *shape):
    return mx_ref.flush((rng.standard_normal(shape, dtype=np.float32) * np.exp2(rng.integers(-2, 3, shape[:-1] + (1,)))).astype(BF))
def wide(rng, *shape, cols=0):
    v = rng.standard_normal(shape, dtype=np.float32) * np.exp2(rng.integers(-12, 13, shape)).astype(np.float32)
    if cols: v *= np.repeat(np.exp2(rng.integers(-cols, cols + 1, shape[:-2] + (1, shape[-1] // 4))) * (rng.random(shape[:-2] + (1, shape[-1] // 4)) > 0.0625), 4, axis=-1).astype(np.float32)
    return mx_ref.flush(v.astype(BF))
C, H, R = 448, 32, 2
def score(a, b):
    e = np.zeros((8, 16, 8, 16, 4), np.float32)
    for g in range(8): e[g, :, g] = 1
    z = (a.astype(np.float32) * b.astype(np.float32)).astype(BF)
    return mx_ref.matmul(mx_ref.quantize(e.reshape(128, 512).astype(BF)), mx_ref.quantize(z))[::16] + np.float32(0.0)
def big(v, k, low):
    v = v.astype(np.float32) * np.float32(k)
    v[np.abs(v) < np.float32(low)] = 0
    return v.astype(BF)
def state(rng):
    return big(f(rng, N, 128, 4 * C), 16, 2.0 ** -12)
def any_lists(rng):
    return rng.integers(0, C, (N, 8, 2, C)), rng.integers(0, N * H, (N, 8, C))
def unit():
    w = np.zeros((128, 4, 128, 4), np.float32)
    i = np.arange(128)
    for b in range(4): w[i, b, i, b] = 32
    return w.reshape(128, 2048).astype(BF)
def pack(rng, x, a, b, k=1, still=None):
    w = big(f(rng, N, 128, 2048), k, 2.0 ** -16)
    if still is not None: w[still] = unit()
    c, p = packed(w, rng)
    return {"x": x, "c1": np.stack([gtable(e.reshape(8, 2 * C)) for e in a]), "c2": np.stack([gtable(e) for e in b]), "v": np.array(f(rng, N, 128, 512)), "wc": c, "ws": p}
def signs(rng):
    return np.stack([rng.permutation(8) % 2 * 2.0 - 1.0 for r in range(N)])
def halves(rng):
    a, b = any_lists(rng)
    q, k, w = [np.zeros((N, 8, C // 2), int) for i in range(3)]
    for r in range(N):
        for g in range(8):
            o = rng.permutation(C)
            q[r, g], k[r, g] = o[:C // 2], o[C // 2:]
            c = 2 * rng.permutation(C // 4)[:H] + 1
            w[r, g] = rng.permutation(np.concatenate([c, c, c, rng.choice(c, C // 2 - 3 * H)]))
            i = rng.permutation(C // 2) % 2
            for n in range(2):
                a[r, g, n, q[r, g]] = k[r, g][np.where(i == n, w[r, g], w[r, g] - 1)]
                a[r, g, n, k[r, g]] = rng.permutation(q[r, g])
    return a, b, q, k, w
def setup_inputs(rng):
    a, b = any_lists(rng)
    return pack(rng, state(rng), a, b)
def setup_inputs_ties(rng):
    x = state(rng)
    e = rng.permutation(N)
    for r in range(N):
        k = np.zeros(C, int) if r == e[0] else rng.permutation(C) % 3
        t = x[r].reshape(128, C, 4)[:, :3].copy()
        t[:, 2] = 0
        x[r] = t[:, k].reshape(128, 4 * C)
    x[e[1]] = 0
    a, b = any_lists(rng)
    return pack(rng, x, a, b)
def setup_inputs_near(rng):
    a, b, q, k, w = halves(rng)
    s = signs(rng)
    d = ((np.arange(C // 2)[:, None] >> np.arange(8)) & 1) * np.exp2(np.arange(8) - 12.0)
    x = np.zeros((N, 8, 16, C, 4))
    z = np.zeros((8, N * H), int)
    for r in range(N):
        for g in range(8):
            m, i, j = rng.integers(4, 8, (13, C // 2, 4)) * rng.choice([-1.0, 1.0], (13, C // 2, 4)), q[r, g], k[r, g]
            p = x[r, g]
            p[0, i, 0] = s[r, g]
            p[0, j, 0] = 1
            p[8:10, i] = 2.0 ** -11
            p[8, j] = d[:, :4]
            p[9, j] = d[:, 4:]
            p[1:4, i] = m[:3] * 0.25
            p[4:8, j] = m[3:7] * 0.25
            p[10:13, i] = m[7:10] * 2.0 ** -9
            p[13:16, j] = m[10:] * 2.0 ** -9
            t, n = np.zeros(C, int), np.zeros(C, int)
            t[i] = j[w[r, g]]
            t[j] = a[r, g, 0, j]
            n[j] = np.arange(C // 2)
            z[g, H * r:H * r + H] = n[np.argsort(-np.bincount(t, minlength=C), kind="stable")[:H]]
    for g in range(8):
        o = np.argsort(z[g], kind="stable")
        t = np.argsort(o)
        for r in range(N): b[r, g, q[r, g]] = o[t[b[r, g, k[r, g][w[r, g]]]] ^ 1]
    return pack(rng, x.astype(np.float32).reshape(N, 128, 4 * C).astype(BF), a, b)
def setup_inputs_huge(rng):
    a, b, q, k, w = halves(rng)
    s = signs(rng)
    c = int(rng.integers(N))
    s[c] = 1
    b = rng.choice(np.flatnonzero(np.arange(N * H) // H != c), (N, 8, C))
    x = np.zeros((N, 8, 16, C, 4))
    odd = np.arange(C // 2) % 2 == 1
    for r in range(N):
        for g in range(8):
            x[r, g][:, q[r, g]] = s[r, g] * (1 + 0.25 * rng.random((16, C // 2, 4)))
            x[r, g][:, k[r, g]] = np.where(odd == (s[r, g] > 0), 1.5, 1.0)[None, :, None] + 0.25 * rng.random((16, C // 2, 4))
    x[c] *= -(2.0 ** -26)
    for g in range(8):
        i = np.concatenate([q[c, g], k[c, g][np.arange(C // 2) % 4 < 2]])
        b[c, g, i] = H * c + rng.integers(0, H, len(i))
    return pack(rng, (x * 2.0 ** 14).astype(np.float32).reshape(N, 128, 4 * C).astype(BF), a, b, 2.0 ** -3, c)
def setup_inputs_star(rng):
    a, b = any_lists(rng)
    e = rng.permutation(N)
    a[e[0]] = rng.integers(0, C, (8, 1, 1))
    b[e[0]] = rng.integers(0, N * H, (8, 1))
    for g in range(8):
        a[e[1], g] = rng.permutation(C)
        t, i = rng.permutation(C)[:2], rng.integers(0, 2, C)
        a[e[2], g, 0], a[e[2], g, 1] = t[i], t[1 - i]
    a[e[3]] = C - 1 - np.minimum(C - 1, (C * rng.random((8, 2, C)) ** 4).astype(int))
    b[e[1]] = H * e[1] + rng.integers(0, H, (8, C))
    b[e[2]] = H * e[3] + rng.integers(0, H, (8, C))
    return pack(rng, state(rng), a, b)
def setup_inputs_spread(rng):
    a, b = any_lists(rng)
    return pack(rng, big(wide(rng, N, 128, 4 * C, cols=2), 2.0 ** -3, 2.0 ** -12), a, b)
def check_inputs(d):
    b = []
    for k in ("x", "v"):
        a = np.abs(d[k].astype(np.float32))
        if not (np.isfinite(a).all() and ((a == 0) | (a >= 2.0 ** -30) & (a <= 2.0 ** 30)).all()): b.append("a value of " + k)
    for k, n in (("c1", C), ("c2", N * H)):
        if not ((d[k] >= 0) & (d[k] < n)).all(): b.append("an entry of " + k)
    if ((d["wc"] & 127) == 127).any(): b.append("a code of wc")
    s = np.stack([mx_ref.live(p) for p in d["ws"]])
    if not ((s >= 1) & (s <= 157)).all(): b.append("a scale of ws")
    return b
def reference(x, c1, c2, v, wc, ws):
    now = [x[r] for r in range(N)]
    hl = np.zeros((N, 8, R * H), np.float32)
    for t in range(R):
        points, hubs = [], []
        for r in range(N):
            e = gentries(c1[r])
            e0, e1 = e[:, :C], e[:, C:]
            p = np.where(score(now[r], gcols(now[r], e1)) > score(now[r], gcols(now[r], e0)), e1, e0)
            n = np.stack([np.bincount(p[g], minlength=C) for g in range(8)])
            h = np.argsort(-n, axis=1, kind="stable")[:, :H]
            points.append(p)
            hubs.append(mx_ref.quantize(gcols(now[r], h)))
            hl[r, :, H * t:H * t + H] = h
        slots = decode(join(*hubs)).astype(BF)
        for r in range(N):
            a0 = gentries(c2[r])
            a1 = np.take_along_axis(a0, points[r], axis=1)
            a = np.where(score(now[r], gcols(slots, a1)) > score(now[r], gcols(slots, a0)), a1, a0)
            m = ((now[r].astype(np.float32) + gcols(slots, a).astype(np.float32)) * np.float32(0.5)).astype(BF)
            q, w = mx_ref.quantize(m), pk(wc[r], ws[r])
            now[r] = tile([mx_ref.matmul(pick(w, np.arange(128 * b, 128 * b + 128)), q) * np.float32(0.03125) for b in range(4)])
    y = np.zeros((N, 128, C), np.float32)
    oc, osc = np.zeros((N, 128, 4 * C), np.uint8), np.zeros((N, 16, C), np.uint8)
    for r in range(N):
        q = mx_ref.quantize(now[r])
        y[r] = mx_ref.matmul(mx_ref.quantize(v[r]), q)
        oc[r], osc[r] = emit(q)
    return {"y": y, "hl": hl, "oc": oc, "osc": osc}

@@ -1,0 +1,423 @@
+from concourse.bass import DstId, RemoteDMATransfer
+from concourse.mybir import dt, AluOpType, AxisListType, ActivationFunctionType
+
+C, H, R, N = 448, 32, 2, 8
+HC = C // 2
+KC = C // 16
+NH = N * H
+MA = 256
+NS = 2
+PRE = False
+Q8, U8, BF, F32, I32, U16 = "float8_e4m3fn_x4", "uint8", "bfloat16", "float32", "int32", "uint16"
+
+SCRATCH = {}
+
+
+def _sb(dtype, **kw):
+    for k, n in kw.items():
+        SCRATCH[k] = ("sbuf", [128, n], dtype)
+
+
+_sb(BF, xa=4 * C, xb=4 * C, xc=4 * C, xh=4 * C, xd=4 * C, z0=4 * C, z1=4 * C, mt=4 * C, ft=4 * NH, fh=4 * NH,
+    vt=512, one=512, pm1=1024, et=2048, sel=512, bd=640, th=1024, bt=512, bu=128, i16=C, thr=C, keep=C, diag=C,
+    ib=HC, mask=C, msc=C, hw=2 * KC, oh=7 * 4 * HC, ab=NS * 4 * HC, cls=C, ind=2 * C, cum=2 * C, junk=3 * C + 64,
+    c2row=C, am=C, asc=C, pre=8 * C)
+_sb(F32, ifl=C, urow=2, pmf=2, scol=2, kcol=2, nscol=2, nthr=2, srow=H, ta=4, tb=4, c1f=2 * KC, t1=2 * KC,
+    t2=2 * KC, pk=2 * KC, dp=2 * KC, hi1=KC, dc=KC, c2f=KC, tw=2 * KC, acc=2, nbc=2, acca=2, bias=2, accc=2,
+    kr=H, dm=H, dsc=H, gt=2 * H, rank=2, hrow=H, hs=R * H, pt=KC, pf=KC, da=KC, at=KC, af=KC, yt=C)
+_sb(I32, c1i=2 * KC, c2i=KC, pi=2, pmi=2, vi=HC, deg=C)
+_sb(U16, o1=8 * KC, c2u=KC, ido=2, hu=2, h4=8, r4=8, ru=2, pu=KC, a1u=KC, au=KC)
+_sb(Q8, wq=512, vq=128, oq=256, eq=512, selq=128, z0q=C, z1q=C, mq=C, xq=C, ohq=7 * HC, thq=256,
+    bq0=128, bq1=128, lc0=NH, lc1=NH)
+_sb(U8, wp=512, vp=128, op=256, ep=512, selp=128, z0p=C, z1p=C, mp=C, xp=C, ohp=7 * HC, thp=256,
+    bp0=128, bp1=128, lp0=NH, lp1=NH)
+for _b in range(8):
+    SCRATCH["pb%d" % _b] = ("psum", [128, 512], F32)
+
+DMAS = ["c1", "x", "c2", "v", "wc", "ws", "hl", "oc0", "oc1", "y0", "y1"] + ["os%d" % i for i in range(4)]
+SEMAPHORES = ["V", "S", "P", "G", "sent", "arr0", "arr1"] + ["d_" + n for n in DMAS]
+
+A = AluOpType
+ACT = ActivationFunctionType
+
+
+def rank_program(g, core, T, topo):
+    rank = T.rank_of(core)
+    if rank is None:
+        return
+    Q = {"V": g.vector, "S": g.scalar, "P": g.tensor, "G": g, "Y": g.sync}
+    count = {}
+    clock = {q: {} for q in Q}
+    snap = {}
+    wrote, read = {}, {}
+
+    def wait(q, ev):
+        s, n = ev
+        if clock[q].get(s, 0) >= n:
+            return
+        Q[q].wait_ge(T.sem[s], n)
+        clock[q][s] = n
+        for k, m in snap.get(ev, {}).items():
+            if clock[q].get(k, 0) < m:
+                clock[q][k] = m
+
+    def op(q, call, r=(), w=(), ps=(), sem=None):
+        need = {}
+
+        def add(ev):
+            if ev is not None and need.get(ev[0], 0) < ev[1]:
+                need[ev[0]] = ev[1]
+        for k in r:
+            add(wrote.get(k))
+        for k in w:
+            add(wrote.get(k))
+            for ev in read.get(k, {}).items():
+                add(ev)
+        for b in ps:
+            for ev in read.get(("ps", b), {}).items():
+                if ev[0] != q:
+                    add(ev)
+        for ev in need.items():
+            wait(q, ev)
+        s, step = (q, 1) if sem is None else (sem, 16)
+        count[s] = count.get(s, 0) + step
+        ev = (s, count[s])
+        call().then_inc(T.sem[s], step)
+        snap[ev] = dict(clock[q])
+        for k in r:
+            read.setdefault(k, {})[s] = ev[1]
+        for k in w:
+            wrote[k] = ev
+            read[k] = {}
+        for b in ps:
+            read.setdefault(("ps", b), {})[s] = ev[1]
+        return ev
+
+    V, S, PE = g.vector, g.scalar, g.tensor
+
+    def ts(out, in0, s1, s2, o0, o1=None, r=(), w=(), ps=()):
+        if o1 is None:
+            return op("V", lambda: V.tensor_scalar(out, in0, s1, None, o0), r, w, ps)
+        return op("V", lambda: V.tensor_scalar(out, in0, s1, s2, o0, o1), r, w, ps)
+
+    def tt(out, in0, in1, o, r=(), w=(), ps=()):
+        return op("V", lambda: V.tensor_tensor(out, in0, in1, o), r, w, ps)
+
+    def cp(out, in_, r=(), w=(), ps=()):
+        return op("V", lambda: V.tensor_copy(out, in_), r, w, ps)
+
+    def scan(out, d0, d1, o0, o1, r=(), w=()):
+        return op("V", lambda: V.tensor_tensor_scan(out, d0, d1, 0.0, o0, o1), r, w)
+
+    def act(out, in_, f, r=(), w=(), ps=(), **kw):
+        return op("S", lambda: S.activation(out, in_, f, **kw), r, w, ps)
+
+    def quant(q, p, tile, a, b, r=(), w=()):
+        return op("V", lambda: V.quantize_mx(T[q][:, a:b], T[p][:, a:b], T[tile][:, 4 * a:4 * b]), r, w)
+
+    def mm(bank, lq, lp, la, rq, rp, a, b, start, stop, r=()):
+        return op("P", lambda: PE.matmul_mx(T["pb%d" % bank][:, 0:b - a], T[lq][:, la:la + 128], T[lp][:, la:la + 128],
+                                            T[rq][:, a:b], T[rp][:, a:b], start, stop), r, (), (bank,))
+
+    def dma(q, name, out, in_, r=(), w=()):
+        return op(q, lambda: Q[q].dma_start(out, in_), r, w, (), "d_" + name)
+
+    def iota(out, pattern, base, cm, w):
+        if out.dtype == dt.int32:
+            return op("G", lambda: g.iota(out, pattern, base, cm), (), w)
+        return op("G", lambda: g.iota(out, pattern, base, cm, allow_small_or_imprecise_dtypes=True), (), w)
+
+    def asel(out, in_, pattern, cmp, fill, base, cm, r, w):
+        return op("G", lambda: g.affine_select(out, in_, pattern, cmp, fill, base, cm), r, w)
+
+    dma("S", "c1", T.c1i[:], T.c1[:], w=["c1i"])
+    dma("Y", "x", T.xa[:], T.x[:], w=["xa0", "xa1"])
+    dma("Y", "c2", T.c2i[:], T.c2[:], w=["c2i"])
+    dma("Y", "wc", T.wq[:].bitcast(dt.uint8), T.wc[:], w=["wq"])
+    dma("Y", "ws", T.wp[:], T.ws[:], w=["wp"])
+    dma("Y", "v", T.vt[:], T.v[:], w=["vt"])
+
+    op("V", lambda: V.memset(T.one[:], 1.0), w=["one"])
+    op("V", lambda: V.memset(T.et[:], 0.0), w=["et"])
+    op("V", lambda: V.memset(T.th[:, 640:1024], 0.0), w=["thz"])
+    op("V", lambda: V.memset(T.bt[:], 0.0), w=["bt"])
+    iota(T.pi[:], [[0, 2]], 0, 1, ["pi"])
+    iota(T.urow[:], [[16, 2]], 0, 0, ["urow"])
+    iota(T.i16[:], [[0, KC], [1, 16]], 0, 0, ["i16"])
+    asel(T.pm1[:, 0:512], T.one[:], [[-16, 8], [0, 64]], A.is_ge, 0.0, 0, 1, ["one"], ["pm1a"])
+    asel(T.pm1[:, 0:512], T.pm1[:, 0:512], [[16, 8], [0, 64]], A.is_ge, 0.0, 15, -1, ["pm1a"], ["pm1a"])
+    iota(T.ifl[:], [[1, C]], 0, 0, ["ifl"])
+    iota(T.ib[:], [[1, HC]], 0, 0, ["ib"])
+    iota(T.bd[:, 0:512], [[0, 8], [2, 16], [32, 4]], -C, 0, ["bd"])
+    iota(T.bd[:, 512:640], [[2, H], [1000, 4]], -C, 0, ["bd2"])
+    asel(T.bd[:, 0:512], T.bd[:, 0:512], [[-16, 8], [0, 64]], A.is_ge, 1000.0, 0, 1, ["bd"], ["bd"])
+    asel(T.bd[:, 0:512], T.bd[:, 0:512], [[16, 8], [0, 64]], A.is_ge, 1000.0, 15, -1, ["bd"], ["bd"])
+    asel(T.sel[:], T.one[:], [[-1, 128], [1, 4]], A.is_equal, 0.0, 0, 0, ["one"], ["sel"])
+    for b in range(4):
+        asel(T.et[:, 512 * b + b:512 * (b + 1):4], T.one[:, 0:128], [[-1, 128]], A.is_equal, 0.0, 0, 1,
+             ["one", "et"], ["et%d" % b])
+
+    ts(T.pmi[:], T.pi[:], 15, None, A.bitwise_and, r=["pi"], w=["pmi"])
+    cp(T.pmf[:], T.pmi[:], ["pmi"], ["pmf"])
+    pm = T.pmf[:, 0:1]
+    ts(T.keep[:], T.i16[:], 0.0, None, A.not_equal, r=["i16"], w=["keep"])
+    ts(T.thr[:], T.i16[:], pm, 1e29, A.not_equal, A.mult, ["i16", "pmf"], ["thr"])
+    tt(T.scol[:], T.urow[:], T.pmf[:], A.add, ["urow", "pmf"], ["scol"])
+    ts(T.nthr[:], T.pmf[:], -1.0, -128.5, A.mult, A.add, ["pmf"], ["nthr"])
+    for t in range(4):
+        ts(T.o1[:, 2 * KC * t:2 * KC * (t + 1)], T.c1i[:], 4.0, float(t), A.mult, A.add, ["c1i"], ["o1%d" % t])
+    cp(T.c1f[:], T.c1i[:], ["c1i"], ["c1f"])
+    ts(T.kcol[:], T.scol[:], -1.0, 15.5, A.mult, A.add, ["scol"], ["kcol"])
+    ts(T.nscol[:], T.scol[:], -1.0 / 64, None, A.mult, r=["scol"], w=["nscol"])
+    cp(T.ido[:], T.scol[:], ["scol"], ["ido"])
+    ts(T.t1[:], T.c1f[:], float(HC), -float(HC), A.is_ge, A.mult, ["c1f"], ["t1"])
+    ts(T.t2[:], T.c1f[:], float(HC), 511.0 / 512, A.is_ge, A.mult, ["c1f"], ["t2"])
+    tt(T.dc[:], T.c1f[:, KC:], T.c1f[:, :KC], A.subtract, ["c1f"], ["dc"])
+    tt(T.pk[:, :KC], T.c1f[:, :KC], T.t1[:, :KC], A.add, ["c1f", "t1"], ["pk0"])
+    tt(T.hi1[:], T.c1f[:, KC:], T.t1[:, KC:], A.add, ["c1f", "t1"], ["hi1"])
+    ts(T.pk[:, KC:], T.t2[:, :KC], 1.0 / 512, None, A.add, r=["t2"], w=["pk1"])
+    tt(T.dp[:, KC:], T.t2[:, KC:], T.t2[:, :KC], A.subtract, ["t2"], ["dp1"])
+    tt(T.dp[:, :KC], T.hi1[:], T.pk[:, :KC], A.subtract, ["hi1", "pk0"], ["dp0"])
+
+    def gathered(out, okey, src, skey, win, wkey, off, offkey, o, a, b):
+        for t in range(4):
+            tt(T[out][:, 4 * a + t:4 * b:4], win(t).indirect(off(t, a // 16, b // 16)), T[src][:, 4 * a + t:4 * b:4], o,
+               wkey(t) + offkey(t) + skey(t), [okey + str(t)])
+        return [okey + str(t) for t in range(4)]
+
+    def compare(X, xk, src, skey, win, wkey, off0, key0, off1, key1, extra=None):
+        def piece(k, h):
+            a, b = HC * h, HC * (h + 1)
+            z, off, key = ("z0", off0, key0) if k == 0 else ("z1", off1, key1)
+            if not PRE or k + h == 0:
+                return gathered(z, "%s%d" % (z, h), src, skey, win, wkey, off, key, A.mult, a, b)
+            ks = ["%s%d%d" % (z, h, t) for t in range(4)]
+            o = 4 * C * k
+            tt(T[z][:, 4 * a:4 * b], T.pre[:, o + 4 * a:o + 4 * b], T[X][:, 4 * a:4 * b], A.mult,
+               xk + ["pre" + e for e in ks], ks)
+            return ks
+        if PRE:
+            for k, h in ((0, 1), (1, 0), (1, 1)):
+                a, b, o = HC * h, HC * (h + 1), 4 * C * k
+                off, key = (off0, key0) if k == 0 else (off1, key1)
+                for t in range(4):
+                    act(T.pre[:, o + 4 * a + t:o + 4 * b:4], win(t).indirect(off(t, a // 16, b // 16)), ACT.Copy,
+                        wkey(t) + key(t), ["prez%d%d%d" % (k, h, t)])
+            k0 = piece(0, 0)
+            if extra:
+                extra()
+            k0 = k0 + piece(0, 1)
+        else:
+            k0 = gathered("z0", "z00", src, skey, win, wkey, off0, key0, A.mult, 0, C)
+            if extra:
+                extra()
+        quant("z0q", "z0p", "z0", 0, C, k0, ["z0q"])
+        for h in range(2):
+            a, b = HC * h, HC * (h + 1)
+            k1 = piece(1, h)
+            mm(h, "oq", "op", 128, "z0q", "z0p", a, b, True, False, ["oq", "z0q"])
+            quant("z1q", "z1p", "z1", a, b, k1, ["z1q%d" % h])
+            mm(h, "oq", "op", 0, "z1q", "z1p", a, b, False, True, ["oq", "z1q%d" % h])
+        for h in range(2):
+            a, b = HC * h, HC * (h + 1)
+            tt(T.mask[:, a:b], T["pb%d" % h][:, 0:HC], T.thr[:, a:b], A.is_gt, ["thr"], ["mask%d" % h], [h])
+            scan(T.msc[:, a:b], T.keep[:, a:b], T.mask[:, a:b], A.mult, A.add, ["keep", "mask%d" % h], ["msc%d" % h])
+
+    m16 = T.msc[:, 15:C:16]
+    mk = ["msc0", "msc1"]
+    peers = [c for c in T.cores if c != core]
+    mask = topo.mask(core, peers[0])
+    for c in peers:
+        mask &= topo.mask(core, c)
+    engines = bin(mask).count("1")
+    dsts = [DstId(rid=topo.addr(c)[0], pnc=topo.addr(c)[1]) for c in peers]
+    names = ["xa", "xb", "xc"]
+
+    for rd in range(R):
+        X, Xn = names[rd], names[rd + 1]
+        xk = [X + "0", X + "1"]
+        bq, bp, lc, lp = "bq%d" % rd, "bp%d" % rd, "lc%d" % rd, "lp%d" % rd
+
+        if PRE:
+            cp(T.xd[:, 0:4 * HC], T[X][:, 0:4 * HC], xk, ["xd0", "xd1", "xd2", "xd3"])
+        else:
+            cp(T.xd[:, 0:4 * C:4], T[X][:, 0:4 * C:4], xk, ["xd0"])
+            for t in range(1, 4):
+                act(T.xd[:, t:4 * C:4], T[X][:, t:4 * C:4], ACT.Copy, xk, ["xd%d" % t])
+
+        def first():
+            ts(T.pm1[:, 512:1024], T.pm1[:, 0:512], -1.0, None, A.mult, r=["pm1a"], w=["pm1b"])
+            cp(T.c2u[:], T.c2i[:], ["c2i"], ["c2u"])
+            quant("oq", "op", "pm1", 0, 256, ["pm1a", "pm1b"], ["oq"])
+        compare(X, xk, "xd", lambda t: ["xd%d" % t], lambda t: T[X][:, 0:4 * C], lambda t: xk,
+                lambda t, a, b: T.o1[:, 2 * KC * t + a:2 * KC * t + b], lambda t: ["o1%d" % t],
+                lambda t, a, b: T.o1[:, 2 * KC * t + KC + a:2 * KC * t + KC + b], lambda t: ["o1%d" % t],
+                first if rd == 0 else None)
+        if not PRE:
+            act(T.xh[:], T[X][:], ACT.Copy, xk, ["xh"], scale=0.5)
+
+        tt(T.tw[:, :KC], m16, T.dp[:, :KC], A.mult, mk + ["dp0"], ["tw0"])
+        tt(T.tw[:, KC:], m16, T.dp[:, KC:], A.mult, mk + ["dp1"], ["tw1"])
+        tt(T.hw[:], T.tw[:], T.pk[:], A.add, ["tw0", "tw1", "pk0", "pk1"], ["hw"])
+        for c in range(4 * (7 - NS), KC):
+            i = c - 4 * (7 - NS)
+            act(T.ab[:, HC * i:HC * (i + 1)], T.ib[:], ACT.Abs, ["ib", "hw"], ["ab%d" % i], bias=T.hw[:, c:c + 1], scale=-1.0)
+            if i % 4 == 3:
+                for j in range(i - 3, i + 1):
+                    e = j + 4 * (7 - NS)
+                    s, t = divmod(e, 4)
+                    act(T.oh[:, 4 * HC * s + t:4 * HC * (s + 1):4], T.ab[:, HC * j:HC * (j + 1)], ACT.Relu,
+                        ["ab%d" % j, "hw"], ["oh%d" % e], bias=T.hw[:, KC + e:KC + e + 1], scale=-1.0)
+
+        def onehot(s):
+            for t in range(4):
+                c = 4 * s + t
+                ts(T.oh[:, 4 * HC * s + t:4 * HC * (s + 1):4], T.ib[:], T.hw[:, c:c + 1], T.hw[:, KC + c:KC + c + 1],
+                   A.is_equal, A.mult, ["ib", "hw"], ["oh%d" % c])
+
+        def summed(s, start, stop):
+            quant("ohq", "ohp", "oh", HC * s, HC * (s + 1), ["oh%d" % (4 * s + t) for t in range(4)], ["ohq%d" % s])
+            mm(2, "oq", "op", 0, "ohq", "ohp", HC * s, HC * (s + 1), start, stop, ["oq", "ohq%d" % s])
+        nv = 7 - NS
+        order = list(range(nv - 1)) + list(range(nv, 6)) + [nv - 1, 6]
+        onehot(0)
+        for i, s in enumerate(order):
+            if i + 1 < nv:
+                onehot(i + 1)
+            summed(s, i == 0, i == 6)
+
+        ts(T.cls[:, HC:], T.pb2[:, 0:HC], 127.5625, 143.0, A.add, A.min, w=["cls1"], ps=[2])
+        ts(T.vi[:], T.pb2[:, 0:HC], 512.0, None, A.mult, w=["vi"], ps=[2])
+        act(T.junk[:, HC:C], T.cls[:, HC:], ACT.Sign, ["cls1", "nthr"], ["j01", "acc1"], bias=T.nthr[:, 0:1], accum_out=T.acc[:, 1:2])
+        ts(T.deg[:, :HC], T.vi[:], 511, None, A.bitwise_and, r=["vi"], w=["deg0"])
+        ts(T.cls[:, :HC], T.deg[:, :HC], 15.0, 128.0, A.min, A.add, ["deg0"], ["cls0"])
+        act(T.junk[:, 0:HC], T.cls[:, :HC], ACT.Sign, ["cls0", "nthr"], ["j00", "acc0"], bias=T.nthr[:, 0:1], accum_out=T.acc[:, 0:1])
+        ts(T.deg[:, HC:], T.vi[:], 9, None, A.logical_shift_right, r=["vi"], w=["deg1"])
+        if rd == 0:
+            quant("selq", "selp", "sel", 0, 128, ["sel"], ["selq"])
+        ts(T.th[:, 0:640], T.bd[:], T.acc[:, 0:1], T.acc[:, 1:2], A.subtract, A.is_lt, ["bd", "bd2", "acc0", "acc1"], ["th"])
+        quant("thq", "thp", "th", 0, 256, ["th", "thz"], ["thq"])
+        mm(3, "thq", "thp", 0, "selq", "selp", 0, 128, True, True, ["thq", "selq"])
+        mm(4, "oq", "op", 0, "thq", "thp", 128, 256, True, True, ["thq", "oq"])
+        if rd == 0:
+            ts(T.srow[:], T.ifl[:, 0:H], 1.0 / 64, None, A.mult, r=["ifl"], w=["srow"])
+            ts(T.ta[:], T.ifl[:, 0:4], 0.5, float(C), A.mult, A.add, ["ifl"], ["ta"])
+            ts(T.tb[:], T.ifl[:, 0:4], 0.25, None, A.mult, r=["ifl"], w=["tb"])
+            ts(T.diag[:], T.i16[:], pm, None, A.is_equal, r=["i16", "pmf"], w=["diag"])
+        ts(T.nbc[:], T.pb3[:, 0:2], -1.0, -0.5, A.mult, A.add, w=["nbc"], ps=[3])
+        cl = ["cls0", "cls1"]
+        for u in range(2):
+            act(T.junk[:, 3 * C + H * u:3 * C + H * (u + 1)], T.pb4[:, 0:H], ACT.Sign, ["nbc"], ["j3%d" % u, "acca%d" % u], [4],
+                bias=T.nbc[:, u:u + 1], accum_out=T.acca[:, u:u + 1])
+        for u in range(2):
+            act(T.bias[:, u:u + 1], T.acca[:, u:u + 1], ACT.Identity, ["acca%d" % u, "kcol"], ["bias%d" % u],
+                bias=T.kcol[:, u:u + 1], scale=0.5)
+        for u in range(2):
+            a, b = C * u, C * (u + 1)
+            ts(T.ind[:, a:b], T.cls[:], T.nbc[:, u:u + 1], 127.5, A.add, A.is_equal, cl + ["nbc"], ["ind%d" % u])
+            scan(T.cum[:, a:b], T.ind[:, a:b], T.ind[:, a:b], A.add, A.max, ["ind%d" % u], ["cum%d" % u])
+            act(T.junk[:, C + a:C + b], T.cum[:, a:b], ACT.Sign, ["cum%d" % u, "bias%d" % u], ["j1%d" % u, "accc%d" % u],
+                bias=T.bias[:, u:u + 1], accum_out=T.accc[:, u:u + 1])
+        ak = ["accc0", "accc1"]
+        ts(T.hu[:], T.accc[:], -0.5, float(HC), A.mult, A.add, ak, ["hu"])
+        for u in range(2):
+            ts(T.h4[:, u:8:2], T.ta[:], T.accc[:, u:u + 1], 2.0, A.subtract, A.mult, ak + ["ta"], ["h4%d" % u])
+        dk = ["deg0", "deg1", "hu"]
+        tt(T.dm[:], T.deg[:, 0:C].indirect(T.hu[:]), T.diag[:, 0:H], A.mult, dk + ["diag"], ["dm"])
+        tt(T.kr[:], T.deg[:, 0:C].indirect(T.hu[:]), T.srow[:], A.subtract, dk + ["srow"], ["kr"])
+        act(T.bu[:], T[X][:, 0:4 * C].indirect(T.h4[:]), ACT.Copy, xk + ["h40", "h41"], ["bu"])
+        act(T.hrow[:], T.ifl[:, 0:C].indirect(T.hu[:]), ACT.Copy, ["ifl", "hu"], ["hrow"])
+        if rd == 0:
+            act(T.c2row[:], T.ifl[:, 0:NH].indirect(T.c2u[:]), ACT.Copy, ["ifl", "c2u"], ["c2row"])
+        if PRE:
+            act(T.xh[:], T[X][:], ACT.Copy, xk, ["xh"], scale=0.5)
+        scan(T.dsc[:], T.keep[:, 0:H], T.dm[:], A.mult, A.add, ["keep", "dm"], ["dsc"])
+        for u in range(2):
+            ts(T.gt[:, H * u:H * (u + 1)], T.kr[:], T.dsc[:, 16 * u + 15:16 * u + 16], T.nscol[:, u:u + 1],
+               A.subtract, A.is_gt, ["kr", "dsc", "nscol"], ["gt%d" % u])
+        for u in range(2):
+            op("V", lambda u=u: V.tensor_reduce(T.rank[:, u:u + 1], T.gt[:, H * u:H * (u + 1)], AxisListType.X, A.add),
+               ["gt%d" % u], ["rank%d" % u])
+        for u in range(2):
+            ts(T.r4[:, u:8:2], T.tb[:], T.rank[:, u:u + 1], 4.0, A.add, A.mult, ["tb", "rank%d" % u], ["r4%d" % u])
+        cp(T.bt[:, 0:4 * H].indirect(T.r4[:]), T.bu[:], ["r40", "r41", "bu"], ["bt"])
+        ev = quant(bq, bp, "bt", 0, 128, ["bt"], [bq])
+
+        wait("G", ev)
+        a, b = H * rank, H * (rank + 1)
+        arr = T.sem["arr%d" % rd]
+        g.remote_dma_fused([RemoteDMATransfer(dst_ids=dsts, dma_engine_mask=mask, remote_sem=arr,
+                                              src=T[bq][:, 0:H].bitcast(dt.uint8),
+                                              dsts=[T[lc][:, a:b].bitcast(dt.uint8) for c in peers])], local_sem=T.sem.sent)
+        g.remote_dma_fused([RemoteDMATransfer(dst_ids=dsts, dma_engine_mask=mask, remote_sem=arr,
+                                              src=T[bp][:, 0:H], dsts=[T[lp][:, a:b] for c in peers])], local_sem=T.sem.sent)
+        count["sent"] = count.get("sent", 0) + 2 * engines
+
+        cp(T[lc][:, a:b].bitcast(dt.uint32), T[bq][:, 0:128].bitcast(dt.uint32).indirect(T.ido[:]), [bq, "ido"], [lc])
+        cp(T[lp][:, a:b], T[bp][:, 0:128].indirect(T.ido[:]), [bq, "ido"], [lp])
+        if rd == 0:
+            quant("eq", "ep", "et", 0, 512, ["et%d" % i for i in range(4)], ["eq"])
+            cp(T.c2f[:], T.c2i[:], ["c2i"], ["c2f"])
+        tt(T.pt[:], m16, T.dc[:], A.mult, mk + ["dc"], ["pt"])
+        cp(T.ru[:], T.rank[:], ["rank0", "rank1"], ["ru"])
+        tt(T.pf[:], T.pt[:], T.c1f[:, :KC], A.add, ["pt", "c1f"], ["pf"])
+        cp(T.hs[:, H * rd:H * (rd + 1)].indirect(T.ru[:]), T.hrow[:], ["ru", "hrow"], ["hs%d" % rd])
+        cp(T.pu[:], T.pf[:], ["pf"], ["pu"])
+        tt(T.am[:], T.c2row[:, 0:C].indirect(T.pu[:]), T.diag[:], A.mult, ["c2row", "pu", "diag"], ["am"])
+        scan(T.asc[:], T.keep[:], T.am[:], A.mult, A.add, ["keep", "am"], ["asc"])
+        cp(T.a1u[:], T.asc[:, 15:C:16], ["asc"], ["a1u"])
+        tt(T.da[:], T.asc[:, 15:C:16], T.c2f[:], A.subtract, ["asc", "c2f"], ["da"])
+        if rd == 0:
+            quant("vq", "vp", "vt", 0, 128, ["vt"], ["vq"])
+        else:
+            dma("Y", "hl", T.hl[:], T.hs[0:128:16, :], ["hs0", "hs1"])
+
+        wait("P", ("arr%d" % rd, 2 * engines * len(peers)))
+        for b in range(4):
+            mm(4 + b, "eq", "ep", 128 * b, lc, lp, 0, NH, True, True, ["eq", lc, lp])
+        for b in range(4):
+            out, src = T.ft[:, NH * b:NH * (b + 1)], T["pb%d" % (4 + b)][:, 0:NH]
+            if b == 0 or (PRE and b == 2):
+                cp(out, src, w=["ft%d" % b], ps=[4 + b])
+            else:
+                act(out, src, ACT.Copy, w=["ft%d" % b], ps=[4 + b])
+
+        compare(X, xk, X, lambda t: xk, lambda t: T.ft[:, NH * t:NH * (t + 1)], lambda t: ["ft%d" % t],
+                lambda t, a, b: T.c2u[:, a:b], lambda t: ["c2u"],
+                lambda t, a, b: T.a1u[:, a:b], lambda t: ["a1u"])
+        act(T.fh[:], T.ft[:], ACT.Copy, ["ft%d" % b for b in range(4)], ["fh"], scale=0.5)
+        tt(T.at[:], m16, T.da[:], A.mult, mk + ["da"], ["at"])
+        tt(T.af[:], T.at[:], T.c2f[:], A.add, ["at", "c2f"], ["af"])
+        cp(T.au[:], T.af[:], ["af"], ["au"])
+
+        pieces = [(0, MA), (MA, C)]
+        for h, (a, b) in enumerate(pieces):
+            k = gathered("mt", "mt%d" % h, "xh", lambda t: ["xh"], lambda t: T.fh[:, NH * t:NH * (t + 1)], lambda t: ["fh"],
+                         lambda t, a, b: T.au[:, a:b], lambda t: ["au"], A.add, a, b)
+            quant("mq", "mp", "mt", a, b, k, ["mq%d" % h])
+            for i in range(4):
+                mm(4 * h + i, "wq", "wp", 128 * i, "mq", "mp", a, b, True, True, ["wq", "wp", "mq%d" % h])
+            for i in range(4):
+                out, src, key = T[Xn][:, 4 * a + i:4 * b:4], T["pb%d" % (4 * h + i)][:, 0:b - a], "%s%d%d" % (Xn, h, i)
+                if h == 1 and i % 2 == 0:
+                    if i == 0 and rd == R - 1:
+                        quant("xq", "xp", Xn, 0, MA, ["%s0%d" % (Xn, j) for j in range(4)], ["xq0"])
+                    ts(out, src, 0.03125, None, A.mult, w=[key], ps=[4 * h + i])
+                else:
+                    act(out, src, ACT.Copy, w=[key], ps=[4 * h + i], scale=0.03125)
+        wrote[Xn + "0"] = wrote["%s12" % Xn]
+        wrote[Xn + "1"] = wrote["%s13" % Xn]
+
+    Xn = names[R]
+    for h, (a, b) in enumerate(pieces):
+        if h == 1:
+            quant("xq", "xp", Xn, a, b, [Xn + "0", Xn + "1"], ["xq1"])
+        mm(h, "vq", "vp", 0, "xq", "xp", a, b, True, True, ["vq", "xq%d" % h])
+        dma("Y", "oc%d" % h, T.oc[:, 4 * a:4 * b], T.xq[:, a:b].bitcast(dt.uint8), ["xq%d" % h])
+        cp(T.yt[:, a:b], T["pb%d" % h][:, 0:b - a], w=["yt%d" % h], ps=[h])
+        if h == 1:
+            for k in range(4):
+                dma("S", "os%d" % k, T.osc[4 * k:4 * k + 4, :], T.xp[32 * k:32 * k + 4, :], ["xq0", "xq1"])
+        dma("Y", "y%d" % h, T.y[:, a:b], T.yt[:, a:b], ["yt%d" % h])
+    for s, n in count.items():
+        wait("G", (s, n))

@@ -7,7 +7,7 @@ KC = C // 16
 NH = N * H
 MA = 256
 NS = 2
-PRE = False
+PRE = True
 Q8, U8, BF, F32, I32, U16 = "float8_e4m3fn_x4", "uint8", "bfloat16", "float32", "int32", "uint16"
 
 SCRATCH = {}
@@ -391,9 +391,18 @@ def rank_program(g, core, T, topo):
         cp(T.au[:], T.af[:], ["af"], ["au"])
 
         pieces = [(0, MA), (MA, C)]
+        if PRE:
+            for t in range(4):
+                act(T.pre[:, 4 * MA + t:4 * C:4], T.fh[:, NH * t:NH * (t + 1)].indirect(T.au[:, MA // 16:KC]), ACT.Copy,
+                    ["fh", "au"], ["prez01%d" % t])
         for h, (a, b) in enumerate(pieces):
-            k = gathered("mt", "mt%d" % h, "xh", lambda t: ["xh"], lambda t: T.fh[:, NH * t:NH * (t + 1)], lambda t: ["fh"],
-                         lambda t, a, b: T.au[:, a:b], lambda t: ["au"], A.add, a, b)
+            if PRE and h == 1:
+                k = ["mt1%d" % t for t in range(4)]
+                tt(T.mt[:, 4 * a:4 * b], T.pre[:, 4 * a:4 * b], T.xh[:, 4 * a:4 * b], A.add,
+                   ["xh"] + ["prez01%d" % t for t in range(4)], k)
+            else:
+                k = gathered("mt", "mt%d" % h, "xh", lambda t: ["xh"], lambda t: T.fh[:, NH * t:NH * (t + 1)],
+                             lambda t: ["fh"], lambda t, a, b: T.au[:, a:b], lambda t: ["au"], A.add, a, b)
             quant("mq", "mp", "mt", a, b, k, ["mq%d" % h])
             for i in range(4):
                 mm(4 * h + i, "wq", "wp", 128 * i, "mq", "mp", a, b, True, True, ["wq", "wp", "mq%d" % h])

@@ -6,8 +6,9 @@ HC = C // 2
 KC = C // 16
 NH = N * H
 MA = 256
-NS = 2
-PRE = True
+K4 = C // 4
+NS = 10
+PIECES = [(0, MA), (MA, C)]
 Q8, U8, BF, F32, I32, U16 = "float8_e4m3fn_x4", "uint8", "bfloat16", "float32", "int32", "uint16"
 
 SCRATCH = {}
@@ -18,23 +19,23 @@ def _sb(dtype, **kw):
         SCRATCH[k] = ("sbuf", [128, n], dtype)
 
 
-_sb(BF, xa=4 * C, xb=4 * C, xc=4 * C, xh=4 * C, xd=4 * C, z0=4 * C, z1=4 * C, mt=4 * C, ft=4 * NH, fh=4 * NH,
-    vt=512, one=512, pm1=1024, et=2048, sel=512, bd=640, th=1024, bt=512, bu=128, i16=C, thr=C, keep=C, diag=C,
-    ib=HC, mask=C, msc=C, hw=2 * KC, oh=7 * 4 * HC, ab=NS * 4 * HC, cls=C, ind=2 * C, cum=2 * C, junk=3 * C + 64,
-    c2row=C, am=C, asc=C, pre=8 * C)
-_sb(F32, ifl=C, urow=2, pmf=2, scol=2, kcol=2, nscol=2, nthr=2, srow=H, ta=4, tb=4, c1f=2 * KC, t1=2 * KC,
-    t2=2 * KC, pk=2 * KC, dp=2 * KC, hi1=KC, dc=KC, c2f=KC, tw=2 * KC, acc=2, nbc=2, acca=2, bias=2, accc=2,
-    kr=H, dm=H, dsc=H, gt=2 * H, rank=2, hrow=H, hs=R * H, pt=KC, pf=KC, da=KC, at=KC, af=KC, yt=C)
-_sb(I32, c1i=2 * KC, c2i=KC, pi=2, pmi=2, vi=HC, deg=C)
-_sb(U16, o1=8 * KC, c2u=KC, ido=2, hu=2, h4=8, r4=8, ru=2, pu=KC, a1u=KC, au=KC)
-_sb(Q8, wq=512, vq=128, oq=256, eq=512, selq=128, z0q=C, z1q=C, mq=C, xq=C, ohq=7 * HC, thq=256,
+_sb(BF, xa=4 * C, xb=4 * C, xc=4 * C, xh=4 * C, xd=4 * MA, z=8 * C, mt=4 * C, ft=4 * NH, fm=4 * C,
+    vt=512, one=512, pm1=1024, et=2048, sel=512, bd=640, th=1024, bt=512, bu=128, i16=MA, thr=MA, keep=MA, diag=H,
+    ib=HC, mask=C, msc=C, hw=2 * KC, oh=7 * 4 * HC, ab=NS * HC, cls=C, ind=2 * C, cum=2 * C, junk=3 * C + 64,
+    c2row=C, am=C, asc=C, pre=8 * C, i4=C, thr4=MA, keep4=C, diag4=C, c2s=C, da=K4, at=K4)
+_sb(F32, ifl=C, urow=2, scol=2, kcol=2, nscol=2, nthr=2, nth2=4, srow=H, tab=8, c1f=2 * KC,
+    t1=2 * KC, t2=2 * KC, pk=2 * KC, dp=2 * KC, dc=KC, tw=2 * KC, acc=2, nbc=2, acca=2, bias=2, accc=2,
+    kr=H, dm=H, dsc=H, gt=2 * H, rank=2, hrow=H, hs=R * H, pt=KC, yt=C, pqf=8)
+_sb(I32, c1i=2 * KC, c2i=KC, pi=2, vi=HC, deg=C, pqi=8)
+_sb(U16, o1=8 * KC, c2u=KC, ido=2, hu=2, h4=8, r4=8, ru=2, pu=KC, a0u=K4, a1u=K4, au=K4)
+_sb(Q8, wq=512, vq=128, oq=256, eq=512, selq=128, zq=2 * C, mq=C, xq=C, ohq=7 * HC, thq=256,
     bq0=128, bq1=128, lc0=NH, lc1=NH)
-_sb(U8, wp=512, vp=128, op=256, ep=512, selp=128, z0p=C, z1p=C, mp=C, xp=C, ohp=7 * HC, thp=256,
+_sb(U8, wp=512, vp=128, op=256, ep=512, selp=128, zp=2 * C, mp=C, xp=C, ohp=7 * HC, thp=256,
     bp0=128, bp1=128, lp0=NH, lp1=NH)
 for _b in range(8):
     SCRATCH["pb%d" % _b] = ("psum", [128, 512], F32)
 
-DMAS = ["c1", "x", "c2", "v", "wc", "ws", "hl", "oc0", "oc1", "y0", "y1"] + ["os%d" % i for i in range(4)]
+DMAS = ["c1", "x0", "x1", "c2", "v", "wc", "ws", "hl", "oc0", "oc1", "y0", "y1"] + ["os%d" % i for i in range(4)]
 SEMAPHORES = ["V", "S", "P", "G", "sent", "arr0", "arr1"] + ["d_" + n for n in DMAS]
 
 A = AluOpType
@@ -131,97 +132,116 @@ def rank_program(g, core, T, topo):
         return op("G", lambda: g.affine_select(out, in_, pattern, cmp, fill, base, cm), r, w)
 
     dma("S", "c1", T.c1i[:], T.c1[:], w=["c1i"])
-    dma("Y", "x", T.xa[:], T.x[:], w=["xa0", "xa1"])
+    dma("Y", "x0", T.xa[:, 0:4 * MA], T.x[:, 0:4 * MA], w=["xa0"])
+    wait("Y", dma("Y", "x1", T.xa[:, 4 * MA:], T.x[:, 4 * MA:], w=["xa1"]))
     dma("Y", "c2", T.c2i[:], T.c2[:], w=["c2i"])
     dma("Y", "wc", T.wq[:].bitcast(dt.uint8), T.wc[:], w=["wq"])
     dma("Y", "ws", T.wp[:], T.ws[:], w=["wp"])
     dma("Y", "v", T.vt[:], T.v[:], w=["vt"])
 
     op("V", lambda: V.memset(T.one[:], 1.0), w=["one"])
-    op("V", lambda: V.memset(T.et[:], 0.0), w=["et"])
     op("V", lambda: V.memset(T.th[:, 640:1024], 0.0), w=["thz"])
     op("V", lambda: V.memset(T.bt[:], 0.0), w=["bt"])
     iota(T.pi[:], [[0, 2]], 0, 1, ["pi"])
     iota(T.urow[:], [[16, 2]], 0, 0, ["urow"])
-    iota(T.i16[:], [[0, KC], [1, 16]], 0, 0, ["i16"])
-    asel(T.pm1[:, 0:512], T.one[:], [[-16, 8], [0, 64]], A.is_ge, 0.0, 0, 1, ["one"], ["pm1a"])
-    asel(T.pm1[:, 0:512], T.pm1[:, 0:512], [[16, 8], [0, 64]], A.is_ge, 0.0, 15, -1, ["pm1a"], ["pm1a"])
-    iota(T.ifl[:], [[1, C]], 0, 0, ["ifl"])
+    iota(T.i16[:], [[0, MA // 16], [1, 16]], 0, 0, ["i16"])
+    iota(T.bd[:, 0:512], [[1, 8], [0, 64]], 0, 0, ["bd"])
     iota(T.ib[:], [[1, HC]], 0, 0, ["ib"])
+    iota(T.ifl[:], [[1, C]], 0, 0, ["ifl"])
+    asel(T.sel[:], T.one[:], [[-1, 128], [1, 4]], A.is_equal, 0.0, 0, 0, ["one"], ["sel"])
+
+    ts(T.pqi[:, 0:2], T.pi[:], 2, 3, A.logical_shift_right, A.bitwise_and, ["pi"], ["pqi0"])
+    ts(T.pqi[:, 2:4], T.pi[:], 3, None, A.bitwise_and, r=["pi"], w=["pqi1"])
+    ts(T.pqi[:, 4:6], T.pi[:], 4, None, A.logical_shift_right, r=["pi"], w=["pqi2"])
+    ts(T.pqi[:, 6:8], T.pi[:], 15, None, A.bitwise_and, r=["pi"], w=["pqi3"])
+    cp(T.pqf[:], T.pqi[:], ["pqi0", "pqi1", "pqi2", "pqi3"], ["pqf"])
+    pq, pe, pg, pm, pmf = T.pqf[:, 0:1], T.pqf[:, 2:3], T.pqf[:, 4:5], T.pqf[:, 6:7], T.pqf[:, 6:8]
+    tt(T.scol[:], T.urow[:], pmf, A.add, ["urow", "pqf"], ["scol"])
+    ts(T.nthr[:], pmf, -1.0, -128.5, A.mult, A.add, ["pqf"], ["nthr"])
+    ts(T.nth2[:, 2:4], pmf, 15.0, -1000.0, A.is_ge, A.mult, ["pqf"], ["nth3"])
+    ts(T.nth2[:, 0:2], T.nthr[:], 127.5625, T.nth2[:, 2:3], A.add, A.add, ["nthr", "nth3"], ["nth2"])
+    for t in range(4):
+        ts(T.o1[:, 2 * KC * t:2 * KC * (t + 1)], T.c1i[:], 4.0, float(t), A.mult, A.add, ["c1i"], ["o1%d" % t])
+    cp(T.c1f[:], T.c1i[:], ["c1i"], ["c1f"])
+    ts(T.keep[:], T.i16[:], 0.0, None, A.not_equal, r=["i16"], w=["keep"])
+    ts(T.t1[:], T.c1f[:], float(HC), -float(HC), A.is_ge, A.mult, ["c1f"], ["t1"])
+    ts(T.t2[:], T.c1f[:], float(HC), 511.0 / 512, A.is_ge, A.mult, ["c1f"], ["t2"])
+    ts(T.thr[:], T.i16[:], pm, 1e29, A.not_equal, A.mult, ["i16", "pqf"], ["thr"])
+    tt(T.pk[:, 0:2 * KC:2], T.c1f[:, :KC], T.t1[:, :KC], A.add, ["c1f", "t1"], ["pk0"])
+    tt(T.dp[:, 0:2 * KC:2], T.c1f[:, KC:], T.t1[:, KC:], A.add, ["c1f", "t1"], ["dp0"])
+    ts(T.pk[:, 1:2 * KC:2], T.t2[:, :KC], 1.0 / 512, None, A.add, r=["t2"], w=["pk1"])
+    tt(T.dp[:, 1:2 * KC:2], T.t2[:, KC:], T.t2[:, :KC], A.subtract, ["t2"], ["dp1"])
+    tt(T.dp[:, 0:2 * KC:2], T.dp[:, 0:2 * KC:2], T.pk[:, 0:2 * KC:2], A.subtract, ["dp0", "pk0"], ["dp0"])
+    for u in range(2):
+        ts(T.pm1[:, 512 * u:512 * (u + 1)], T.bd[:, 0:512], pg, 1.0 - 2 * u, A.is_equal, A.mult,
+           ["bd", "pqf"], ["pm1%d" % u])
+    cp(T.xd[:], T.xa[:, 0:4 * MA], ["xa0"], ["xd"])
+    quant("oq", "op", "pm1", 0, 256, ["pm10", "pm11"], ["oq"])
+
     iota(T.bd[:, 0:512], [[0, 8], [2, 16], [32, 4]], -C, 0, ["bd"])
     iota(T.bd[:, 512:640], [[2, H], [1000, 4]], -C, 0, ["bd2"])
     asel(T.bd[:, 0:512], T.bd[:, 0:512], [[-16, 8], [0, 64]], A.is_ge, 1000.0, 0, 1, ["bd"], ["bd"])
     asel(T.bd[:, 0:512], T.bd[:, 0:512], [[16, 8], [0, 64]], A.is_ge, 1000.0, 15, -1, ["bd"], ["bd"])
-    asel(T.sel[:], T.one[:], [[-1, 128], [1, 4]], A.is_equal, 0.0, 0, 0, ["one"], ["sel"])
+    iota(T.i4[:], [[0, K4], [1, 4]], 0, 0, ["i4"])
     for b in range(4):
-        asel(T.et[:, 512 * b + b:512 * (b + 1):4], T.one[:, 0:128], [[-1, 128]], A.is_equal, 0.0, 0, 1,
-             ["one", "et"], ["et%d" % b])
+        asel(T.et[:, 512 * b:512 * (b + 1)], T.one[:], [[-1, 128], [1000, 4]], A.is_equal, 0.0, -1000 * b, 1,
+             ["one"], ["et%d" % b])
 
-    ts(T.pmi[:], T.pi[:], 15, None, A.bitwise_and, r=["pi"], w=["pmi"])
-    cp(T.pmf[:], T.pmi[:], ["pmi"], ["pmf"])
-    pm = T.pmf[:, 0:1]
-    ts(T.keep[:], T.i16[:], 0.0, None, A.not_equal, r=["i16"], w=["keep"])
-    ts(T.thr[:], T.i16[:], pm, 1e29, A.not_equal, A.mult, ["i16", "pmf"], ["thr"])
-    tt(T.scol[:], T.urow[:], T.pmf[:], A.add, ["urow", "pmf"], ["scol"])
-    ts(T.nthr[:], T.pmf[:], -1.0, -128.5, A.mult, A.add, ["pmf"], ["nthr"])
-    for t in range(4):
-        ts(T.o1[:, 2 * KC * t:2 * KC * (t + 1)], T.c1i[:], 4.0, float(t), A.mult, A.add, ["c1i"], ["o1%d" % t])
-    cp(T.c1f[:], T.c1i[:], ["c1i"], ["c1f"])
-    ts(T.kcol[:], T.scol[:], -1.0, 15.5, A.mult, A.add, ["scol"], ["kcol"])
-    ts(T.nscol[:], T.scol[:], -1.0 / 64, None, A.mult, r=["scol"], w=["nscol"])
-    cp(T.ido[:], T.scol[:], ["scol"], ["ido"])
-    ts(T.t1[:], T.c1f[:], float(HC), -float(HC), A.is_ge, A.mult, ["c1f"], ["t1"])
-    ts(T.t2[:], T.c1f[:], float(HC), 511.0 / 512, A.is_ge, A.mult, ["c1f"], ["t2"])
-    tt(T.dc[:], T.c1f[:, KC:], T.c1f[:, :KC], A.subtract, ["c1f"], ["dc"])
-    tt(T.pk[:, :KC], T.c1f[:, :KC], T.t1[:, :KC], A.add, ["c1f", "t1"], ["pk0"])
-    tt(T.hi1[:], T.c1f[:, KC:], T.t1[:, KC:], A.add, ["c1f", "t1"], ["hi1"])
-    ts(T.pk[:, KC:], T.t2[:, :KC], 1.0 / 512, None, A.add, r=["t2"], w=["pk1"])
-    tt(T.dp[:, KC:], T.t2[:, KC:], T.t2[:, :KC], A.subtract, ["t2"], ["dp1"])
-    tt(T.dp[:, :KC], T.hi1[:], T.pk[:, :KC], A.subtract, ["hi1", "pk0"], ["dp0"])
+    def compare(X, xk, src, skey, parts, thr, keep, lists, filler):
+        def at(k, h):
+            a, b = PIECES[h]
+            return a, b, 2 * a + k * (b - a)
+        got = {}
+        for k, h in ((1, 0), (0, 1), (1, 1)):
+            a, b, o = at(k, h)
+            got[k, h] = []
+            for t, step, ap, keys in parts(k, a, b):
+                ks = ["pre%d%d%d" % (k, h, e) for e in (range(4) if step == 1 else [t])]
+                got[k, h] += ks
+                act(T.pre[:, 4 * o + t:4 * (o + b - a):step], ap, ACT.Copy, keys, ks)
 
-    def gathered(out, okey, src, skey, win, wkey, off, offkey, o, a, b):
-        for t in range(4):
-            tt(T[out][:, 4 * a + t:4 * b:4], win(t).indirect(off(t, a // 16, b // 16)), T[src][:, 4 * a + t:4 * b:4], o,
-               wkey(t) + offkey(t) + skey(t), [okey + str(t)])
-        return [okey + str(t) for t in range(4)]
+        def product(k, h, i=0, n=1):
+            a, b, o = at(k, h)
+            w = (b - a) // n
+            a, b, o = a + i * w, a + (i + 1) * w, o + i * w
+            tt(T.z[:, 4 * o:4 * (o + b - a)], T.pre[:, 4 * o:4 * (o + b - a)], T[X][:, 4 * a:4 * b], A.mult,
+               xk + got[k, h], ["z%d%d%d" % (k, h, i)])
 
-    def compare(X, xk, src, skey, win, wkey, off0, key0, off1, key1, extra=None):
-        def piece(k, h):
-            a, b = HC * h, HC * (h + 1)
-            z, off, key = ("z0", off0, key0) if k == 0 else ("z1", off1, key1)
-            if not PRE or k + h == 0:
-                return gathered(z, "%s%d" % (z, h), src, skey, win, wkey, off, key, A.mult, a, b)
-            ks = ["%s%d%d" % (z, h, t) for t in range(4)]
-            o = 4 * C * k
-            tt(T[z][:, 4 * a:4 * b], T.pre[:, o + 4 * a:o + 4 * b], T[X][:, 4 * a:4 * b], A.mult,
-               xk + ["pre" + e for e in ks], ks)
-            return ks
-        if PRE:
-            for k, h in ((0, 1), (1, 0), (1, 1)):
-                a, b, o = HC * h, HC * (h + 1), 4 * C * k
-                off, key = (off0, key0) if k == 0 else (off1, key1)
-                for t in range(4):
-                    act(T.pre[:, o + 4 * a + t:o + 4 * b:4], win(t).indirect(off(t, a // 16, b // 16)), ACT.Copy,
-                        wkey(t) + key(t), ["prez%d%d%d" % (k, h, t)])
-            k0 = piece(0, 0)
-            if extra:
-                extra()
-            k0 = k0 + piece(0, 1)
-        else:
-            k0 = gathered("z0", "z00", src, skey, win, wkey, off0, key0, A.mult, 0, C)
-            if extra:
-                extra()
-        quant("z0q", "z0p", "z0", 0, C, k0, ["z0q"])
-        for h in range(2):
-            a, b = HC * h, HC * (h + 1)
-            k1 = piece(1, h)
-            mm(h, "oq", "op", 128, "z0q", "z0p", a, b, True, False, ["oq", "z0q"])
-            quant("z1q", "z1p", "z1", a, b, k1, ["z1q%d" % h])
-            mm(h, "oq", "op", 0, "z1q", "z1p", a, b, False, True, ["oq", "z1q%d" % h])
-        for h in range(2):
-            a, b = HC * h, HC * (h + 1)
-            tt(T.mask[:, a:b], T["pb%d" % h][:, 0:HC], T.thr[:, a:b], A.is_gt, ["thr"], ["mask%d" % h], [h])
-            scan(T.msc[:, a:b], T.keep[:, a:b], T.mask[:, a:b], A.mult, A.add, ["keep", "mask%d" % h], ["msc%d" % h])
+        def score(k, h):
+            a, b, o = at(k, h)
+            mm(h, "oq", "op", 128 * (1 - k), "zq", "zp", o, o + b - a, k == 0, k == 1, ["oq", "zq%d%d" % (k, h)])
+
+        def sign(h):
+            a, b = PIECES[h]
+            tt(T.mask[:, a:b], T["pb%d" % h][:, 0:b - a], T[thr][:, 0:b - a], A.is_gt, [thr], ["mask%d" % h], [h])
+
+        def carry(h):
+            a, b = PIECES[h]
+            scan(T.msc[:, a:b], T[keep][:, 0:b - a], T.mask[:, a:b], A.mult, A.add, [keep, "mask%d" % h], ["msc%d" % h])
+        zk = ["zz%d" % t for t in range(4)]
+        for t, step, ap, keys in parts(0, 0, MA):
+            tt(T.z[:, t:4 * MA:step], ap, T[src][:, t:4 * MA:step], A.mult, keys + skey, zk[t:t + 1] if step > 1 else zk)
+        product(1, 0)
+        quant("zq", "zp", "z", 0, MA, zk, ["zq00"])
+        score(0, 0)
+        quant("zq", "zp", "z", MA, 2 * MA, ["z100"], ["zq10"])
+        score(1, 0)
+        product(0, 1)
+        sign(0)
+        quant("zq", "zp", "z", 2 * MA, MA + C, ["z010"], ["zq01"])
+        score(0, 1)
+        carry(0)
+        lists(0, lambda: product(1, 1, 0, 2))
+        product(1, 1, 1, 2)
+        filler(4)
+        quant("zq", "zp", "z", MA + C, 2 * C, ["z110", "z111"], ["zq11"])
+        score(1, 1)
+        filler(0)
+        sign(1)
+        filler(1)
+        carry(1)
+        filler(2)
+        lists(1, lambda: filler(3))
 
     m16 = T.msc[:, 15:C:16]
     mk = ["msc0", "msc1"]
@@ -232,78 +252,77 @@ def rank_program(g, core, T, topo):
     engines = bin(mask).count("1")
     dsts = [DstId(rid=topo.addr(c)[0], pnc=topo.addr(c)[1]) for c in peers]
     names = ["xa", "xb", "xc"]
+    ta, tb = T.tab[:, 0:4], T.tab[:, 4:8]
 
     for rd in range(R):
         X, Xn = names[rd], names[rd + 1]
         xk = [X + "0", X + "1"]
         bq, bp, lc, lp = "bq%d" % rd, "bp%d" % rd, "lc%d" % rd, "lp%d" % rd
 
-        if PRE:
-            cp(T.xd[:, 0:4 * HC], T[X][:, 0:4 * HC], xk, ["xd0", "xd1", "xd2", "xd3"])
-        else:
-            cp(T.xd[:, 0:4 * C:4], T[X][:, 0:4 * C:4], xk, ["xd0"])
-            for t in range(1, 4):
-                act(T.xd[:, t:4 * C:4], T[X][:, t:4 * C:4], ACT.Copy, xk, ["xd%d" % t])
+        def xparts(k, a, b):
+            return [(t, 4, T[X][:, 0:4 * C].indirect(T.o1[:, KC * (2 * t + k) + a // 16:KC * (2 * t + k) + b // 16]),
+                     xk + ["o1%d" % t]) for t in range(4)]
 
-        def first():
-            ts(T.pm1[:, 512:1024], T.pm1[:, 0:512], -1.0, None, A.mult, r=["pm1a"], w=["pm1b"])
-            cp(T.c2u[:], T.c2i[:], ["c2i"], ["c2u"])
-            quant("oq", "op", "pm1", 0, 256, ["pm1a", "pm1b"], ["oq"])
-        compare(X, xk, "xd", lambda t: ["xd%d" % t], lambda t: T[X][:, 0:4 * C], lambda t: xk,
-                lambda t, a, b: T.o1[:, 2 * KC * t + a:2 * KC * t + b], lambda t: ["o1%d" % t],
-                lambda t, a, b: T.o1[:, 2 * KC * t + KC + a:2 * KC * t + KC + b], lambda t: ["o1%d" % t],
-                first if rd == 0 else None)
-        if not PRE:
-            act(T.xh[:], T[X][:], ACT.Copy, xk, ["xh"], scale=0.5)
+        def ohrow(c):
+            s, t = divmod(c, 4)
+            return T.oh[:, 4 * HC * s + t:4 * HC * (s + 1):4]
 
-        tt(T.tw[:, :KC], m16, T.dp[:, :KC], A.mult, mk + ["dp0"], ["tw0"])
-        tt(T.tw[:, KC:], m16, T.dp[:, KC:], A.mult, mk + ["dp1"], ["tw1"])
-        tt(T.hw[:], T.tw[:], T.pk[:], A.add, ["tw0", "tw1", "pk0", "pk1"], ["hw"])
-        for c in range(4 * (7 - NS), KC):
-            i = c - 4 * (7 - NS)
-            act(T.ab[:, HC * i:HC * (i + 1)], T.ib[:], ACT.Abs, ["ib", "hw"], ["ab%d" % i], bias=T.hw[:, c:c + 1], scale=-1.0)
-            if i % 4 == 3:
-                for j in range(i - 3, i + 1):
-                    e = j + 4 * (7 - NS)
-                    s, t = divmod(e, 4)
-                    act(T.oh[:, 4 * HC * s + t:4 * HC * (s + 1):4], T.ab[:, HC * j:HC * (j + 1)], ACT.Relu,
-                        ["ab%d" % j, "hw"], ["oh%d" % e], bias=T.hw[:, KC + e:KC + e + 1], scale=-1.0)
+        def bins(h, gap):
+            a, b = PIECES[h]
+            m, a, b = T.msc[:, a + 15:b:16], a // 8, b // 8
+            tt(T.tw[:, a:b:2], m, T.dp[:, a:b:2], A.mult, ["msc%d" % h, "dp0"], ["tw0%d" % h])
+            tt(T.tw[:, a + 1:b:2], m, T.dp[:, a + 1:b:2], A.mult, ["msc%d" % h, "dp1"], ["tw1%d" % h])
+            if h == 1:
+                gap()
+            tt(T.hw[:, a:b], T.tw[:, a:b], T.pk[:, a:b], A.add, ["tw0%d" % h, "tw1%d" % h, "pk0", "pk1"], ["hw%d" % h])
+            if h == 0:
+                gap()
+                for c0 in range(0, NS, 4):
+                    cs = range(c0, min(NS, c0 + 4))
+                    for c in cs:
+                        act(T.ab[:, HC * c:HC * (c + 1)], T.ib[:], ACT.Abs, ["ib", "hw0"], ["ab%d" % c],
+                            bias=T.hw[:, 2 * c:2 * c + 1], scale=-1.0)
+                    for c in cs:
+                        act(ohrow(c), T.ab[:, HC * c:HC * (c + 1)], ACT.Relu, ["ab%d" % c, "hw0"], ["oh%d" % c],
+                            bias=T.hw[:, 2 * c + 1:2 * c + 2], scale=-1.0)
 
-        def onehot(s):
-            for t in range(4):
-                c = 4 * s + t
-                ts(T.oh[:, 4 * HC * s + t:4 * HC * (s + 1):4], T.ib[:], T.hw[:, c:c + 1], T.hw[:, KC + c:KC + c + 1],
-                   A.is_equal, A.mult, ["ib", "hw"], ["oh%d" % c])
+        def onehot(cs):
+            for c in cs:
+                ts(ohrow(c), T.ib[:], T.hw[:, 2 * c:2 * c + 1], T.hw[:, 2 * c + 1:2 * c + 2],
+                   A.is_equal, A.mult, ["ib", "hw%d" % (c >= MA // 16)], ["oh%d" % c])
 
-        def summed(s, start, stop):
+        def summed(s, start=False, stop=False):
             quant("ohq", "ohp", "oh", HC * s, HC * (s + 1), ["oh%d" % (4 * s + t) for t in range(4)], ["ohq%d" % s])
             mm(2, "oq", "op", 0, "ohq", "ohp", HC * s, HC * (s + 1), start, stop, ["oq", "ohq%d" % s])
-        nv = 7 - NS
-        order = list(range(nv - 1)) + list(range(nv, 6)) + [nv - 1, 6]
-        onehot(0)
-        for i, s in enumerate(order):
-            if i + 1 < nv:
-                onehot(i + 1)
-            summed(s, i == 0, i == 6)
+        compare(X, xk, "xd", ["xd"], xparts, "thr", "keep", bins,
+                lambda i: onehot(([13, 14], [15], [NS], range(NS + 1, 12), [12])[i]))
+        summed(3, start=True)
+        onehot(range(16, 20))
+        summed(0)
+        onehot(range(20, 24))
+        summed(4)
+        onehot(range(24, 28))
+        summed(5)
+        summed(6)
+        summed(1)
+        summed(2, stop=True)
+        if rd == 0:
+            quant("selq", "selp", "sel", 0, 128, ["sel"], ["selq"])
+            ts(T.kcol[:], T.scol[:], -1.0, 15.5, A.mult, A.add, ["scol"], ["kcol"])
 
-        ts(T.cls[:, HC:], T.pb2[:, 0:HC], 127.5625, 143.0, A.add, A.min, w=["cls1"], ps=[2])
         ts(T.vi[:], T.pb2[:, 0:HC], 512.0, None, A.mult, w=["vi"], ps=[2])
-        act(T.junk[:, HC:C], T.cls[:, HC:], ACT.Sign, ["cls1", "nthr"], ["j01", "acc1"], bias=T.nthr[:, 0:1], accum_out=T.acc[:, 1:2])
+        act(T.junk[:, HC:C], T.pb2[:, 0:HC], ACT.Sign, ["nth2"], ["j01", "acc1"], [2], bias=T.nth2[:, 0:1], accum_out=T.acc[:, 1:2])
         ts(T.deg[:, :HC], T.vi[:], 511, None, A.bitwise_and, r=["vi"], w=["deg0"])
         ts(T.cls[:, :HC], T.deg[:, :HC], 15.0, 128.0, A.min, A.add, ["deg0"], ["cls0"])
         act(T.junk[:, 0:HC], T.cls[:, :HC], ACT.Sign, ["cls0", "nthr"], ["j00", "acc0"], bias=T.nthr[:, 0:1], accum_out=T.acc[:, 0:1])
+        ts(T.cls[:, HC:], T.pb2[:, 0:HC], 127.5625, 143.0, A.add, A.min, w=["cls1"], ps=[2])
+        ts(T.th[:, 0:512], T.bd[:, 0:512], T.acc[:, 0:1], T.acc[:, 1:2], A.subtract, A.is_lt, ["bd", "acc0", "acc1"], ["th0"])
+        ts(T.th[:, 512:640], T.bd[:, 512:640], T.acc[:, 0:1], T.acc[:, 1:2], A.subtract, A.is_lt, ["bd2", "acc0", "acc1"], ["th1"])
+        quant("thq", "thp", "th", 0, 128, ["th0"], ["thq0"])
+        mm(3, "thq", "thp", 0, "selq", "selp", 0, 128, True, True, ["thq0", "selq"])
+        quant("thq", "thp", "th", 128, 256, ["th1", "thz"], ["thq1"])
+        mm(4, "oq", "op", 0, "thq", "thp", 128, 256, True, True, ["thq1", "oq"])
         ts(T.deg[:, HC:], T.vi[:], 9, None, A.logical_shift_right, r=["vi"], w=["deg1"])
-        if rd == 0:
-            quant("selq", "selp", "sel", 0, 128, ["sel"], ["selq"])
-        ts(T.th[:, 0:640], T.bd[:], T.acc[:, 0:1], T.acc[:, 1:2], A.subtract, A.is_lt, ["bd", "bd2", "acc0", "acc1"], ["th"])
-        quant("thq", "thp", "th", 0, 256, ["th", "thz"], ["thq"])
-        mm(3, "thq", "thp", 0, "selq", "selp", 0, 128, True, True, ["thq", "selq"])
-        mm(4, "oq", "op", 0, "thq", "thp", 128, 256, True, True, ["thq", "oq"])
-        if rd == 0:
-            ts(T.srow[:], T.ifl[:, 0:H], 1.0 / 64, None, A.mult, r=["ifl"], w=["srow"])
-            ts(T.ta[:], T.ifl[:, 0:4], 0.5, float(C), A.mult, A.add, ["ifl"], ["ta"])
-            ts(T.tb[:], T.ifl[:, 0:4], 0.25, None, A.mult, r=["ifl"], w=["tb"])
-            ts(T.diag[:], T.i16[:], pm, None, A.is_equal, r=["i16", "pmf"], w=["diag"])
         ts(T.nbc[:], T.pb3[:, 0:2], -1.0, -0.5, A.mult, A.add, w=["nbc"], ps=[3])
         cl = ["cls0", "cls1"]
         for u in range(2):
@@ -315,13 +334,23 @@ def rank_program(g, core, T, topo):
         for u in range(2):
             a, b = C * u, C * (u + 1)
             ts(T.ind[:, a:b], T.cls[:], T.nbc[:, u:u + 1], 127.5, A.add, A.is_equal, cl + ["nbc"], ["ind%d" % u])
+        for u in range(2):
+            a, b = C * u, C * (u + 1)
             scan(T.cum[:, a:b], T.ind[:, a:b], T.ind[:, a:b], A.add, A.max, ["ind%d" % u], ["cum%d" % u])
             act(T.junk[:, C + a:C + b], T.cum[:, a:b], ACT.Sign, ["cum%d" % u, "bias%d" % u], ["j1%d" % u, "accc%d" % u],
                 bias=T.bias[:, u:u + 1], accum_out=T.accc[:, u:u + 1])
+        if rd == 0:
+            ts(ta, T.ifl[:, 0:4], 0.5, float(C), A.mult, A.add, ["ifl"], ["ta"])
+            ts(T.diag[:], T.i16[:, 0:H], pm, None, A.is_equal, r=["i16", "pqf"], w=["diag"])
+            ts(T.srow[:], T.ifl[:, 0:H], 1.0 / 64, None, A.mult, r=["ifl"], w=["srow"])
+            ts(tb, T.ifl[:, 0:4], 0.25, None, A.mult, r=["ifl"], w=["tb"])
+            ts(T.nscol[:], T.scol[:], -1.0 / 64, None, A.mult, r=["scol"], w=["nscol"])
+            cp(T.ido[:], T.scol[:], ["scol"], ["ido"])
+            cp(T.c2u[:], T.c2i[:], ["c2i"], ["c2u"])
         ak = ["accc0", "accc1"]
         ts(T.hu[:], T.accc[:], -0.5, float(HC), A.mult, A.add, ak, ["hu"])
         for u in range(2):
-            ts(T.h4[:, u:8:2], T.ta[:], T.accc[:, u:u + 1], 2.0, A.subtract, A.mult, ak + ["ta"], ["h4%d" % u])
+            ts(T.h4[:, u:8:2], ta, T.accc[:, u:u + 1], 2.0, A.subtract, A.mult, ak + ["ta"], ["h4%d" % u])
         dk = ["deg0", "deg1", "hu"]
         tt(T.dm[:], T.deg[:, 0:C].indirect(T.hu[:]), T.diag[:, 0:H], A.mult, dk + ["diag"], ["dm"])
         tt(T.kr[:], T.deg[:, 0:C].indirect(T.hu[:]), T.srow[:], A.subtract, dk + ["srow"], ["kr"])
@@ -329,8 +358,7 @@ def rank_program(g, core, T, topo):
         act(T.hrow[:], T.ifl[:, 0:C].indirect(T.hu[:]), ACT.Copy, ["ifl", "hu"], ["hrow"])
         if rd == 0:
             act(T.c2row[:], T.ifl[:, 0:NH].indirect(T.c2u[:]), ACT.Copy, ["ifl", "c2u"], ["c2row"])
-        if PRE:
-            act(T.xh[:], T[X][:], ACT.Copy, xk, ["xh"], scale=0.5)
+        act(T.xh[:], T[X][:], ACT.Copy, xk, ["xh"], scale=0.5)
         scan(T.dsc[:], T.keep[:, 0:H], T.dm[:], A.mult, A.add, ["keep", "dm"], ["dsc"])
         for u in range(2):
             ts(T.gt[:, H * u:H * (u + 1)], T.kr[:], T.dsc[:, 16 * u + 15:16 * u + 16], T.nscol[:, u:u + 1],
@@ -339,7 +367,7 @@ def rank_program(g, core, T, topo):
             op("V", lambda u=u: V.tensor_reduce(T.rank[:, u:u + 1], T.gt[:, H * u:H * (u + 1)], AxisListType.X, A.add),
                ["gt%d" % u], ["rank%d" % u])
         for u in range(2):
-            ts(T.r4[:, u:8:2], T.tb[:], T.rank[:, u:u + 1], 4.0, A.add, A.mult, ["tb", "rank%d" % u], ["r4%d" % u])
+            ts(T.r4[:, u:8:2], tb, T.rank[:, u:u + 1], 4.0, A.add, A.mult, ["tb", "rank%d" % u], ["r4%d" % u])
         cp(T.bt[:, 0:4 * H].indirect(T.r4[:]), T.bu[:], ["r40", "r41", "bu"], ["bt"])
         ev = quant(bq, bp, "bt", 0, 128, ["bt"], [bq])
 
@@ -353,59 +381,72 @@ def rank_program(g, core, T, topo):
                                               src=T[bp][:, 0:H], dsts=[T[lp][:, a:b] for c in peers])], local_sem=T.sem.sent)
         count["sent"] = count.get("sent", 0) + 2 * engines
 
+        if rd == 0:
+            tt(T.dc[:], T.c1f[:, KC:], T.c1f[:, :KC], A.subtract, ["c1f"], ["dc"])
+            ts(T.diag4[:], T.i4[:], pq, None, A.is_equal, r=["i4", "pqf"], w=["diag4"])
+            ts(T.keep4[:], T.i4[:], 0.0, None, A.not_equal, r=["i4"], w=["keep4"])
+        tt(T.pt[:], m16, T.dc[:], A.mult, mk + ["dc"], ["pt"])
         cp(T[lc][:, a:b].bitcast(dt.uint32), T[bq][:, 0:128].bitcast(dt.uint32).indirect(T.ido[:]), [bq, "ido"], [lc])
         cp(T[lp][:, a:b], T[bp][:, 0:128].indirect(T.ido[:]), [bq, "ido"], [lp])
-        if rd == 0:
-            quant("eq", "ep", "et", 0, 512, ["et%d" % i for i in range(4)], ["eq"])
-            cp(T.c2f[:], T.c2i[:], ["c2i"], ["c2f"])
-        tt(T.pt[:], m16, T.dc[:], A.mult, mk + ["dc"], ["pt"])
+        tt(T.pt[:], T.pt[:], T.c1f[:, :KC], A.add, ["pt", "c1f"], ["pt"])
         cp(T.ru[:], T.rank[:], ["rank0", "rank1"], ["ru"])
-        tt(T.pf[:], T.pt[:], T.c1f[:, :KC], A.add, ["pt", "c1f"], ["pf"])
-        cp(T.hs[:, H * rd:H * (rd + 1)].indirect(T.ru[:]), T.hrow[:], ["ru", "hrow"], ["hs%d" % rd])
-        cp(T.pu[:], T.pf[:], ["pf"], ["pu"])
-        tt(T.am[:], T.c2row[:, 0:C].indirect(T.pu[:]), T.diag[:], A.mult, ["c2row", "pu", "diag"], ["am"])
-        scan(T.asc[:], T.keep[:], T.am[:], A.mult, A.add, ["keep", "am"], ["asc"])
-        cp(T.a1u[:], T.asc[:, 15:C:16], ["asc"], ["a1u"])
-        tt(T.da[:], T.asc[:, 15:C:16], T.c2f[:], A.subtract, ["asc", "c2f"], ["da"])
         if rd == 0:
-            quant("vq", "vp", "vt", 0, 128, ["vt"], ["vq"])
+            tt(T.am[:], T.c2row[:], T.diag4[:], A.mult, ["c2row", "diag4"], ["am"])
+            quant("eq", "ep", "et", 0, 512, ["et%d" % i for i in range(4)], ["eq"])
+            scan(T.c2s[:], T.keep4[:], T.am[:], A.mult, A.add, ["keep4", "am"], ["c2s"])
+        cp(T.pu[:], T.pt[:], ["pt"], ["pu"])
+        cp(T.hs[:, H * rd:H * (rd + 1)].indirect(T.ru[:]), T.hrow[:], ["ru", "hrow"], ["hs%d" % rd])
+        tt(T.am[:], T.c2row[:, 0:C].indirect(T.pu[:]), T.diag4[:], A.mult, ["c2row", "pu", "diag4"], ["am"])
+        if rd == 0:
+            ts(T.a0u[:], T.c2s[:, 3:C:4], 4.0, pe, A.mult, A.add, ["c2s", "pqf"], ["a0u"])
+            ts(T.thr4[:], T.i4[:, 0:MA], pq, 1e29, A.not_equal, A.mult, ["i4", "pqf"], ["thr4"])
         else:
+            quant("vq", "vp", "vt", 0, 128, ["vt"], ["vq"])
             dma("Y", "hl", T.hl[:], T.hs[0:128:16, :], ["hs0", "hs1"])
+        scan(T.asc[:], T.keep4[:], T.am[:], A.mult, A.add, ["keep4", "am"], ["asc"])
+        ts(T.a1u[:], T.asc[:, 3:C:4], 4.0, pe, A.mult, A.add, ["asc", "pqf"], ["a1u"])
+        tt(T.da[:], T.asc[:, 3:C:4], T.c2s[:, 3:C:4], A.subtract, ["asc", "c2s"], ["da"])
 
         wait("P", ("arr%d" % rd, 2 * engines * len(peers)))
         for b in range(4):
             mm(4 + b, "eq", "ep", 128 * b, lc, lp, 0, NH, True, True, ["eq", lc, lp])
         for b in range(4):
-            out, src = T.ft[:, NH * b:NH * (b + 1)], T["pb%d" % (4 + b)][:, 0:NH]
-            if b == 0 or (PRE and b == 2):
+            out, src = T.ft[:, b:4 * NH:4], T["pb%d" % (4 + b)][:, 0:NH]
+            if b % 2 == 1:
                 cp(out, src, w=["ft%d" % b], ps=[4 + b])
             else:
                 act(out, src, ACT.Copy, w=["ft%d" % b], ps=[4 + b])
 
-        compare(X, xk, X, lambda t: xk, lambda t: T.ft[:, NH * t:NH * (t + 1)], lambda t: ["ft%d" % t],
-                lambda t, a, b: T.c2u[:, a:b], lambda t: ["c2u"],
-                lambda t, a, b: T.a1u[:, a:b], lambda t: ["a1u"])
-        act(T.fh[:], T.ft[:], ACT.Copy, ["ft%d" % b for b in range(4)], ["fh"], scale=0.5)
-        tt(T.at[:], m16, T.da[:], A.mult, mk + ["da"], ["at"])
-        tt(T.af[:], T.at[:], T.c2f[:], A.add, ["at", "c2f"], ["af"])
-        cp(T.au[:], T.af[:], ["af"], ["au"])
+        fk = ["ft%d" % b for b in range(4)]
 
-        pieces = [(0, MA), (MA, C)]
-        if PRE:
-            for t in range(4):
-                act(T.pre[:, 4 * MA + t:4 * C:4], T.fh[:, NH * t:NH * (t + 1)].indirect(T.au[:, MA // 16:KC]), ACT.Copy,
-                    ["fh", "au"], ["prez01%d" % t])
-        for h, (a, b) in enumerate(pieces):
-            if PRE and h == 1:
-                k = ["mt1%d" % t for t in range(4)]
-                tt(T.mt[:, 4 * a:4 * b], T.pre[:, 4 * a:4 * b], T.xh[:, 4 * a:4 * b], A.add,
-                   ["xh"] + ["prez01%d" % t for t in range(4)], k)
+        def fparts(k, a, b):
+            off = "a%du" % k
+            return [(0, 1, T.ft[:, 0:4 * NH].indirect(T[off][:, a // 4:b // 4]), fk + [off])]
+
+        def chosen(h, gap):
+            a, b = PIECES[h]
+            c, d = a // 4, b // 4
+            tt(T.at[:, c:d], T.msc[:, a + 3:b:4], T.da[:, c:d], A.mult, ["msc%d" % h, "da"], ["at%d" % h])
+            gap()
+            tt(T.at[:, c:d], T.at[:, c:d], T.c2s[:, a + 3:b:4], A.add, ["at%d" % h, "c2s"], ["at%d" % h])
+            ts(T.au[:, c:d], T.at[:, c:d], 4.0, pe, A.mult, A.add, ["at%d" % h, "pqf"], ["au%d" % h])
+            act(T.fm[:, 4 * a:4 * b], T.ft[:, 0:4 * NH].indirect(T.au[:, c:d]), ACT.Copy, fk + ["au%d" % h],
+                ["fm%d" % h], scale=0.5)
+        compare(X, xk, X, xk, fparts, "thr4", "keep4", chosen, lambda i: None)
+
+        for h, (a, b) in enumerate(PIECES):
+            if h == 0:
+                k = ["mt00", "mt01"]
+                for i in range(2):
+                    c, d = 2 * MA * i, 2 * MA * (i + 1)
+                    tt(T.mt[:, c:d], T.fm[:, c:d], T.xh[:, c:d], A.add, ["xh", "fm0"], k[i:i + 1])
+                quant("mq", "mp", "mt", 0, MA // 2, k[0:1], ["mq0a"])
+                quant("mq", "mp", "mt", MA // 2, MA, k[1:2], ["mq0"])
             else:
-                k = gathered("mt", "mt%d" % h, "xh", lambda t: ["xh"], lambda t: T.fh[:, NH * t:NH * (t + 1)],
-                             lambda t: ["fh"], lambda t, a, b: T.au[:, a:b], lambda t: ["au"], A.add, a, b)
-            quant("mq", "mp", "mt", a, b, k, ["mq%d" % h])
+                tt(T.mt[:, 4 * a:4 * b], T.fm[:, 4 * a:4 * b], T.xh[:, 4 * a:4 * b], A.add, ["xh", "fm1"], ["mt1"])
+                quant("mq", "mp", "mt", a, b, ["mt1"], ["mq1"])
             for i in range(4):
-                mm(4 * h + i, "wq", "wp", 128 * i, "mq", "mp", a, b, True, True, ["wq", "wp", "mq%d" % h])
+                mm(4 * h + i, "wq", "wp", 128 * i, "mq", "mp", a, b, True, True, ["wq", "wp", "mq%d" % h, "mq0a"])
             for i in range(4):
                 out, src, key = T[Xn][:, 4 * a + i:4 * b:4], T["pb%d" % (4 * h + i)][:, 0:b - a], "%s%d%d" % (Xn, h, i)
                 if h == 1 and i % 2 == 0:
@@ -416,15 +457,19 @@ def rank_program(g, core, T, topo):
                     act(out, src, ACT.Copy, w=[key], ps=[4 * h + i], scale=0.03125)
         wrote[Xn + "0"] = wrote["%s12" % Xn]
         wrote[Xn + "1"] = wrote["%s13" % Xn]
+        if rd < R - 1:
+            cp(T.xd[:], T[Xn][:, 0:4 * MA], ["%s0%d" % (Xn, j) for j in range(4)], ["xd"])
 
     Xn = names[R]
-    for h, (a, b) in enumerate(pieces):
+    for h, (a, b) in enumerate(PIECES):
         if h == 1:
             quant("xq", "xp", Xn, a, b, [Xn + "0", Xn + "1"], ["xq1"])
         mm(h, "vq", "vp", 0, "xq", "xp", a, b, True, True, ["vq", "xq%d" % h])
         dma("Y", "oc%d" % h, T.oc[:, 4 * a:4 * b], T.xq[:, a:b].bitcast(dt.uint8), ["xq%d" % h])
-        cp(T.yt[:, a:b], T["pb%d" % h][:, 0:b - a], w=["yt%d" % h], ps=[h])
-        if h == 1:
+        if h == 0:
+            act(T.yt[:, a:b], T["pb%d" % h][:, 0:b - a], ACT.Copy, w=["yt%d" % h], ps=[h])
+        else:
+            cp(T.yt[:, a:b], T["pb%d" % h][:, 0:b - a], w=["yt%d" % h], ps=[h])
             for k in range(4):
                 dma("S", "os%d" % k, T.osc[4 * k:4 * k + 4, :], T.xp[32 * k:32 * k + 4, :], ["xq0", "xq1"])
         dma("Y", "y%d" % h, T.y[:, a:b], T.yt[:, a:b], ["yt%d" % h])

@@ -5,10 +5,42 @@ C, H, R, N = 448, 32, 2, 8
 HC = C // 2
 KC = C // 16
 NH = N * H
-MA = 256
 K4 = C // 4
+BIG = 2.0 ** 96
+PP = [0, 256, 448]
+PS = [0, 192, 320, 448]
+W = 128
 NS = 10
-PIECES = [(0, MA), (MA, C)]
+SUMS = [3, 0, 4, 1, 5, 2, 6]
+EVAC = "VSSSSSSVVSVS"
+BANKS = [4, 5, 6, 7, 0, 1, 2, 4, 5, 6, 7, 0]
+YB = [3, 1, 2]
+MA = max(PP[1], PS[1])
+
+ORDER = {
+    "Va": "one pqi0 pqi1 pqi2 pqi3 pqi4 bt pqf o10 o11 o12 ido o13 pm10 t1 pw1 pw0 xd0 oq",
+    "Vp": "dp z000 z001 z002 z003 c2u z100 zq00 zq10 z010 mask0 z012 msc0 zq01 tw10 tw00 dc vq hw0 z110 z112 oh12 zq11 "
+          "oh14 oh13 mask1 oh15 msc1 oh10 tw11 tw01 oh11 hw1 ohq3 oh18 oh16 oh19 oh24 oh17 oh21 oh23 oh22 ohq0 oh25 "
+          "ohq4 oh20 ohq1 oh27 ohq5 oh26 ohq2 ohq6 pt pt' deg1 pu lo cls1 cls0 th0 aa tht0 th1 csc tht1 ind0 ysc cum0 "
+          "bias ind1 cum1 deg0 an hu h41 h40 dm kr0 dsc kr1 r40 r41 bt bq asc lp am lc c2s a1u ru hs da eq a0u",
+    "Vs0": "ft1 ft3 z000 z100 zq00 zq10 z010 z012 mask0 zq01 msc0 z110 at0 z112 at0' zq11 au0 z020 mask1 z120 msc1 zq02 "
+           "zq12 au1 mt0 mask2 msc2 au2 mq0 mt1 xn00 mq1 mt2 mq2 xd0 xn13 xn20 xn22 xd1",
+    "Vs1": "ft1 ft3 z000 z100 zq00 zq10 z010 z012 mask0 zq01 msc0 z110 at0 z112 at0' zq11 au0 z020 mask1 z120 msc1 zq02 "
+           "zq12 au1 mt0 mask2 msc2 au2 mq0 mt1 xn00 mq1 mt2 xq0 mq2 xn13 xq1 xn20 xn22 xq2 yt2",
+    "Sa": "c1i scol k2 nscol nb far nth pm11 thr",
+    "Sp": "diag pre100 pre101 pre102 pre103 pre010 pre011 pre012 pre013 pre110 pre111 pre112 pre113 c2row ab1 ab7 ab2 "
+          "oh1 ab4 ab0 ab3 ab5 oh0 oh3 ab8 oh2 oh5 oh7 ab6 oh4 oh6 ab9 oh8 oh9 sl1 sl0 thr4 bdt bdy j01 j00 diag4 a1row "
+          "srow1 j10 j11 srow0 kap beta bu j30 j31 xh0 hrow xh1",
+    "Ss0": "ft0 ft2 pre100 pre010 pre110 pre020 pre120 fm0 fm1 fm2 xn01 xn02 xn03 xn10 xn11 xn21 xn12 xn23",
+    "Ss1": "ft0 ft2 pre100 pre010 pre110 pre020 pre120 fm0 fm1 fm2 xn01 xn03 xn02 xn10 xn12 xn11 yt0 xn21 xn23 yt1 os0 "
+           "os1 os2 os3",
+    "Pp": "0zq00 0zq10 1zq01 1zq11 3ohq3 4ohq3 3ohq0 4ohq0 3ohq4 4ohq4 3ohq1 4ohq1 3ohq5 4ohq5 3ohq2 3ohq6 4ohq2 4ohq6",
+    "Ps0": "4lp 5lp 6lp 7lp 0zq00 0zq10 1zq01 1zq11 2zq02 2zq12 4mq0 5mq0 6mq0 7mq0 4mq1 1mq1 0mq1 2mq1 6mq2 5mq2 7mq2 "
+           "0mq2",
+    "Ps1": "4lp 5lp 6lp 7lp 0zq00 0zq10 1zq01 1zq11 2zq02 2zq12 4mq0 5mq0 7mq0 6mq0 1mq1 0mq1 2mq1 4mq1 3xq0 6mq2 5mq2 "
+           "0mq2 7mq2 1xq1 2xq2",
+    "Pa": "",
+}
 Q8, U8, BF, F32, I32, U16 = "float8_e4m3fn_x4", "uint8", "bfloat16", "float32", "int32", "uint16"
 
 SCRATCH = {}
@@ -19,27 +51,33 @@ def _sb(dtype, **kw):
         SCRATCH[k] = ("sbuf", [128, n], dtype)
 
 
-_sb(BF, xa=4 * C, xb=4 * C, xc=4 * C, xh=4 * C, xd=4 * MA, z=8 * C, mt=4 * C, ft=4 * NH, fm=4 * C,
-    vt=512, one=512, pm1=1024, et=2048, sel=512, bd=640, th=1024, bt=512, bu=128, i16=MA, thr=MA, keep=MA, diag=H,
+_sb(BF, xa=4 * C, xb=4 * C, xc=4 * C, xh=4 * C, xd=4 * PP[1], z=8 * C, mt=4 * C, ft=4 * NH, fm=4 * C,
+    vt=512, one=512, pm1=1024, et=2048, bd=512, bt=512, bu=128, i16=MA, thr=MA, keep=MA, diag=H,
     ib=HC, mask=C, msc=C, hw=2 * KC, oh=7 * 4 * HC, ab=NS * HC, cls=C, ind=2 * C, cum=2 * C, junk=3 * C + 64,
-    c2row=C, am=C, asc=C, pre=8 * C, i4=C, thr4=MA, keep4=C, diag4=C, c2s=C, da=K4, at=K4)
-_sb(F32, ifl=C, urow=2, scol=2, kcol=2, nscol=2, nthr=2, nth2=4, srow=H, tab=8, c1f=2 * KC,
-    t1=2 * KC, t2=2 * KC, pk=2 * KC, dp=2 * KC, dc=KC, tw=2 * KC, acc=2, nbc=2, acca=2, bias=2, accc=2,
-    kr=H, dm=H, dsc=H, gt=2 * H, rank=2, hrow=H, hs=R * H, pt=KC, yt=C, pqf=8)
-_sb(I32, c1i=2 * KC, c2i=KC, pi=2, vi=HC, deg=C, pqi=8)
+    c2row=C, a1row=C, am=C, an=C, asc=C, pre=8 * C, i4=C, thr4=C, keep4=C, diag4=C, c2s=C, da=K4, at=K4,
+    kap=W, bt2=128, th=128, tht=128, k32=64, ysc=64)
+_sb(F32, ifl=C, urow=2, scol=2, k2=2, nscol=2, nth=4, srow=2 * H, tab=8, lo=HC, sl=128,
+    t1=2 * KC, pw=4 * KC, dp=2 * KC, dc=KC, tw=2 * KC, acc=4, csc=64, bias=2, accc=2,
+    kr=2 * H, dm=H, dsc=H, rank=2, hrow=H, hs=R * H, pt=KC, yt=C, pqf=10, nb=4)
+_sb(I32, c1i=2 * KC, c2i=KC, pi=2, deg=C, pqi=10)
 _sb(U16, o1=8 * KC, c2u=KC, ido=2, hu=2, h4=8, r4=8, ru=2, pu=KC, a0u=K4, a1u=K4, au=K4)
-_sb(Q8, wq=512, vq=128, oq=256, eq=512, selq=128, zq=2 * C, mq=C, xq=C, ohq=7 * HC, thq=256,
+_sb(Q8, wq=512, vq=128, oq=256, eq=512, zq=2 * C, mq=C, xq=C, ohq=7 * HC,
     bq0=128, bq1=128, lc0=NH, lc1=NH)
-_sb(U8, wp=512, vp=128, op=256, ep=512, selp=128, zp=2 * C, mp=C, xp=C, ohp=7 * HC, thp=256,
+_sb(U8, wp=512, vp=128, op=256, ep=512, zp=2 * C, mp=C, xp=C, ohp=7 * HC,
     bp0=128, bp1=128, lp0=NH, lp1=NH)
 for _b in range(8):
     SCRATCH["pb%d" % _b] = ("psum", [128, 512], F32)
 
-DMAS = ["c1", "x0", "x1", "c2", "v", "wc", "ws", "hl", "oc0", "oc1", "y0", "y1"] + ["os%d" % i for i in range(4)]
+DMAS = (["c1", "x0", "x1", "c2", "v", "wc", "ws", "hl"] + ["oc%d" % i for i in range(3)] + ["y%d" % i for i in range(3)]
+        + ["os%d" % i for i in range(4)])
 SEMAPHORES = ["V", "S", "P", "G", "sent", "arr0", "arr1"] + ["d_" + n for n in DMAS]
 
 A = AluOpType
 ACT = ActivationFunctionType
+
+
+def pieces(P):
+    return list(zip(P, P[1:]))
 
 
 def rank_program(g, core, T, topo):
@@ -47,81 +85,122 @@ def rank_program(g, core, T, topo):
     if rank is None:
         return
     Q = {"V": g.vector, "S": g.scalar, "P": g.tensor, "G": g, "Y": g.sync}
-    count = {}
-    clock = {q: {} for q in Q}
-    snap = {}
-    wrote, read = {}, {}
+    calls, phase, named = [], ["a"], {}
+    wrote, read, bank_use = {}, {}, {}
 
-    def wait(q, ev):
-        s, n = ev
-        if clock[q].get(s, 0) >= n:
-            return
-        Q[q].wait_ge(T.sem[s], n)
-        clock[q][s] = n
-        for k, m in snap.get(ev, {}).items():
-            if clock[q].get(k, 0) < m:
-                clock[q][k] = m
-
-    def op(q, call, r=(), w=(), ps=(), sem=None):
-        need = {}
-
-        def add(ev):
-            if ev is not None and need.get(ev[0], 0) < ev[1]:
-                need[ev[0]] = ev[1]
+    def op(q, call, r=(), w=(), ps=(), sem=None, arrival=None, name=None):
+        me, after, behind = len(calls), set(), set()
         for k in r:
-            add(wrote.get(k))
+            after.add(wrote[k])
         for k in w:
-            add(wrote.get(k))
-            for ev in read.get(k, {}).items():
-                add(ev)
+            if k in wrote:
+                after.add(wrote[k])
+            after.update(read.get(k, ()))
         for b in ps:
-            for ev in read.get(("ps", b), {}).items():
-                if ev[0] != q:
-                    add(ev)
-        for ev in need.items():
-            wait(q, ev)
-        s, step = (q, 1) if sem is None else (sem, 16)
-        count[s] = count.get(s, 0) + step
-        ev = (s, count[s])
-        call().then_inc(T.sem[s], step)
-        snap[ev] = dict(clock[q])
+            for i in bank_use.setdefault(b, []):
+                if calls[i]["q"] != q:
+                    after.add(i)
+                elif q == "P":
+                    behind.add(i)
+            bank_use[b].append(me)
         for k in r:
-            read.setdefault(k, {})[s] = ev[1]
+            read.setdefault(k, []).append(me)
         for k in w:
-            wrote[k] = ev
-            read[k] = {}
-        for b in ps:
-            read.setdefault(("ps", b), {})[s] = ev[1]
-        return ev
+            wrote[k] = me
+            read[k] = []
+        name = name or w[0]
+        while (q, phase[0], name) in named:
+            name += "'"
+        named[q, phase[0], name] = me
+        calls.append(dict(q=q, call=call, after=after, behind=behind, sem=sem, arrival=arrival, name=phase[0] + ":" + name))
+
+    def planned():
+        lines = {q: [i for i, c in enumerate(calls) if c["q"] == q] for q in "GY"}
+        for q in "VSP":
+            lines[q] = [named[q, p, n] for p in ("a", "p0", "s0", "p1", "s1")
+                        for n in ORDER.get(q + p, ORDER.get(q + p[0])).split() if (q, p, n) in named]
+        assert sorted(i for line in lines.values() for i in line) == list(range(len(calls)))
+        order, done, at = [], set(), {q: 0 for q in lines}
+        while len(order) < len(calls):
+            moved = False
+            for q, line in lines.items():
+                while at[q] < len(line) and (calls[line[at[q]]]["after"] | calls[line[at[q]]]["behind"]) <= done:
+                    order.append(line[at[q]])
+                    done.add(line[at[q]])
+                    at[q] += 1
+                    moved = True
+            assert moved
+        return order
+
+    def issue(order):
+        count, snap, done = {}, {}, {}
+        clock = {q: {} for q in Q}
+
+        def wait(q, ev):
+            s, n = ev
+            if clock[q].get(s, 0) >= n:
+                return
+            Q[q].wait_ge(T.sem[s], n)
+            clock[q][s] = n
+            for k, m in snap.get(ev, {}).items():
+                if clock[q].get(k, 0) < m:
+                    clock[q][k] = m
+        for i in order:
+            c = calls[i]
+            q, need = c["q"], {}
+            for ev in [done[j] for j in c["after"]] + ([c["arrival"]] if c["arrival"] else []):
+                need[ev[0]] = max(need.get(ev[0], 0), ev[1])
+            for ev in sorted(need.items()):
+                wait(q, ev)
+            if c["sem"] == "sent":
+                count["sent"] = count.get("sent", 0) + c["call"]()
+                done[i] = None
+                continue
+            s, step = (q, 1) if c["sem"] is None else (c["sem"], 16)
+            count[s] = count.get(s, 0) + step
+            done[i] = (s, count[s])
+            c["call"]().then_inc(T.sem[s], step)
+            snap[done[i]] = dict(clock[q])
+        for ev in count.items():
+            wait("G", ev)
 
     V, S, PE = g.vector, g.scalar, g.tensor
 
-    def ts(out, in0, s1, s2, o0, o1=None, r=(), w=(), ps=()):
+    def ts(out, in0, s1, s2, o0, o1=None, r=(), w=(), ps=(), name=None):
         if o1 is None:
-            return op("V", lambda: V.tensor_scalar(out, in0, s1, None, o0), r, w, ps)
-        return op("V", lambda: V.tensor_scalar(out, in0, s1, s2, o0, o1), r, w, ps)
+            return op("V", lambda: V.tensor_scalar(out, in0, s1, None, o0), r, w, ps, name=name)
+        return op("V", lambda: V.tensor_scalar(out, in0, s1, s2, o0, o1), r, w, ps, name=name)
 
     def tt(out, in0, in1, o, r=(), w=(), ps=()):
         return op("V", lambda: V.tensor_tensor(out, in0, in1, o), r, w, ps)
 
-    def cp(out, in_, r=(), w=(), ps=()):
-        return op("V", lambda: V.tensor_copy(out, in_), r, w, ps)
+    def cp(out, in_, r=(), w=(), name=None):
+        return op("V", lambda: V.tensor_copy(out, in_), r, w, name=name)
 
-    def scan(out, d0, d1, o0, o1, r=(), w=()):
-        return op("V", lambda: V.tensor_tensor_scan(out, d0, d1, 0.0, o0, o1), r, w)
+    def scan(out, d0, d1, o0, o1, r=(), w=(), first=0.0):
+        return op("V", lambda: V.tensor_tensor_scan(out, d0, d1, first, o0, o1), r, w)
 
-    def act(out, in_, f, r=(), w=(), ps=(), **kw):
-        return op("S", lambda: S.activation(out, in_, f, **kw), r, w, ps)
+    def turn(out, in_, r=(), w=()):
+        return op("V", lambda: V.transpose(out, in_), r, w)
 
-    def quant(q, p, tile, a, b, r=(), w=()):
-        return op("V", lambda: V.quantize_mx(T[q][:, a:b], T[p][:, a:b], T[tile][:, 4 * a:4 * b]), r, w)
+    def act(out, in_, f, r=(), w=(), ps=(), name=None, **kw):
+        return op("S", lambda: S.activation(out, in_, f, **kw), r, w, ps, name=name)
 
-    def mm(bank, lq, lp, la, rq, rp, a, b, start, stop, r=()):
+    def scaled(q, out, in_, k, w, ps, name=None):
+        if q == "V":
+            return ts(out, in_, k, None, A.mult, w=w, ps=ps, name=name)
+        return act(out, in_, ACT.Copy, w=w, ps=ps, name=name, scale=k)
+
+    def quant(q, p, tile, a, b, r=(), w=(), name=None):
+        return op("V", lambda: V.quantize_mx(T[q][:, a:b], T[p][:, a:b], T[tile][:, 4 * a:4 * b]), r, w, name=name)
+
+    def mm(bank, lq, lp, la, rq, rp, a, b, start, stop, r=(), arrival=None, name=None):
         return op("P", lambda: PE.matmul_mx(T["pb%d" % bank][:, 0:b - a], T[lq][:, la:la + 128], T[lp][:, la:la + 128],
-                                            T[rq][:, a:b], T[rp][:, a:b], start, stop), r, (), (bank,))
+                                            T[rq][:, a:b], T[rp][:, a:b], start, stop), r, (), (bank,), None, arrival,
+                  "%d%s" % (bank, name or r[-1]))
 
     def dma(q, name, out, in_, r=(), w=()):
-        return op(q, lambda: Q[q].dma_start(out, in_), r, w, (), "d_" + name)
+        return op(q, lambda: Q[q].dma_start(out, in_), r, w, (), "d_" + name, name=w[0] if w else name)
 
     def iota(out, pattern, base, cm, w):
         if out.dtype == dt.int32:
@@ -131,121 +210,102 @@ def rank_program(g, core, T, topo):
     def asel(out, in_, pattern, cmp, fill, base, cm, r, w):
         return op("G", lambda: g.affine_select(out, in_, pattern, cmp, fill, base, cm), r, w)
 
+    xa = PP[1]
     dma("S", "c1", T.c1i[:], T.c1[:], w=["c1i"])
-    dma("Y", "x0", T.xa[:, 0:4 * MA], T.x[:, 0:4 * MA], w=["xa0"])
-    wait("Y", dma("Y", "x1", T.xa[:, 4 * MA:], T.x[:, 4 * MA:], w=["xa1"]))
-    dma("Y", "c2", T.c2i[:], T.c2[:], w=["c2i"])
-    dma("Y", "wc", T.wq[:].bitcast(dt.uint8), T.wc[:], w=["wq"])
-    dma("Y", "ws", T.wp[:], T.ws[:], w=["wp"])
-    dma("Y", "v", T.vt[:], T.v[:], w=["vt"])
+    dma("Y", "x0", T.xa[:, 0:4 * xa], T.x[:, 0:4 * xa], w=["xa0"])
+    dma("Y", "x1", T.xa[:, 4 * xa:], T.x[:, 4 * xa:], w=["xa1"])
+    dma("Y", "c2", T.c2i[:], T.c2[:], ["xa1"], ["c2i"])
+    dma("Y", "wc", T.wq[:].bitcast(dt.uint8), T.wc[:], ["xa1"], ["wq"])
+    dma("Y", "ws", T.wp[:], T.ws[:], ["xa1"], ["wp"])
+    dma("Y", "v", T.vt[:], T.v[:], ["xa1"], ["vt"])
 
     op("V", lambda: V.memset(T.one[:], 1.0), w=["one"])
-    op("V", lambda: V.memset(T.th[:, 640:1024], 0.0), w=["thz"])
     op("V", lambda: V.memset(T.bt[:], 0.0), w=["bt"])
     iota(T.pi[:], [[0, 2]], 0, 1, ["pi"])
     iota(T.urow[:], [[16, 2]], 0, 0, ["urow"])
+    iota(T.bd[:], [[1, 8], [0, 64]], 0, 0, ["bd"])
     iota(T.i16[:], [[0, MA // 16], [1, 16]], 0, 0, ["i16"])
-    iota(T.bd[:, 0:512], [[1, 8], [0, 64]], 0, 0, ["bd"])
     iota(T.ib[:], [[1, HC]], 0, 0, ["ib"])
+    asel(T.keep[:], T.one[:, 0:MA], [[0, MA // 16], [1, 16]], A.not_equal, 0.0, 0, 0, ["one"], ["keep"])
     iota(T.ifl[:], [[1, C]], 0, 0, ["ifl"])
-    asel(T.sel[:], T.one[:], [[-1, 128], [1, 4]], A.is_equal, 0.0, 0, 0, ["one"], ["sel"])
+    iota(T.sl[:, 0:64], [[32, 2], [1024, 2], [2, 16]], 0, 0, ["sl0"])
+    iota(T.sl[:, 64:128], [[-32, 2], [1024, 2], [-2, 16]], 62, 0, ["sl1"])
+    asel(T.k32[:], T.one[:, 0:64], [[0, 2], [1, 32]], A.not_equal, 0.0, 0, 0, ["one"], ["k32"])
+    iota(T.tab[:, 0:4], [[1, 4]], 2 * C, 0, ["ta"])
+    iota(T.tab[:, 4:8], [[1, 4]], 2 * (H - 1), 0, ["tb"])
+    iota(T.i4[:], [[0, K4], [1, 4]], 0, 0, ["i4"])
+    asel(T.keep4[:], T.one[:, 0:C], [[0, K4], [1, 4]], A.not_equal, 0.0, 0, 0, ["one"], ["keep4"])
+    iota(T.kap[:], [[-1, W // 4], [0, 4]], W // 4, 0, ["kap"])
+    asel(T.kap[:], T.kap[:], [[0, W // 4], [1, 4]], A.is_equal, 1024.0, 0, 0, ["kap"], ["kap"])
+    for b in range(4):
+        asel(T.et[:, 512 * b:512 * (b + 1)], T.one[:], [[-1, 128], [1000, 4]], A.is_equal, 0.0, -1000 * b, 1,
+             ["one"], ["et%d" % b])
 
     ts(T.pqi[:, 0:2], T.pi[:], 2, 3, A.logical_shift_right, A.bitwise_and, ["pi"], ["pqi0"])
     ts(T.pqi[:, 2:4], T.pi[:], 3, None, A.bitwise_and, r=["pi"], w=["pqi1"])
     ts(T.pqi[:, 4:6], T.pi[:], 4, None, A.logical_shift_right, r=["pi"], w=["pqi2"])
     ts(T.pqi[:, 6:8], T.pi[:], 15, None, A.bitwise_and, r=["pi"], w=["pqi3"])
-    cp(T.pqf[:], T.pqi[:], ["pqi0", "pqi1", "pqi2", "pqi3"], ["pqf"])
-    pq, pe, pg, pm, pmf = T.pqf[:, 0:1], T.pqf[:, 2:3], T.pqf[:, 4:5], T.pqf[:, 6:7], T.pqf[:, 6:8]
-    tt(T.scol[:], T.urow[:], pmf, A.add, ["urow", "pqf"], ["scol"])
-    ts(T.nthr[:], pmf, -1.0, -128.5, A.mult, A.add, ["pqf"], ["nthr"])
-    ts(T.nth2[:, 2:4], pmf, 15.0, -1000.0, A.is_ge, A.mult, ["pqf"], ["nth3"])
-    ts(T.nth2[:, 0:2], T.nthr[:], 127.5625, T.nth2[:, 2:3], A.add, A.add, ["nthr", "nth3"], ["nth2"])
+    ts(T.pqi[:, 8:10], T.pi[:], 4, 1, A.logical_shift_right, A.bitwise_and, ["pi"], ["pqi4"])
+    cp(T.pqf[:], T.pqi[:], ["pqi%d" % i for i in range(5)], ["pqf"])
+    pe, pg, pmf = T.pqf[:, 2:3], T.pqf[:, 4:5], T.pqf[:, 6:8]
+    act(T.nb[:, 0:2], T.pqf[:, 0:7:6], ACT.Copy, ["pqf"], ["nb"], scale=-BIG)
+    act(T.scol[:], T.urow[:], ACT.Identity, ["urow", "pqf"], ["scol"], bias=T.pqf[:, 6:7])
+    act(T.nth[:, 0:2], pmf, ACT.Identity, ["pqf"], ["nth"], scale=-1.0, bias=-0.9375)
+    act(T.nth[:, 2:4], T.pqf[:, 8:10], ACT.Copy, ["pqf"], ["far"], scale=-1024.0)
+    act(T.k2[:], T.scol[:], ACT.Identity, ["scol"], ["k2"], scale=-2.0, bias=-1.0)
+    act(T.nscol[:], T.scol[:], ACT.Copy, ["scol"], ["nscol"], scale=-1.0 / 64)
+    cp(T.ido[:], T.scol[:], ["scol"], ["ido"])
     for t in range(4):
         ts(T.o1[:, 2 * KC * t:2 * KC * (t + 1)], T.c1i[:], 4.0, float(t), A.mult, A.add, ["c1i"], ["o1%d" % t])
-    cp(T.c1f[:], T.c1i[:], ["c1i"], ["c1f"])
-    ts(T.keep[:], T.i16[:], 0.0, None, A.not_equal, r=["i16"], w=["keep"])
-    ts(T.t1[:], T.c1f[:], float(HC), -float(HC), A.is_ge, A.mult, ["c1f"], ["t1"])
-    ts(T.t2[:], T.c1f[:], float(HC), 511.0 / 512, A.is_ge, A.mult, ["c1f"], ["t2"])
-    ts(T.thr[:], T.i16[:], pm, 1e29, A.not_equal, A.mult, ["i16", "pqf"], ["thr"])
-    tt(T.pk[:, 0:2 * KC:2], T.c1f[:, :KC], T.t1[:, :KC], A.add, ["c1f", "t1"], ["pk0"])
-    tt(T.dp[:, 0:2 * KC:2], T.c1f[:, KC:], T.t1[:, KC:], A.add, ["c1f", "t1"], ["dp0"])
-    ts(T.pk[:, 1:2 * KC:2], T.t2[:, :KC], 1.0 / 512, None, A.add, r=["t2"], w=["pk1"])
-    tt(T.dp[:, 1:2 * KC:2], T.t2[:, KC:], T.t2[:, :KC], A.subtract, ["t2"], ["dp1"])
-    tt(T.dp[:, 0:2 * KC:2], T.dp[:, 0:2 * KC:2], T.pk[:, 0:2 * KC:2], A.subtract, ["dp0", "pk0"], ["dp0"])
-    for u in range(2):
-        ts(T.pm1[:, 512 * u:512 * (u + 1)], T.bd[:, 0:512], pg, 1.0 - 2 * u, A.is_equal, A.mult,
-           ["bd", "pqf"], ["pm1%d" % u])
-    cp(T.xd[:], T.xa[:, 0:4 * MA], ["xa0"], ["xd"])
+    ts(T.pm1[:, 0:512], T.bd[:], pg, None, A.is_equal, r=["bd", "pqf"], w=["pm10"])
+    act(T.pm1[:, 512:1024], T.pm1[:, 0:512], ACT.Copy, ["pm10"], ["pm11"], scale=-1.0)
+    ts(T.t1[:], T.c1i[:], float(HC), -float(HC), A.is_ge, A.mult, ["c1i"], ["t1"])
+    ts(T.pw[:, 1:4 * KC:2], T.c1i[:], float(HC), 1.0 / 512, A.is_ge, A.max, ["c1i"], ["pw1"])
     quant("oq", "op", "pm1", 0, 256, ["pm10", "pm11"], ["oq"])
+    tt(T.pw[:, 0:4 * KC:2], T.t1[:], T.c1i[:], A.add, ["c1i", "t1"], ["pw0"])
+    act(T.thr[:], T.i16[:], ACT.Abs, ["i16", "nb"], ["thr"], scale=BIG, bias=T.nb[:, 1:2])
+    cp(T.xd[:], T.xa[:, 0:4 * xa], ["xa0"], ["xd0", "xd1"])
+    phase[0] = "p0"
+    tt(T.dp[:], T.pw[:, 2 * KC:], T.pw[:, :2 * KC], A.subtract, ["pw0", "pw1"], ["dp"])
 
-    iota(T.bd[:, 0:512], [[0, 8], [2, 16], [32, 4]], -C, 0, ["bd"])
-    iota(T.bd[:, 512:640], [[2, H], [1000, 4]], -C, 0, ["bd2"])
-    asel(T.bd[:, 0:512], T.bd[:, 0:512], [[-16, 8], [0, 64]], A.is_ge, 1000.0, 0, 1, ["bd"], ["bd"])
-    asel(T.bd[:, 0:512], T.bd[:, 0:512], [[16, 8], [0, 64]], A.is_ge, 1000.0, 15, -1, ["bd"], ["bd"])
-    iota(T.i4[:], [[0, K4], [1, 4]], 0, 0, ["i4"])
-    for b in range(4):
-        asel(T.et[:, 512 * b:512 * (b + 1)], T.one[:], [[-1, 128], [1000, 4]], A.is_equal, 0.0, -1000 * b, 1,
-             ["one"], ["et%d" % b])
+    zk = ["z%d%d%d" % (k, h, t) for k in range(2) for h in range(3) for t in range(4)]
 
-    def compare(X, xk, src, skey, parts, thr, keep, lists, filler):
-        def at(k, h):
-            a, b = PIECES[h]
-            return a, b, 2 * a + k * (b - a)
-        got = {}
-        for k, h in ((1, 0), (0, 1), (1, 1)):
-            a, b, o = at(k, h)
-            got[k, h] = []
-            for t, step, ap, keys in parts(k, a, b):
-                ks = ["pre%d%d%d" % (k, h, e) for e in (range(4) if step == 1 else [t])]
-                got[k, h] += ks
-                act(T.pre[:, 4 * o + t:4 * (o + b - a):step], ap, ACT.Copy, keys, ks)
-
-        def product(k, h, i=0, n=1):
-            a, b, o = at(k, h)
-            w = (b - a) // n
-            a, b, o = a + i * w, a + (i + 1) * w, o + i * w
-            tt(T.z[:, 4 * o:4 * (o + b - a)], T.pre[:, 4 * o:4 * (o + b - a)], T[X][:, 4 * a:4 * b], A.mult,
-               xk + got[k, h], ["z%d%d%d" % (k, h, i)])
-
-        def score(k, h):
-            a, b, o = at(k, h)
-            mm(h, "oq", "op", 128 * (1 - k), "zq", "zp", o, o + b - a, k == 0, k == 1, ["oq", "zq%d%d" % (k, h)])
-
-        def sign(h):
-            a, b = PIECES[h]
+    def compare(P, X, xk, first, fkey, parts, thr, carry, lists):
+        for h, (a, b) in enumerate(pieces(P)):
+            for k in range(2):
+                o = 2 * a + (k if h == 0 else 1 - k) * (b - a)
+                zs = ["z%d%d%d" % (k, h, t) for t in range(4)]
+                if h == 0 and k == 0:
+                    for t, step, ap, keys in parts(k, a, b):
+                        tt(T.z[:, t:4 * b:step], ap, T[first][:, t:4 * b:step], A.mult, keys + fkey,
+                           zs[t:t + 1] if step > 1 else zs)
+                else:
+                    got = ["pre%d%d%d" % (k, h, t) for t in range(4)]
+                    for t, step, ap, keys in parts(k, a, b):
+                        act(T.pre[:, 4 * o + t:4 * (o + b - a):step], ap, ACT.Copy, keys, got[t:t + 1] if step > 1 else got)
+                    n = 2 if h == 1 else 1
+                    for i in range(n):
+                        c, d = 4 * i * (b - a) // n, 4 * (i + 1) * (b - a) // n
+                        tt(T.z[:, 4 * o + c:4 * o + d], T.pre[:, 4 * o + c:4 * o + d], T[X][:, 4 * a + c:4 * a + d],
+                           A.mult, xk + got, zs[4 // n * i:4 // n * (i + 1)])
+                quant("zq", "zp", "z", o, o + b - a, zs, ["zq%d%d" % (k, h)])
+                mm(h, "oq", "op", 128 * (1 - k), "zq", "zp", o, o + b - a, k == 0, k == 1, ["oq", "zq%d%d" % (k, h)])
             tt(T.mask[:, a:b], T["pb%d" % h][:, 0:b - a], T[thr][:, 0:b - a], A.is_gt, [thr], ["mask%d" % h], [h])
+            run, o0, first0 = carry(h)
+            scan(T.msc[:, a:b], T[run][:, 0:b - a], T.mask[:, a:b], o0, A.add, [run, "mask%d" % h], ["msc%d" % h], first0)
+            lists(h, a, b)
 
-        def carry(h):
-            a, b = PIECES[h]
-            scan(T.msc[:, a:b], T[keep][:, 0:b - a], T.mask[:, a:b], A.mult, A.add, [keep, "mask%d" % h], ["msc%d" % h])
-        zk = ["zz%d" % t for t in range(4)]
-        for t, step, ap, keys in parts(0, 0, MA):
-            tt(T.z[:, t:4 * MA:step], ap, T[src][:, t:4 * MA:step], A.mult, keys + skey, zk[t:t + 1] if step > 1 else zk)
-        product(1, 0)
-        quant("zq", "zp", "z", 0, MA, zk, ["zq00"])
-        score(0, 0)
-        quant("zq", "zp", "z", MA, 2 * MA, ["z100"], ["zq10"])
-        score(1, 0)
-        product(0, 1)
-        sign(0)
-        quant("zq", "zp", "z", 2 * MA, MA + C, ["z010"], ["zq01"])
-        score(0, 1)
-        carry(0)
-        lists(0, lambda: product(1, 1, 0, 2))
-        product(1, 1, 1, 2)
-        filler(4)
-        quant("zq", "zp", "z", MA + C, 2 * C, ["z110", "z111"], ["zq11"])
-        score(1, 1)
-        filler(0)
-        sign(1)
-        filler(1)
-        carry(1)
-        filler(2)
-        lists(1, lambda: filler(3))
+    def fence(keys):
+        before = set()
+        for k in keys:
+            if k in wrote:
+                before.add(wrote[k])
+            before.update(read.get(k, ()))
+        for k in keys:
+            read[k] = sorted(before)
 
     m16 = T.msc[:, 15:C:16]
-    mk = ["msc0", "msc1"]
-    peers = [c for c in T.cores if c != core]
+    peers = [T.cores[(rank + i) % N] for i in range(1, N)]
     mask = topo.mask(core, peers[0])
     for c in peers:
         mask &= topo.mask(core, c)
@@ -253,225 +313,193 @@ def rank_program(g, core, T, topo):
     dsts = [DstId(rid=topo.addr(c)[0], pnc=topo.addr(c)[1]) for c in peers]
     names = ["xa", "xb", "xc"]
     ta, tb = T.tab[:, 0:4], T.tab[:, 4:8]
+    xk = ["xa0", "xa1"]
+    shared = (zk + ["pre" + k[1:] for k in zk] + ["zq%d%d" % (k, h) for k in range(2) for h in range(3)]
+              + ["mask%d" % h for h in range(3)] + ["msc%d" % h for h in range(3)])
 
     for rd in range(R):
         X, Xn = names[rd], names[rd + 1]
-        xk = [X + "0", X + "1"]
         bq, bp, lc, lp = "bq%d" % rd, "bp%d" % rd, "lc%d" % rd, "lp%d" % rd
+        mk = ["msc%d" % h for h in range(len(PP) - 1)]
+        phase[0] = "p%d" % rd
 
         def xparts(k, a, b):
             return [(t, 4, T[X][:, 0:4 * C].indirect(T.o1[:, KC * (2 * t + k) + a // 16:KC * (2 * t + k) + b // 16]),
                      xk + ["o1%d" % t]) for t in range(4)]
 
-        def ohrow(c):
-            s, t = divmod(c, 4)
-            return T.oh[:, 4 * HC * s + t:4 * HC * (s + 1):4]
+        def bins(h, a, b):
+            m, c, d = T.msc[:, a + 15:b:16], a // 8, b // 8
+            tt(T.tw[:, c:d:2], m, T.dp[:, c:d:2], A.mult, ["msc%d" % h, "dp"], ["tw0%d" % h])
+            tt(T.tw[:, c + 1:d:2], m, T.dp[:, c + 1:d:2], A.mult, ["msc%d" % h, "dp"], ["tw1%d" % h])
+            tt(T.hw[:, c:d], T.tw[:, c:d], T.pw[:, c:d], A.add, ["tw0%d" % h, "tw1%d" % h, "pw0", "pw1"], ["hw%d" % h])
+            for c in range(a // 16, b // 16):
+                s, t = divmod(c, 4)
+                row = T.oh[:, 4 * HC * s + t:4 * HC * (s + 1):4]
+                place, weight = T.hw[:, 2 * c:2 * c + 1], T.hw[:, 2 * c + 1:2 * c + 2]
+                if c < NS:
+                    off = T.ab[:, HC * c:HC * (c + 1)]
+                    act(off, T.ib[:], ACT.Abs, ["ib", "hw%d" % h], ["ab%d" % c], bias=place, scale=-1.0)
+                    act(row, off, ACT.Relu, ["ab%d" % c, "hw%d" % h], ["oh%d" % c], bias=weight, scale=-1.0)
+                else:
+                    ts(row, T.ib[:], place, weight, A.is_equal, A.mult, ["ib", "hw%d" % h], ["oh%d" % c])
 
-        def bins(h, gap):
-            a, b = PIECES[h]
-            m, a, b = T.msc[:, a + 15:b:16], a // 8, b // 8
-            tt(T.tw[:, a:b:2], m, T.dp[:, a:b:2], A.mult, ["msc%d" % h, "dp0"], ["tw0%d" % h])
-            tt(T.tw[:, a + 1:b:2], m, T.dp[:, a + 1:b:2], A.mult, ["msc%d" % h, "dp1"], ["tw1%d" % h])
-            if h == 1:
-                gap()
-            tt(T.hw[:, a:b], T.tw[:, a:b], T.pk[:, a:b], A.add, ["tw0%d" % h, "tw1%d" % h, "pk0", "pk1"], ["hw%d" % h])
-            if h == 0:
-                gap()
-                for c0 in range(0, NS, 4):
-                    cs = range(c0, min(NS, c0 + 4))
-                    for c in cs:
-                        act(T.ab[:, HC * c:HC * (c + 1)], T.ib[:], ACT.Abs, ["ib", "hw0"], ["ab%d" % c],
-                            bias=T.hw[:, 2 * c:2 * c + 1], scale=-1.0)
-                    for c in cs:
-                        act(ohrow(c), T.ab[:, HC * c:HC * (c + 1)], ACT.Relu, ["ab%d" % c, "hw0"], ["oh%d" % c],
-                            bias=T.hw[:, 2 * c + 1:2 * c + 2], scale=-1.0)
-
-        def onehot(cs):
-            for c in cs:
-                ts(ohrow(c), T.ib[:], T.hw[:, 2 * c:2 * c + 1], T.hw[:, 2 * c + 1:2 * c + 2],
-                   A.is_equal, A.mult, ["ib", "hw%d" % (c >= MA // 16)], ["oh%d" % c])
-
-        def summed(s, start=False, stop=False):
+        fence(shared)
+        compare(PP, X, xk, "xd", ["xd0", "xd1"], xparts, "thr", lambda h: ("keep", A.mult, 0.0), bins)
+        for s in SUMS:
             quant("ohq", "ohp", "oh", HC * s, HC * (s + 1), ["oh%d" % (4 * s + t) for t in range(4)], ["ohq%d" % s])
-            mm(2, "oq", "op", 0, "ohq", "ohp", HC * s, HC * (s + 1), start, stop, ["oq", "ohq%d" % s])
-        compare(X, xk, "xd", ["xd"], xparts, "thr", "keep", bins,
-                lambda i: onehot(([13, 14], [15], [NS], range(NS + 1, 12), [12])[i]))
-        summed(3, start=True)
-        onehot(range(16, 20))
-        summed(0)
-        onehot(range(20, 24))
-        summed(4)
-        onehot(range(24, 28))
-        summed(5)
-        summed(6)
-        summed(1)
-        summed(2, stop=True)
+            for bank in (3, 4):
+                mm(bank, "oq", "op", 0, "ohq", "ohp", HC * s, HC * (s + 1), s == SUMS[0], s == SUMS[-1], ["oq", "ohq%d" % s])
         if rd == 0:
-            quant("selq", "selp", "sel", 0, 128, ["sel"], ["selq"])
-            ts(T.kcol[:], T.scol[:], -1.0, 15.5, A.mult, A.add, ["scol"], ["kcol"])
-
-        ts(T.vi[:], T.pb2[:, 0:HC], 512.0, None, A.mult, w=["vi"], ps=[2])
-        act(T.junk[:, HC:C], T.pb2[:, 0:HC], ACT.Sign, ["nth2"], ["j01", "acc1"], [2], bias=T.nth2[:, 0:1], accum_out=T.acc[:, 1:2])
-        ts(T.deg[:, :HC], T.vi[:], 511, None, A.bitwise_and, r=["vi"], w=["deg0"])
-        ts(T.cls[:, :HC], T.deg[:, :HC], 15.0, 128.0, A.min, A.add, ["deg0"], ["cls0"])
-        act(T.junk[:, 0:HC], T.cls[:, :HC], ACT.Sign, ["cls0", "nthr"], ["j00", "acc0"], bias=T.nthr[:, 0:1], accum_out=T.acc[:, 0:1])
-        ts(T.cls[:, HC:], T.pb2[:, 0:HC], 127.5625, 143.0, A.add, A.min, w=["cls1"], ps=[2])
-        ts(T.th[:, 0:512], T.bd[:, 0:512], T.acc[:, 0:1], T.acc[:, 1:2], A.subtract, A.is_lt, ["bd", "acc0", "acc1"], ["th0"])
-        ts(T.th[:, 512:640], T.bd[:, 512:640], T.acc[:, 0:1], T.acc[:, 1:2], A.subtract, A.is_lt, ["bd2", "acc0", "acc1"], ["th1"])
-        quant("thq", "thp", "th", 0, 128, ["th0"], ["thq0"])
-        mm(3, "thq", "thp", 0, "selq", "selp", 0, 128, True, True, ["thq0", "selq"])
-        quant("thq", "thp", "th", 128, 256, ["th1", "thz"], ["thq1"])
-        mm(4, "oq", "op", 0, "thq", "thp", 128, 256, True, True, ["thq1", "oq"])
-        ts(T.deg[:, HC:], T.vi[:], 9, None, A.logical_shift_right, r=["vi"], w=["deg1"])
-        ts(T.nbc[:], T.pb3[:, 0:2], -1.0, -0.5, A.mult, A.add, w=["nbc"], ps=[3])
-        cl = ["cls0", "cls1"]
-        for u in range(2):
-            act(T.junk[:, 3 * C + H * u:3 * C + H * (u + 1)], T.pb4[:, 0:H], ACT.Sign, ["nbc"], ["j3%d" % u, "acca%d" % u], [4],
-                bias=T.nbc[:, u:u + 1], accum_out=T.acca[:, u:u + 1])
-        for u in range(2):
-            act(T.bias[:, u:u + 1], T.acca[:, u:u + 1], ACT.Identity, ["acca%d" % u, "kcol"], ["bias%d" % u],
-                bias=T.kcol[:, u:u + 1], scale=0.5)
-        for u in range(2):
-            a, b = C * u, C * (u + 1)
-            ts(T.ind[:, a:b], T.cls[:], T.nbc[:, u:u + 1], 127.5, A.add, A.is_equal, cl + ["nbc"], ["ind%d" % u])
-        for u in range(2):
-            a, b = C * u, C * (u + 1)
-            scan(T.cum[:, a:b], T.ind[:, a:b], T.ind[:, a:b], A.add, A.max, ["ind%d" % u], ["cum%d" % u])
-            act(T.junk[:, C + a:C + b], T.cum[:, a:b], ACT.Sign, ["cum%d" % u, "bias%d" % u], ["j1%d" % u, "accc%d" % u],
-                bias=T.bias[:, u:u + 1], accum_out=T.accc[:, u:u + 1])
-        if rd == 0:
-            ts(ta, T.ifl[:, 0:4], 0.5, float(C), A.mult, A.add, ["ifl"], ["ta"])
-            ts(T.diag[:], T.i16[:, 0:H], pm, None, A.is_equal, r=["i16", "pqf"], w=["diag"])
-            ts(T.srow[:], T.ifl[:, 0:H], 1.0 / 64, None, A.mult, r=["ifl"], w=["srow"])
-            ts(tb, T.ifl[:, 0:4], 0.25, None, A.mult, r=["ifl"], w=["tb"])
-            ts(T.nscol[:], T.scol[:], -1.0 / 64, None, A.mult, r=["scol"], w=["nscol"])
-            cp(T.ido[:], T.scol[:], ["scol"], ["ido"])
-            cp(T.c2u[:], T.c2i[:], ["c2i"], ["c2u"])
-        ak = ["accc0", "accc1"]
-        ts(T.hu[:], T.accc[:], -0.5, float(HC), A.mult, A.add, ak, ["hu"])
-        for u in range(2):
-            ts(T.h4[:, u:8:2], ta, T.accc[:, u:u + 1], 2.0, A.subtract, A.mult, ak + ["ta"], ["h4%d" % u])
-        dk = ["deg0", "deg1", "hu"]
-        tt(T.dm[:], T.deg[:, 0:C].indirect(T.hu[:]), T.diag[:, 0:H], A.mult, dk + ["diag"], ["dm"])
-        tt(T.kr[:], T.deg[:, 0:C].indirect(T.hu[:]), T.srow[:], A.subtract, dk + ["srow"], ["kr"])
-        act(T.bu[:], T[X][:, 0:4 * C].indirect(T.h4[:]), ACT.Copy, xk + ["h40", "h41"], ["bu"])
-        act(T.hrow[:], T.ifl[:, 0:C].indirect(T.hu[:]), ACT.Copy, ["ifl", "hu"], ["hrow"])
-        if rd == 0:
-            act(T.c2row[:], T.ifl[:, 0:NH].indirect(T.c2u[:]), ACT.Copy, ["ifl", "c2u"], ["c2row"])
-        act(T.xh[:], T[X][:], ACT.Copy, xk, ["xh"], scale=0.5)
-        scan(T.dsc[:], T.keep[:, 0:H], T.dm[:], A.mult, A.add, ["keep", "dm"], ["dsc"])
-        for u in range(2):
-            ts(T.gt[:, H * u:H * (u + 1)], T.kr[:], T.dsc[:, 16 * u + 15:16 * u + 16], T.nscol[:, u:u + 1],
-               A.subtract, A.is_gt, ["kr", "dsc", "nscol"], ["gt%d" % u])
-        for u in range(2):
-            op("V", lambda u=u: V.tensor_reduce(T.rank[:, u:u + 1], T.gt[:, H * u:H * (u + 1)], AxisListType.X, A.add),
-               ["gt%d" % u], ["rank%d" % u])
-        for u in range(2):
-            ts(T.r4[:, u:8:2], tb, T.rank[:, u:u + 1], 4.0, A.add, A.mult, ["tb", "rank%d" % u], ["r4%d" % u])
-        cp(T.bt[:, 0:4 * H].indirect(T.r4[:]), T.bu[:], ["r40", "r41", "bu"], ["bt"])
-        ev = quant(bq, bp, "bt", 0, 128, ["bt"], [bq])
-
-        wait("G", ev)
-        a, b = H * rank, H * (rank + 1)
-        arr = T.sem["arr%d" % rd]
-        g.remote_dma_fused([RemoteDMATransfer(dst_ids=dsts, dma_engine_mask=mask, remote_sem=arr,
-                                              src=T[bq][:, 0:H].bitcast(dt.uint8),
-                                              dsts=[T[lc][:, a:b].bitcast(dt.uint8) for c in peers])], local_sem=T.sem.sent)
-        g.remote_dma_fused([RemoteDMATransfer(dst_ids=dsts, dma_engine_mask=mask, remote_sem=arr,
-                                              src=T[bp][:, 0:H], dsts=[T[lp][:, a:b] for c in peers])], local_sem=T.sem.sent)
-        count["sent"] = count.get("sent", 0) + 2 * engines
-
-        if rd == 0:
-            tt(T.dc[:], T.c1f[:, KC:], T.c1f[:, :KC], A.subtract, ["c1f"], ["dc"])
-            ts(T.diag4[:], T.i4[:], pq, None, A.is_equal, r=["i4", "pqf"], w=["diag4"])
-            ts(T.keep4[:], T.i4[:], 0.0, None, A.not_equal, r=["i4"], w=["keep4"])
-        tt(T.pt[:], m16, T.dc[:], A.mult, mk + ["dc"], ["pt"])
-        cp(T[lc][:, a:b].bitcast(dt.uint32), T[bq][:, 0:128].bitcast(dt.uint32).indirect(T.ido[:]), [bq, "ido"], [lc])
-        cp(T[lp][:, a:b], T[bp][:, 0:128].indirect(T.ido[:]), [bq, "ido"], [lp])
-        tt(T.pt[:], T.pt[:], T.c1f[:, :KC], A.add, ["pt", "c1f"], ["pt"])
-        cp(T.ru[:], T.rank[:], ["rank0", "rank1"], ["ru"])
-        if rd == 0:
-            tt(T.am[:], T.c2row[:], T.diag4[:], A.mult, ["c2row", "diag4"], ["am"])
-            quant("eq", "ep", "et", 0, 512, ["et%d" % i for i in range(4)], ["eq"])
-            scan(T.c2s[:], T.keep4[:], T.am[:], A.mult, A.add, ["keep4", "am"], ["c2s"])
-        cp(T.pu[:], T.pt[:], ["pt"], ["pu"])
-        cp(T.hs[:, H * rd:H * (rd + 1)].indirect(T.ru[:]), T.hrow[:], ["ru", "hrow"], ["hs%d" % rd])
-        tt(T.am[:], T.c2row[:, 0:C].indirect(T.pu[:]), T.diag4[:], A.mult, ["c2row", "pu", "diag4"], ["am"])
-        if rd == 0:
-            ts(T.a0u[:], T.c2s[:, 3:C:4], 4.0, pe, A.mult, A.add, ["c2s", "pqf"], ["a0u"])
-            ts(T.thr4[:], T.i4[:, 0:MA], pq, 1e29, A.not_equal, A.mult, ["i4", "pqf"], ["thr4"])
+            for i in range(2):
+                act(T.sl[:, 64 * i:64 * (i + 1)], T.sl[:, 64 * i:64 * (i + 1)], ACT.Abs, ["sl%d" % i, "far"], ["sl%d" % i],
+                    bias=T.nth[:, 2:3])
+            act(T.bt2[:, 0:64], T.sl[:, 0:64], ACT.Identity, ["sl0"], ["bdt"], bias=-float(C))
+            act(T.bt2[:, 64:128], T.sl[:, 64:128], ACT.Identity, ["sl1"], ["bdy"], scale=-1.0, bias=62.0)
+            tt(T.dc[:], T.c1i[:, KC:], T.c1i[:, :KC], A.subtract, ["c1i"], ["dc"])
         else:
             quant("vq", "vp", "vt", 0, 128, ["vt"], ["vq"])
+
+        nth, a0, a1, aa = T.nth[:, 0:1], T.acc[:, 0:1], T.acc[:, 1:2], T.acc[:, 2:3]
+        ts(T.deg[:, HC:], T.pb3[:, 0:HC], -0.4375, None, A.add, w=["deg1"], ps=[3])
+        act(T.junk[:, HC:C], T.pb4[:, 0:HC], ACT.Sign, ["nth"], ["j01", "acc1"], [4], bias=nth, accum_out=a1)
+        tt(T.lo[:], T.pb3[:, 0:HC], T.deg[:, HC:], A.subtract, ["deg1"], ["lo"], [3])
+        act(T.junk[:, 0:HC], T.lo[:], ACT.Sign, ["lo", "nth"], ["j00", "acc0"], bias=nth, scale=512.0, accum_out=a0)
+        ts(T.cls[:, HC:], T.deg[:, HC:], 16.0, None, A.min, r=["deg1"], w=["cls1"])
+        ts(T.cls[:, :HC], T.lo[:], 512.0, 16.0, A.mult, A.min, ["lo"], ["cls0"])
+        if rd == 0:
+            cp(T.c2u[:], T.c2i[:], ["c2i"], ["c2u"])
+            act(T.diag[:], T.thr[:, 0:H], ACT.Relu, ["thr"], ["diag"], scale=-1.0, bias=1.0)
+            for u in range(2):
+                act(T.srow[:, H * u:H * (u + 1)], T.ifl[:, 0:H], ACT.Identity, ["ifl", "nscol"], ["srow%d" % u],
+                    scale=1.0 / 64, bias=T.nscol[:, u:u + 1])
+            act(T.c2row[:], T.ifl[:, 0:NH].indirect(T.c2u[:]), ACT.Copy, ["ifl", "c2u"], ["c2row"])
+        ts(T.th[:, 0:64], T.bt2[:, 0:64], a0, a1, A.subtract, A.is_lt, ["bdt", "acc0", "acc1"], ["th0"])
+        ts(aa, a0, a1, float(C), A.add, A.add, ["acc0", "acc1"], ["aa"])
+        turn(T.tht[:, 0:64], T.th[:, 0:64], ["th0"], ["tht0"])
+        ts(T.th[:, 64:128], T.bt2[:, 64:128], aa, aa, A.is_ge, A.mult, ["bdy", "aa"], ["th1"])
+        scan(T.csc[:], T.k32[:], T.tht[:, 0:64], A.mult, A.add, ["k32", "tht0"], ["csc"])
+        turn(T.tht[:, 64:128], T.th[:, 64:128], ["th1"], ["tht1"])
+        cl = ["cls0", "cls1", "csc"]
+        ts(T.ind[:, 0:C], T.cls[:], T.csc[:, 31:32], None, A.is_equal, r=cl, w=["ind0"])
+        scan(T.ysc[:], T.k32[:], T.tht[:, 64:128], A.mult, A.max, ["k32", "tht1"], ["ysc"])
+        scan(T.cum[:, 0:C], T.ind[:, 0:C], T.ind[:, 0:C], A.add, A.max, ["ind0"], ["cum0"])
+        tt(T.bias[:], T.ysc[:, 31:64:32], T.k2[:], A.add, ["ysc", "k2"], ["bias"])
+        ts(T.ind[:, C:], T.cls[:], T.csc[:, 63:64], None, A.is_equal, r=cl, w=["ind1"])
+        act(T.junk[:, C:2 * C], T.cum[:, 0:C], ACT.Sign, ["cum0", "bias"], ["j10", "accc0"],
+            bias=T.bias[:, 0:1], scale=2.0, accum_out=T.accc[:, 0:1])
+        tt(T.pt[:], m16, T.dc[:], A.mult, mk + ["dc"], ["pt"])
+        scan(T.cum[:, C:], T.ind[:, C:], T.ind[:, C:], A.add, A.max, ["ind1"], ["cum1"])
+        act(T.junk[:, 2 * C:3 * C], T.cum[:, C:], ACT.Sign, ["cum1", "bias"], ["j11", "accc1"],
+            bias=T.bias[:, 1:2], scale=2.0, accum_out=T.accc[:, 1:2])
+        ts(T.deg[:, :HC], T.lo[:], 512.0, None, A.mult, r=["lo"], w=["deg0"])
+        tt(T.pt[:], T.pt[:], T.c1i[:, :KC], A.add, ["pt", "c1i"], ["pt"])
+
+        a_0, a_1 = T.accc[:, 0:1], T.accc[:, 1:2]
+        ts(T.h4[:, 0:8:2], ta, a_0, a_0, A.subtract, A.subtract, ["accc0", "ta"], ["h40"])
+        cp(T.pu[:], T.pt[:], ["pt"], ["pu"])
+        ts(T.hu[:], T.accc[:], -0.5, float(HC), A.mult, A.add, ["accc0", "accc1"], ["hu"])
+        ts(T.h4[:, 1:8:2], ta, a_1, a_1, A.subtract, A.subtract, ["accc1", "ta"], ["h41"])
+        dk = ["deg0", "deg1", "hu"]
+        tt(T.dm[:], T.deg[:, 0:C].indirect(T.hu[:]), T.diag[:], A.mult, dk + ["diag"], ["dm"])
+        act(T.bu[:], T[X][:, 0:4 * C].indirect(T.h4[:]), ACT.Copy, xk + ["h40", "h41"], ["bu"])
+        tt(T.kr[:, 0:H], T.deg[:, 0:C].indirect(T.hu[:]), T.srow[:, 0:H], A.subtract, dk + ["srow0"], ["kr0"])
+        scan(T.dsc[:], T.keep[:, 0:H], T.dm[:], A.mult, A.subtract, ["keep", "dm"], ["dsc"])
+        tt(T.kr[:, H:], T.deg[:, 0:C].indirect(T.hu[:]), T.srow[:, H:], A.subtract, dk + ["srow1"], ["kr1"])
+        for u in range(2):
+            act(T.junk[:, 3 * C + H * u:3 * C + H * (u + 1)], T.kr[:, H * u:H * (u + 1)], ACT.Sign, ["kr%d" % u, "dsc"],
+                ["j3%d" % u, "rank%d" % u], bias=T.dsc[:, 16 * u + 15:16 * u + 16], accum_out=T.rank[:, u:u + 1])
+        for u in range(2):
+            ts(T.r4[:, u:8:2], tb, T.rank[:, u:u + 1], T.rank[:, u:u + 1], A.add, A.add, ["tb", "rank%d" % u], ["r4%d" % u])
+        cp(T.bt[:, 0:4 * H].indirect(T.r4[:]), T.bu[:], ["r40", "r41", "bu"], ["bt"])
+        quant(bq, bp, "bt", 0, 128, ["bt"], [bq], "bq")
+
+        a, b = H * rank, H * (rank + 1)
+
+        def send(src, land, arr=T.sem["arr%d" % rd]):
+            g.remote_dma_fused([RemoteDMATransfer(dst_ids=dsts, dma_engine_mask=mask, remote_sem=arr, src=src,
+                                                  dsts=[land for c in peers])], local_sem=T.sem.sent)
+            return engines
+        for src, land in ((T[bq][:, 0:H].bitcast(dt.uint8), T[lc][:, a:b].bitcast(dt.uint8)), (T[bp][:, 0:H], T[lp][:, a:b])):
+            op("G", lambda src=src, land=land, send=send: send(src, land), [bq], (), (), "sent", name="send")
+        read[bq] = []
+
+        act(T.a1row[:], T.c2row[:, 0:C].indirect(T.pu[:]), ACT.Copy, ["c2row", "pu"], ["a1row"])
+        act(T.hrow[:], T.ifl[:, 0:C].indirect(T.hu[:]), ACT.Copy, ["ifl", "hu"], ["hrow"])
+        if rd == 0:
+            act(T.thr4[:], T.i4[:], ACT.Abs, ["i4", "nb"], ["thr4"], scale=BIG, bias=T.nb[:, 0:1])
+            act(T.kap[:], T.kap[:], ACT.Copy, ["kap"], ["kap"], scale=4.0 / W)
+            act(T.nb[:, 2:4], pmf, ACT.Identity, ["pqf"], ["beta"], bias=8.0 * W)
+            act(T.diag4[:], T.thr4[:], ACT.Relu, ["thr4"], ["diag4"], scale=-1.0, bias=1.0)
+        for i in range(2):
+            act(T.xh[:, 2 * C * i:2 * C * (i + 1)], T[X][:, 2 * C * i:2 * C * (i + 1)], ACT.Copy, xk, ["xh%d" % i], scale=0.5)
+        cp(T[lc][:, a:b].bitcast(dt.uint32), T[bq][:, 0:128].bitcast(dt.uint32).indirect(T.ido[:]), [bq, "ido"], [lc], "lc")
+        cp(T[lp][:, a:b], T[bp][:, 0:128].indirect(T.ido[:]), [bq, "ido"], [lp], "lp")
+        ts(T.ru[:], T.rank[:], 0.5, (H - 1) / 2, A.mult, A.add, ["rank0", "rank1"], ["ru"])
+        if rd == 0:
+            quant("eq", "ep", "et", 0, 512, ["et%d" % i for i in range(4)], ["eq"])
+        cp(T.hs[:, H * rd:H * (rd + 1)].indirect(T.ru[:]), T.hrow[:], ["ru", "hrow"], ["hs%d" % rd], "hs")
+        if rd == 0:
+            tt(T.am[:], T.c2row[:], T.diag4[:], A.mult, ["c2row", "diag4"], ["am"])
+        else:
             dma("Y", "hl", T.hl[:], T.hs[0:128:16, :], ["hs0", "hs1"])
-        scan(T.asc[:], T.keep4[:], T.am[:], A.mult, A.add, ["keep4", "am"], ["asc"])
+        tt(T.an[:], T.a1row[:], T.diag4[:], A.mult, ["a1row", "diag4"], ["an"])
+        if rd == 0:
+            scan(T.c2s[:], T.keep4[:], T.am[:], A.mult, A.add, ["keep4", "am"], ["c2s"])
+        scan(T.asc[:], T.keep4[:], T.an[:], A.mult, A.add, ["keep4", "an"], ["asc"])
+        if rd == 0:
+            ts(T.a0u[:], T.c2s[:, 3:C:4], 4.0, pe, A.mult, A.add, ["c2s", "pqf"], ["a0u"])
         ts(T.a1u[:], T.asc[:, 3:C:4], 4.0, pe, A.mult, A.add, ["asc", "pqf"], ["a1u"])
-        tt(T.da[:], T.asc[:, 3:C:4], T.c2s[:, 3:C:4], A.subtract, ["asc", "c2s"], ["da"])
+        tt(T.da[:, 0:PS[1] // 4], T.asc[:, 3:PS[1]:4], T.c2s[:, 3:PS[1]:4], A.subtract, ["asc", "c2s"], ["da"])
 
-        wait("P", ("arr%d" % rd, 2 * engines * len(peers)))
-        for b in range(4):
-            mm(4 + b, "eq", "ep", 128 * b, lc, lp, 0, NH, True, True, ["eq", lc, lp])
-        for b in range(4):
-            out, src = T.ft[:, b:4 * NH:4], T["pb%d" % (4 + b)][:, 0:NH]
-            if b % 2 == 1:
-                cp(out, src, w=["ft%d" % b], ps=[4 + b])
-            else:
-                act(out, src, ACT.Copy, w=["ft%d" % b], ps=[4 + b])
-
-        fk = ["ft%d" % b for b in range(4)]
+        phase[0] = "s%d" % rd
+        for i in range(4):
+            mm(4 + i, "eq", "ep", 128 * i, lc, lp, 0, NH, True, True, ["eq", lc, lp],
+               ("arr%d" % rd, 2 * engines * len(peers)), "lp")
+        for i in range(4):
+            scaled("SV"[i % 2], T.ft[:, i:4 * NH:4], T["pb%d" % (4 + i)][:, 0:NH], 1.0, ["ft%d" % i], [4 + i])
+        fk = ["ft%d" % i for i in range(4)]
 
         def fparts(k, a, b):
             off = "a%du" % k
             return [(0, 1, T.ft[:, 0:4 * NH].indirect(T[off][:, a // 4:b // 4]), fk + [off])]
 
-        def chosen(h, gap):
-            a, b = PIECES[h]
+        def chosen(h, a, b):
             c, d = a // 4, b // 4
-            tt(T.at[:, c:d], T.msc[:, a + 3:b:4], T.da[:, c:d], A.mult, ["msc%d" % h, "da"], ["at%d" % h])
-            gap()
-            tt(T.at[:, c:d], T.at[:, c:d], T.c2s[:, a + 3:b:4], A.add, ["at%d" % h, "c2s"], ["at%d" % h])
-            ts(T.au[:, c:d], T.at[:, c:d], 4.0, pe, A.mult, A.add, ["at%d" % h, "pqf"], ["au%d" % h])
-            act(T.fm[:, 4 * a:4 * b], T.ft[:, 0:4 * NH].indirect(T.au[:, c:d]), ACT.Copy, fk + ["au%d" % h],
-                ["fm%d" % h], scale=0.5)
-        compare(X, xk, X, xk, fparts, "thr4", "keep4", chosen, lambda i: None)
-
-        for h, (a, b) in enumerate(PIECES):
             if h == 0:
-                k = ["mt00", "mt01"]
-                for i in range(2):
-                    c, d = 2 * MA * i, 2 * MA * (i + 1)
-                    tt(T.mt[:, c:d], T.fm[:, c:d], T.xh[:, c:d], A.add, ["xh", "fm0"], k[i:i + 1])
-                quant("mq", "mp", "mt", 0, MA // 2, k[0:1], ["mq0a"])
-                quant("mq", "mp", "mt", MA // 2, MA, k[1:2], ["mq0"])
+                tt(T.at[:, c:d], T.msc[:, a + 3:b:4], T.da[:, c:d], A.mult, ["msc0", "da"], ["at0"])
+                tt(T.at[:, c:d], T.at[:, c:d], T.c2s[:, a + 3:b:4], A.add, ["at0", "c2s"], ["at0"])
+                ts(T.au[:, c:d], T.at[:, c:d], 4.0, pe, A.mult, A.add, ["at0", "pqf"], ["au0"])
+                win, keys = T.ft[:, 0:4 * NH], fk
             else:
-                tt(T.mt[:, 4 * a:4 * b], T.fm[:, 4 * a:4 * b], T.xh[:, 4 * a:4 * b], A.add, ["xh", "fm1"], ["mt1"])
-                quant("mq", "mp", "mt", a, b, ["mt1"], ["mq1"])
-            for i in range(4):
-                mm(4 * h + i, "wq", "wp", 128 * i, "mq", "mp", a, b, True, True, ["wq", "wp", "mq%d" % h, "mq0a"])
-            for i in range(4):
-                out, src, key = T[Xn][:, 4 * a + i:4 * b:4], T["pb%d" % (4 * h + i)][:, 0:b - a], "%s%d%d" % (Xn, h, i)
-                if h == 1 and i % 2 == 0:
-                    if i == 0 and rd == R - 1:
-                        quant("xq", "xp", Xn, 0, MA, ["%s0%d" % (Xn, j) for j in range(4)], ["xq0"])
-                    ts(out, src, 0.03125, None, A.mult, w=[key], ps=[4 * h + i])
-                else:
-                    act(out, src, ACT.Copy, w=[key], ps=[4 * h + i], scale=0.03125)
-        wrote[Xn + "0"] = wrote["%s12" % Xn]
-        wrote[Xn + "1"] = wrote["%s13" % Xn]
-        if rd < R - 1:
-            cp(T.xd[:], T[Xn][:, 0:4 * MA], ["%s0%d" % (Xn, j) for j in range(4)], ["xd"])
+                ts(T.au[:, c:d], T.msc[:, a + 3:b:4], -4.0 * W, T.nb[:, 2:3], A.mult, A.add, ["msc%d" % h, "beta"], ["au%d" % h])
+                win, keys = T.pre[:, 8 * a:8 * b], ["pre0%d0" % h, "pre1%d0" % h]
+            act(T.fm[:, 4 * a:4 * b], win.indirect(T.au[:, c:d]), ACT.Copy, keys + ["au%d" % h], ["fm%d" % h], scale=0.5)
+            tt(T.mt[:, 4 * a:4 * b], T.fm[:, 4 * a:4 * b], T.xh[:, 4 * a:4 * b], A.add, ["xh0", "xh1", "fm%d" % h], ["mt%d" % h])
 
-    Xn = names[R]
-    for h, (a, b) in enumerate(PIECES):
-        if h == 1:
-            quant("xq", "xp", Xn, a, b, [Xn + "0", Xn + "1"], ["xq1"])
-        mm(h, "vq", "vp", 0, "xq", "xp", a, b, True, True, ["vq", "xq%d" % h])
-        dma("Y", "oc%d" % h, T.oc[:, 4 * a:4 * b], T.xq[:, a:b].bitcast(dt.uint8), ["xq%d" % h])
-        if h == 0:
-            act(T.yt[:, a:b], T["pb%d" % h][:, 0:b - a], ACT.Copy, w=["yt%d" % h], ps=[h])
-        else:
-            cp(T.yt[:, a:b], T["pb%d" % h][:, 0:b - a], w=["yt%d" % h], ps=[h])
-            for k in range(4):
-                dma("S", "os%d" % k, T.osc[4 * k:4 * k + 4, :], T.xp[32 * k:32 * k + 4, :], ["xq0", "xq1"])
-        dma("Y", "y%d" % h, T.y[:, a:b], T.yt[:, a:b], ["yt%d" % h])
-    for s, n in count.items():
-        wait("G", (s, n))
+        fence(shared)
+        compare(PS, X, xk, X, xk, fparts, "thr4", lambda h: ("kap", A.min, 4.0) if h else ("keep4", A.mult, 0.0), chosen)
+
+        xk = []
+        for h, (a, b) in enumerate(pieces(PS)):
+            quant("mq", "mp", "mt", a, b, ["mt%d" % h], ["mq%d" % h])
+            for i in range(4):
+                mm(BANKS[4 * h + i], "wq", "wp", 128 * i, "mq", "mp", a, b, True, True, ["wq", "wp", "mq%d" % h])
+            ks = ["%s%d%d" % (Xn, h, i) for i in range(4)]
+            for i in range(4):
+                bank = BANKS[4 * h + i]
+                scaled(EVAC[4 * h + i], T[Xn][:, 4 * a + i:4 * b:4], T["pb%d" % bank][:, 0:b - a], 0.03125, ks[i:i + 1], [bank],
+                       "xn%d%d" % (h, i))
+            xk = xk + ks
+            if rd < R - 1 and a < xa:
+                e = min(b, xa)
+                cp(T.xd[:, 4 * a:4 * e], T[Xn][:, 4 * a:4 * e], ks, ["xd%d" % h])
+            if rd == R - 1:
+                bank = YB[h]
+                quant("xq", "xp", Xn, a, b, ks, ["xq%d" % h])
+                mm(bank, "vq", "vp", 0, "xq", "xp", a, b, True, True, ["vq", "xq%d" % h])
+                dma("Y", "oc%d" % h, T.oc[:, 4 * a:4 * b], T.xq[:, a:b].bitcast(dt.uint8), ["xq%d" % h])
+                scaled("V" if b == C else "S", T.yt[:, a:b], T["pb%d" % bank][:, 0:b - a], 1.0, ["yt%d" % h], [bank])
+                dma("Y", "y%d" % h, T.y[:, a:b], T.yt[:, a:b], ["yt%d" % h])
+    for k in range(4):
+        dma("S", "os%d" % k, T.osc[4 * k:4 * k + 4, :], T.xp[32 * k:32 * k + 4, :], ["xq%d" % h for h in range(len(PS) - 1)])
+    issue(planned())

from concourse.bass import DstId, RemoteDMATransfer
from concourse.mybir import dt, AluOpType, AxisListType, ActivationFunctionType

C, H, R, N = 448, 32, 2, 8
HC = C // 2
KC = C // 16
NH = N * H
K4 = C // 4
BIG = 2.0 ** 96
PP = [0, 256, 448]
PS = [0, 192, 320, 448]
W = 128
NS = 10
SUMS = [3, 0, 4, 1, 5, 2, 6]
EVAC = "VSSSSSSVVSVS"
BANKS = [4, 5, 6, 7, 0, 1, 2, 4, 5, 6, 7, 0]
YB = [3, 1, 2]
MA = max(PP[1], PS[1])

ORDER = {
    "Va": "one pqi0 pqi1 pqi2 pqi3 pqi4 bt pqf o10 o11 o12 ido o13 pm10 t1 pw1 pw0 xd0 oq",
    "Vp": "dp z000 z001 z002 z003 c2u z100 zq00 zq10 z010 mask0 z012 msc0 zq01 tw10 tw00 dc vq hw0 z110 z112 oh12 zq11 "
          "oh14 oh13 mask1 oh15 msc1 oh10 tw11 tw01 oh11 hw1 ohq3 oh18 oh16 oh19 oh24 oh17 oh21 oh23 oh22 ohq0 oh25 "
          "ohq4 oh20 ohq1 oh27 ohq5 oh26 ohq2 ohq6 pt pt' deg1 pu lo cls1 cls0 th0 aa tht0 th1 csc tht1 ind0 ysc cum0 "
          "bias ind1 cum1 deg0 an hu h41 h40 dm kr0 dsc kr1 r40 r41 bt bq asc lp am lc c2s a1u ru hs da eq a0u",
    "Vs0": "ft1 ft3 z000 z100 zq00 zq10 z010 z012 mask0 zq01 msc0 z110 at0 z112 at0' zq11 au0 z020 mask1 z120 msc1 zq02 "
           "zq12 au1 mt0 mask2 msc2 au2 mq0 mt1 xn00 mq1 mt2 mq2 xd0 xn13 xn20 xn22 xd1",
    "Vs1": "ft1 ft3 z000 z100 zq00 zq10 z010 z012 mask0 zq01 msc0 z110 at0 z112 at0' zq11 au0 z020 mask1 z120 msc1 zq02 "
           "zq12 au1 mt0 mask2 msc2 au2 mq0 mt1 xn00 mq1 mt2 xq0 mq2 xn13 xq1 xn20 xn22 xq2 yt2",
    "Sa": "c1i scol k2 nscol nb far nth pm11 thr",
    "Sp": "diag pre100 pre101 pre102 pre103 pre010 pre011 pre012 pre013 pre110 pre111 pre112 pre113 c2row ab1 ab7 ab2 "
          "oh1 ab4 ab0 ab3 ab5 oh0 oh3 ab8 oh2 oh5 oh7 ab6 oh4 oh6 ab9 oh8 oh9 sl1 sl0 thr4 bdt bdy j01 j00 diag4 a1row "
          "srow1 j10 j11 srow0 kap beta bu j30 j31 xh0 hrow xh1",
    "Ss0": "ft0 ft2 pre100 pre010 pre110 pre020 pre120 fm0 fm1 fm2 xn01 xn02 xn03 xn10 xn11 xn21 xn12 xn23",
    "Ss1": "ft0 ft2 pre100 pre010 pre110 pre020 pre120 fm0 fm1 fm2 xn01 xn03 xn02 xn10 xn12 xn11 yt0 xn21 xn23 yt1 os0 "
           "os1 os2 os3",
    "Pp": "0zq00 0zq10 1zq01 1zq11 3ohq3 4ohq3 3ohq0 4ohq0 3ohq4 4ohq4 3ohq1 4ohq1 3ohq5 4ohq5 3ohq2 3ohq6 4ohq2 4ohq6",
    "Ps0": "4lp 5lp 6lp 7lp 0zq00 0zq10 1zq01 1zq11 2zq02 2zq12 4mq0 5mq0 6mq0 7mq0 4mq1 1mq1 0mq1 2mq1 6mq2 5mq2 7mq2 "
           "0mq2",
    "Ps1": "4lp 5lp 6lp 7lp 0zq00 0zq10 1zq01 1zq11 2zq02 2zq12 4mq0 5mq0 7mq0 6mq0 1mq1 0mq1 2mq1 4mq1 3xq0 6mq2 5mq2 "
           "0mq2 7mq2 1xq1 2xq2",
    "Pa": "",
}
Q8, U8, BF, F32, I32, U16 = "float8_e4m3fn_x4", "uint8", "bfloat16", "float32", "int32", "uint16"

SCRATCH = {}


def _sb(dtype, **kw):
    for k, n in kw.items():
        SCRATCH[k] = ("sbuf", [128, n], dtype)


_sb(BF, xa=4 * C, xb=4 * C, xc=4 * C, xh=4 * C, xd=4 * PP[1], z=8 * C, mt=4 * C, ft=4 * NH, fm=4 * C,
    vt=512, one=512, pm1=1024, et=2048, bd=512, bt=512, bu=128, i16=MA, thr=MA, keep=MA, diag=H,
    ib=HC, mask=C, msc=C, hw=2 * KC, oh=7 * 4 * HC, ab=NS * HC, cls=C, ind=2 * C, cum=2 * C, junk=3 * C + 64,
    c2row=C, a1row=C, am=C, an=C, asc=C, pre=8 * C, i4=C, thr4=C, keep4=C, diag4=C, c2s=C, da=K4, at=K4,
    kap=W, bt2=128, th=128, tht=128, k32=64, ysc=64)
_sb(F32, ifl=C, urow=2, scol=2, k2=2, nscol=2, nth=4, srow=2 * H, tab=8, lo=HC, sl=128,
    t1=2 * KC, pw=4 * KC, dp=2 * KC, dc=KC, tw=2 * KC, acc=4, csc=64, bias=2, accc=2,
    kr=2 * H, dm=H, dsc=H, rank=2, hrow=H, hs=R * H, pt=KC, yt=C, pqf=10, nb=4)
_sb(I32, c1i=2 * KC, c2i=KC, pi=2, deg=C, pqi=10)
_sb(U16, o1=8 * KC, c2u=KC, ido=2, hu=2, h4=8, r4=8, ru=2, pu=KC, a0u=K4, a1u=K4, au=K4)
_sb(Q8, wq=512, vq=128, oq=256, eq=512, zq=2 * C, mq=C, xq=C, ohq=7 * HC,
    bq0=128, bq1=128, lc0=NH, lc1=NH)
_sb(U8, wp=512, vp=128, op=256, ep=512, zp=2 * C, mp=C, xp=C, ohp=7 * HC,
    bp0=128, bp1=128, lp0=NH, lp1=NH)
for _b in range(8):
    SCRATCH["pb%d" % _b] = ("psum", [128, 512], F32)

DMAS = (["c1", "x0", "x1", "c2", "v", "wc", "ws", "hl"] + ["oc%d" % i for i in range(3)] + ["y%d" % i for i in range(3)]
        + ["os%d" % i for i in range(4)])
SEMAPHORES = ["V", "S", "P", "G", "sent", "arr0", "arr1"] + ["d_" + n for n in DMAS]

A = AluOpType
ACT = ActivationFunctionType


def pieces(P):
    return list(zip(P, P[1:]))


def rank_program(g, core, T, topo):
    rank = T.rank_of(core)
    if rank is None:
        return
    Q = {"V": g.vector, "S": g.scalar, "P": g.tensor, "G": g, "Y": g.sync}
    calls, phase, named = [], ["a"], {}
    wrote, read, bank_use = {}, {}, {}

    def op(q, call, r=(), w=(), ps=(), sem=None, arrival=None, name=None):
        me, after, behind = len(calls), set(), set()
        for k in r:
            after.add(wrote[k])
        for k in w:
            if k in wrote:
                after.add(wrote[k])
            after.update(read.get(k, ()))
        for b in ps:
            for i in bank_use.setdefault(b, []):
                if calls[i]["q"] != q:
                    after.add(i)
                elif q == "P":
                    behind.add(i)
            bank_use[b].append(me)
        for k in r:
            read.setdefault(k, []).append(me)
        for k in w:
            wrote[k] = me
            read[k] = []
        name = name or w[0]
        while (q, phase[0], name) in named:
            name += "'"
        named[q, phase[0], name] = me
        calls.append(dict(q=q, call=call, after=after, behind=behind, sem=sem, arrival=arrival, name=phase[0] + ":" + name))

    def planned():
        lines = {q: [i for i, c in enumerate(calls) if c["q"] == q] for q in "GY"}
        for q in "VSP":
            lines[q] = [named[q, p, n] for p in ("a", "p0", "s0", "p1", "s1")
                        for n in ORDER.get(q + p, ORDER.get(q + p[0])).split() if (q, p, n) in named]
        assert sorted(i for line in lines.values() for i in line) == list(range(len(calls)))
        order, done, at = [], set(), {q: 0 for q in lines}
        while len(order) < len(calls):
            moved = False
            for q, line in lines.items():
                while at[q] < len(line) and (calls[line[at[q]]]["after"] | calls[line[at[q]]]["behind"]) <= done:
                    order.append(line[at[q]])
                    done.add(line[at[q]])
                    at[q] += 1
                    moved = True
            assert moved
        return order

    def issue(order):
        count, snap, done = {}, {}, {}
        clock = {q: {} for q in Q}

        def wait(q, ev):
            s, n = ev
            if clock[q].get(s, 0) >= n:
                return
            Q[q].wait_ge(T.sem[s], n)
            clock[q][s] = n
            for k, m in snap.get(ev, {}).items():
                if clock[q].get(k, 0) < m:
                    clock[q][k] = m
        for i in order:
            c = calls[i]
            q, need = c["q"], {}
            for ev in [done[j] for j in c["after"]] + ([c["arrival"]] if c["arrival"] else []):
                need[ev[0]] = max(need.get(ev[0], 0), ev[1])
            for ev in sorted(need.items()):
                wait(q, ev)
            if c["sem"] == "sent":
                count["sent"] = count.get("sent", 0) + c["call"]()
                done[i] = None
                continue
            s, step = (q, 1) if c["sem"] is None else (c["sem"], 16)
            count[s] = count.get(s, 0) + step
            done[i] = (s, count[s])
            c["call"]().then_inc(T.sem[s], step)
            snap[done[i]] = dict(clock[q])
        for ev in count.items():
            wait("G", ev)

    V, S, PE = g.vector, g.scalar, g.tensor

    def ts(out, in0, s1, s2, o0, o1=None, r=(), w=(), ps=(), name=None):
        if o1 is None:
            return op("V", lambda: V.tensor_scalar(out, in0, s1, None, o0), r, w, ps, name=name)
        return op("V", lambda: V.tensor_scalar(out, in0, s1, s2, o0, o1), r, w, ps, name=name)

    def tt(out, in0, in1, o, r=(), w=(), ps=()):
        return op("V", lambda: V.tensor_tensor(out, in0, in1, o), r, w, ps)

    def cp(out, in_, r=(), w=(), name=None):
        return op("V", lambda: V.tensor_copy(out, in_), r, w, name=name)

    def scan(out, d0, d1, o0, o1, r=(), w=(), first=0.0):
        return op("V", lambda: V.tensor_tensor_scan(out, d0, d1, first, o0, o1), r, w)

    def turn(out, in_, r=(), w=()):
        return op("V", lambda: V.transpose(out, in_), r, w)

    def act(out, in_, f, r=(), w=(), ps=(), name=None, **kw):
        return op("S", lambda: S.activation(out, in_, f, **kw), r, w, ps, name=name)

    def scaled(q, out, in_, k, w, ps, name=None):
        if q == "V":
            return ts(out, in_, k, None, A.mult, w=w, ps=ps, name=name)
        return act(out, in_, ACT.Copy, w=w, ps=ps, name=name, scale=k)

    def quant(q, p, tile, a, b, r=(), w=(), name=None):
        return op("V", lambda: V.quantize_mx(T[q][:, a:b], T[p][:, a:b], T[tile][:, 4 * a:4 * b]), r, w, name=name)

    def mm(bank, lq, lp, la, rq, rp, a, b, start, stop, r=(), arrival=None, name=None):
        return op("P", lambda: PE.matmul_mx(T["pb%d" % bank][:, 0:b - a], T[lq][:, la:la + 128], T[lp][:, la:la + 128],
                                            T[rq][:, a:b], T[rp][:, a:b], start, stop), r, (), (bank,), None, arrival,
                  "%d%s" % (bank, name or r[-1]))

    def dma(q, name, out, in_, r=(), w=()):
        return op(q, lambda: Q[q].dma_start(out, in_), r, w, (), "d_" + name, name=w[0] if w else name)

    def iota(out, pattern, base, cm, w):
        if out.dtype == dt.int32:
            return op("G", lambda: g.iota(out, pattern, base, cm), (), w)
        return op("G", lambda: g.iota(out, pattern, base, cm, allow_small_or_imprecise_dtypes=True), (), w)

    def asel(out, in_, pattern, cmp, fill, base, cm, r, w):
        return op("G", lambda: g.affine_select(out, in_, pattern, cmp, fill, base, cm), r, w)

    xa = PP[1]
    dma("S", "c1", T.c1i[:], T.c1[:], w=["c1i"])
    dma("Y", "x0", T.xa[:, 0:4 * xa], T.x[:, 0:4 * xa], w=["xa0"])
    dma("Y", "x1", T.xa[:, 4 * xa:], T.x[:, 4 * xa:], w=["xa1"])
    dma("Y", "c2", T.c2i[:], T.c2[:], ["xa1"], ["c2i"])
    dma("Y", "wc", T.wq[:].bitcast(dt.uint8), T.wc[:], ["xa1"], ["wq"])
    dma("Y", "ws", T.wp[:], T.ws[:], ["xa1"], ["wp"])
    dma("Y", "v", T.vt[:], T.v[:], ["xa1"], ["vt"])

    op("V", lambda: V.memset(T.one[:], 1.0), w=["one"])
    op("V", lambda: V.memset(T.bt[:], 0.0), w=["bt"])
    iota(T.pi[:], [[0, 2]], 0, 1, ["pi"])
    iota(T.urow[:], [[16, 2]], 0, 0, ["urow"])
    iota(T.bd[:], [[1, 8], [0, 64]], 0, 0, ["bd"])
    iota(T.i16[:], [[0, MA // 16], [1, 16]], 0, 0, ["i16"])
    iota(T.ib[:], [[1, HC]], 0, 0, ["ib"])
    asel(T.keep[:], T.one[:, 0:MA], [[0, MA // 16], [1, 16]], A.not_equal, 0.0, 0, 0, ["one"], ["keep"])
    iota(T.ifl[:], [[1, C]], 0, 0, ["ifl"])
    iota(T.sl[:, 0:64], [[32, 2], [1024, 2], [2, 16]], 0, 0, ["sl0"])
    iota(T.sl[:, 64:128], [[-32, 2], [1024, 2], [-2, 16]], 62, 0, ["sl1"])
    asel(T.k32[:], T.one[:, 0:64], [[0, 2], [1, 32]], A.not_equal, 0.0, 0, 0, ["one"], ["k32"])
    iota(T.tab[:, 0:4], [[1, 4]], 2 * C, 0, ["ta"])
    iota(T.tab[:, 4:8], [[1, 4]], 2 * (H - 1), 0, ["tb"])
    iota(T.i4[:], [[0, K4], [1, 4]], 0, 0, ["i4"])
    asel(T.keep4[:], T.one[:, 0:C], [[0, K4], [1, 4]], A.not_equal, 0.0, 0, 0, ["one"], ["keep4"])
    iota(T.kap[:], [[-1, W // 4], [0, 4]], W // 4, 0, ["kap"])
    asel(T.kap[:], T.kap[:], [[0, W // 4], [1, 4]], A.is_equal, 1024.0, 0, 0, ["kap"], ["kap"])
    for b in range(4):
        asel(T.et[:, 512 * b:512 * (b + 1)], T.one[:], [[-1, 128], [1000, 4]], A.is_equal, 0.0, -1000 * b, 1,
             ["one"], ["et%d" % b])

    ts(T.pqi[:, 0:2], T.pi[:], 2, 3, A.logical_shift_right, A.bitwise_and, ["pi"], ["pqi0"])
    ts(T.pqi[:, 2:4], T.pi[:], 3, None, A.bitwise_and, r=["pi"], w=["pqi1"])
    ts(T.pqi[:, 4:6], T.pi[:], 4, None, A.logical_shift_right, r=["pi"], w=["pqi2"])
    ts(T.pqi[:, 6:8], T.pi[:], 15, None, A.bitwise_and, r=["pi"], w=["pqi3"])
    ts(T.pqi[:, 8:10], T.pi[:], 4, 1, A.logical_shift_right, A.bitwise_and, ["pi"], ["pqi4"])
    cp(T.pqf[:], T.pqi[:], ["pqi%d" % i for i in range(5)], ["pqf"])
    pe, pg, pmf = T.pqf[:, 2:3], T.pqf[:, 4:5], T.pqf[:, 6:8]
    act(T.nb[:, 0:2], T.pqf[:, 0:7:6], ACT.Copy, ["pqf"], ["nb"], scale=-BIG)
    act(T.scol[:], T.urow[:], ACT.Identity, ["urow", "pqf"], ["scol"], bias=T.pqf[:, 6:7])
    act(T.nth[:, 0:2], pmf, ACT.Identity, ["pqf"], ["nth"], scale=-1.0, bias=-0.9375)
    act(T.nth[:, 2:4], T.pqf[:, 8:10], ACT.Copy, ["pqf"], ["far"], scale=-1024.0)
    act(T.k2[:], T.scol[:], ACT.Identity, ["scol"], ["k2"], scale=-2.0, bias=-1.0)
    act(T.nscol[:], T.scol[:], ACT.Copy, ["scol"], ["nscol"], scale=-1.0 / 64)
    cp(T.ido[:], T.scol[:], ["scol"], ["ido"])
    for t in range(4):
        ts(T.o1[:, 2 * KC * t:2 * KC * (t + 1)], T.c1i[:], 4.0, float(t), A.mult, A.add, ["c1i"], ["o1%d" % t])
    ts(T.pm1[:, 0:512], T.bd[:], pg, None, A.is_equal, r=["bd", "pqf"], w=["pm10"])
    act(T.pm1[:, 512:1024], T.pm1[:, 0:512], ACT.Copy, ["pm10"], ["pm11"], scale=-1.0)
    ts(T.t1[:], T.c1i[:], float(HC), -float(HC), A.is_ge, A.mult, ["c1i"], ["t1"])
    ts(T.pw[:, 1:4 * KC:2], T.c1i[:], float(HC), 1.0 / 512, A.is_ge, A.max, ["c1i"], ["pw1"])
    quant("oq", "op", "pm1", 0, 256, ["pm10", "pm11"], ["oq"])
    tt(T.pw[:, 0:4 * KC:2], T.t1[:], T.c1i[:], A.add, ["c1i", "t1"], ["pw0"])
    act(T.thr[:], T.i16[:], ACT.Abs, ["i16", "nb"], ["thr"], scale=BIG, bias=T.nb[:, 1:2])
    cp(T.xd[:], T.xa[:, 0:4 * xa], ["xa0"], ["xd0", "xd1"])
    phase[0] = "p0"
    tt(T.dp[:], T.pw[:, 2 * KC:], T.pw[:, :2 * KC], A.subtract, ["pw0", "pw1"], ["dp"])

    zk = ["z%d%d%d" % (k, h, t) for k in range(2) for h in range(3) for t in range(4)]

    def compare(P, X, xk, first, fkey, parts, thr, carry, lists):
        for h, (a, b) in enumerate(pieces(P)):
            for k in range(2):
                o = 2 * a + (k if h == 0 else 1 - k) * (b - a)
                zs = ["z%d%d%d" % (k, h, t) for t in range(4)]
                if h == 0 and k == 0:
                    for t, step, ap, keys in parts(k, a, b):
                        tt(T.z[:, t:4 * b:step], ap, T[first][:, t:4 * b:step], A.mult, keys + fkey,
                           zs[t:t + 1] if step > 1 else zs)
                else:
                    got = ["pre%d%d%d" % (k, h, t) for t in range(4)]
                    for t, step, ap, keys in parts(k, a, b):
                        act(T.pre[:, 4 * o + t:4 * (o + b - a):step], ap, ACT.Copy, keys, got[t:t + 1] if step > 1 else got)
                    n = 2 if h == 1 else 1
                    for i in range(n):
                        c, d = 4 * i * (b - a) // n, 4 * (i + 1) * (b - a) // n
                        tt(T.z[:, 4 * o + c:4 * o + d], T.pre[:, 4 * o + c:4 * o + d], T[X][:, 4 * a + c:4 * a + d],
                           A.mult, xk + got, zs[4 // n * i:4 // n * (i + 1)])
                quant("zq", "zp", "z", o, o + b - a, zs, ["zq%d%d" % (k, h)])
                mm(h, "oq", "op", 128 * (1 - k), "zq", "zp", o, o + b - a, k == 0, k == 1, ["oq", "zq%d%d" % (k, h)])
            tt(T.mask[:, a:b], T["pb%d" % h][:, 0:b - a], T[thr][:, 0:b - a], A.is_gt, [thr], ["mask%d" % h], [h])
            run, o0, first0 = carry(h)
            scan(T.msc[:, a:b], T[run][:, 0:b - a], T.mask[:, a:b], o0, A.add, [run, "mask%d" % h], ["msc%d" % h], first0)
            lists(h, a, b)

    def fence(keys):
        before = set()
        for k in keys:
            if k in wrote:
                before.add(wrote[k])
            before.update(read.get(k, ()))
        for k in keys:
            read[k] = sorted(before)

    m16 = T.msc[:, 15:C:16]
    peers = [T.cores[(rank + i) % N] for i in range(1, N)]
    mask = topo.mask(core, peers[0])
    for c in peers:
        mask &= topo.mask(core, c)
    engines = bin(mask).count("1")
    dsts = [DstId(rid=topo.addr(c)[0], pnc=topo.addr(c)[1]) for c in peers]
    names = ["xa", "xb", "xc"]
    ta, tb = T.tab[:, 0:4], T.tab[:, 4:8]
    xk = ["xa0", "xa1"]
    shared = (zk + ["pre" + k[1:] for k in zk] + ["zq%d%d" % (k, h) for k in range(2) for h in range(3)]
              + ["mask%d" % h for h in range(3)] + ["msc%d" % h for h in range(3)])

    for rd in range(R):
        X, Xn = names[rd], names[rd + 1]
        bq, bp, lc, lp = "bq%d" % rd, "bp%d" % rd, "lc%d" % rd, "lp%d" % rd
        mk = ["msc%d" % h for h in range(len(PP) - 1)]
        phase[0] = "p%d" % rd

        def xparts(k, a, b):
            return [(t, 4, T[X][:, 0:4 * C].indirect(T.o1[:, KC * (2 * t + k) + a // 16:KC * (2 * t + k) + b // 16]),
                     xk + ["o1%d" % t]) for t in range(4)]

        def bins(h, a, b):
            m, c, d = T.msc[:, a + 15:b:16], a // 8, b // 8
            tt(T.tw[:, c:d:2], m, T.dp[:, c:d:2], A.mult, ["msc%d" % h, "dp"], ["tw0%d" % h])
            tt(T.tw[:, c + 1:d:2], m, T.dp[:, c + 1:d:2], A.mult, ["msc%d" % h, "dp"], ["tw1%d" % h])
            tt(T.hw[:, c:d], T.tw[:, c:d], T.pw[:, c:d], A.add, ["tw0%d" % h, "tw1%d" % h, "pw0", "pw1"], ["hw%d" % h])
            for c in range(a // 16, b // 16):
                s, t = divmod(c, 4)
                row = T.oh[:, 4 * HC * s + t:4 * HC * (s + 1):4]
                place, weight = T.hw[:, 2 * c:2 * c + 1], T.hw[:, 2 * c + 1:2 * c + 2]
                if c < NS:
                    off = T.ab[:, HC * c:HC * (c + 1)]
                    act(off, T.ib[:], ACT.Abs, ["ib", "hw%d" % h], ["ab%d" % c], bias=place, scale=-1.0)
                    act(row, off, ACT.Relu, ["ab%d" % c, "hw%d" % h], ["oh%d" % c], bias=weight, scale=-1.0)
                else:
                    ts(row, T.ib[:], place, weight, A.is_equal, A.mult, ["ib", "hw%d" % h], ["oh%d" % c])

        fence(shared)
        compare(PP, X, xk, "xd", ["xd0", "xd1"], xparts, "thr", lambda h: ("keep", A.mult, 0.0), bins)
        for s in SUMS:
            quant("ohq", "ohp", "oh", HC * s, HC * (s + 1), ["oh%d" % (4 * s + t) for t in range(4)], ["ohq%d" % s])
            for bank in (3, 4):
                mm(bank, "oq", "op", 0, "ohq", "ohp", HC * s, HC * (s + 1), s == SUMS[0], s == SUMS[-1], ["oq", "ohq%d" % s])
        if rd == 0:
            for i in range(2):
                act(T.sl[:, 64 * i:64 * (i + 1)], T.sl[:, 64 * i:64 * (i + 1)], ACT.Abs, ["sl%d" % i, "far"], ["sl%d" % i],
                    bias=T.nth[:, 2:3])
            act(T.bt2[:, 0:64], T.sl[:, 0:64], ACT.Identity, ["sl0"], ["bdt"], bias=-float(C))
            act(T.bt2[:, 64:128], T.sl[:, 64:128], ACT.Identity, ["sl1"], ["bdy"], scale=-1.0, bias=62.0)
            tt(T.dc[:], T.c1i[:, KC:], T.c1i[:, :KC], A.subtract, ["c1i"], ["dc"])
        else:
            quant("vq", "vp", "vt", 0, 128, ["vt"], ["vq"])

        nth, a0, a1, aa = T.nth[:, 0:1], T.acc[:, 0:1], T.acc[:, 1:2], T.acc[:, 2:3]
        ts(T.deg[:, HC:], T.pb3[:, 0:HC], -0.4375, None, A.add, w=["deg1"], ps=[3])
        act(T.junk[:, HC:C], T.pb4[:, 0:HC], ACT.Sign, ["nth"], ["j01", "acc1"], [4], bias=nth, accum_out=a1)
        tt(T.lo[:], T.pb3[:, 0:HC], T.deg[:, HC:], A.subtract, ["deg1"], ["lo"], [3])
        act(T.junk[:, 0:HC], T.lo[:], ACT.Sign, ["lo", "nth"], ["j00", "acc0"], bias=nth, scale=512.0, accum_out=a0)
        ts(T.cls[:, HC:], T.deg[:, HC:], 16.0, None, A.min, r=["deg1"], w=["cls1"])
        ts(T.cls[:, :HC], T.lo[:], 512.0, 16.0, A.mult, A.min, ["lo"], ["cls0"])
        if rd == 0:
            cp(T.c2u[:], T.c2i[:], ["c2i"], ["c2u"])
            act(T.diag[:], T.thr[:, 0:H], ACT.Relu, ["thr"], ["diag"], scale=-1.0, bias=1.0)
            for u in range(2):
                act(T.srow[:, H * u:H * (u + 1)], T.ifl[:, 0:H], ACT.Identity, ["ifl", "nscol"], ["srow%d" % u],
                    scale=1.0 / 64, bias=T.nscol[:, u:u + 1])
            act(T.c2row[:], T.ifl[:, 0:NH].indirect(T.c2u[:]), ACT.Copy, ["ifl", "c2u"], ["c2row"])
        ts(T.th[:, 0:64], T.bt2[:, 0:64], a0, a1, A.subtract, A.is_lt, ["bdt", "acc0", "acc1"], ["th0"])
        ts(aa, a0, a1, float(C), A.add, A.add, ["acc0", "acc1"], ["aa"])
        turn(T.tht[:, 0:64], T.th[:, 0:64], ["th0"], ["tht0"])
        ts(T.th[:, 64:128], T.bt2[:, 64:128], aa, aa, A.is_ge, A.mult, ["bdy", "aa"], ["th1"])
        scan(T.csc[:], T.k32[:], T.tht[:, 0:64], A.mult, A.add, ["k32", "tht0"], ["csc"])
        turn(T.tht[:, 64:128], T.th[:, 64:128], ["th1"], ["tht1"])
        cl = ["cls0", "cls1", "csc"]
        ts(T.ind[:, 0:C], T.cls[:], T.csc[:, 31:32], None, A.is_equal, r=cl, w=["ind0"])
        scan(T.ysc[:], T.k32[:], T.tht[:, 64:128], A.mult, A.max, ["k32", "tht1"], ["ysc"])
        scan(T.cum[:, 0:C], T.ind[:, 0:C], T.ind[:, 0:C], A.add, A.max, ["ind0"], ["cum0"])
        tt(T.bias[:], T.ysc[:, 31:64:32], T.k2[:], A.add, ["ysc", "k2"], ["bias"])
        ts(T.ind[:, C:], T.cls[:], T.csc[:, 63:64], None, A.is_equal, r=cl, w=["ind1"])
        act(T.junk[:, C:2 * C], T.cum[:, 0:C], ACT.Sign, ["cum0", "bias"], ["j10", "accc0"],
            bias=T.bias[:, 0:1], scale=2.0, accum_out=T.accc[:, 0:1])
        tt(T.pt[:], m16, T.dc[:], A.mult, mk + ["dc"], ["pt"])
        scan(T.cum[:, C:], T.ind[:, C:], T.ind[:, C:], A.add, A.max, ["ind1"], ["cum1"])
        act(T.junk[:, 2 * C:3 * C], T.cum[:, C:], ACT.Sign, ["cum1", "bias"], ["j11", "accc1"],
            bias=T.bias[:, 1:2], scale=2.0, accum_out=T.accc[:, 1:2])
        ts(T.deg[:, :HC], T.lo[:], 512.0, None, A.mult, r=["lo"], w=["deg0"])
        tt(T.pt[:], T.pt[:], T.c1i[:, :KC], A.add, ["pt", "c1i"], ["pt"])

        a_0, a_1 = T.accc[:, 0:1], T.accc[:, 1:2]
        ts(T.h4[:, 0:8:2], ta, a_0, a_0, A.subtract, A.subtract, ["accc0", "ta"], ["h40"])
        cp(T.pu[:], T.pt[:], ["pt"], ["pu"])
        ts(T.hu[:], T.accc[:], -0.5, float(HC), A.mult, A.add, ["accc0", "accc1"], ["hu"])
        ts(T.h4[:, 1:8:2], ta, a_1, a_1, A.subtract, A.subtract, ["accc1", "ta"], ["h41"])
        dk = ["deg0", "deg1", "hu"]
        tt(T.dm[:], T.deg[:, 0:C].indirect(T.hu[:]), T.diag[:], A.mult, dk + ["diag"], ["dm"])
        act(T.bu[:], T[X][:, 0:4 * C].indirect(T.h4[:]), ACT.Copy, xk + ["h40", "h41"], ["bu"])
        tt(T.kr[:, 0:H], T.deg[:, 0:C].indirect(T.hu[:]), T.srow[:, 0:H], A.subtract, dk + ["srow0"], ["kr0"])
        scan(T.dsc[:], T.keep[:, 0:H], T.dm[:], A.mult, A.subtract, ["keep", "dm"], ["dsc"])
        tt(T.kr[:, H:], T.deg[:, 0:C].indirect(T.hu[:]), T.srow[:, H:], A.subtract, dk + ["srow1"], ["kr1"])
        for u in range(2):
            act(T.junk[:, 3 * C + H * u:3 * C + H * (u + 1)], T.kr[:, H * u:H * (u + 1)], ACT.Sign, ["kr%d" % u, "dsc"],
                ["j3%d" % u, "rank%d" % u], bias=T.dsc[:, 16 * u + 15:16 * u + 16], accum_out=T.rank[:, u:u + 1])
        for u in range(2):
            ts(T.r4[:, u:8:2], tb, T.rank[:, u:u + 1], T.rank[:, u:u + 1], A.add, A.add, ["tb", "rank%d" % u], ["r4%d" % u])
        cp(T.bt[:, 0:4 * H].indirect(T.r4[:]), T.bu[:], ["r40", "r41", "bu"], ["bt"])
        quant(bq, bp, "bt", 0, 128, ["bt"], [bq], "bq")

        a, b = H * rank, H * (rank + 1)

        def send(src, land, arr=T.sem["arr%d" % rd]):
            g.remote_dma_fused([RemoteDMATransfer(dst_ids=dsts, dma_engine_mask=mask, remote_sem=arr, src=src,
                                                  dsts=[land for c in peers])], local_sem=T.sem.sent)
            return engines
        for src, land in ((T[bq][:, 0:H].bitcast(dt.uint8), T[lc][:, a:b].bitcast(dt.uint8)), (T[bp][:, 0:H], T[lp][:, a:b])):
            op("G", lambda src=src, land=land, send=send: send(src, land), [bq], (), (), "sent", name="send")
        read[bq] = []

        act(T.a1row[:], T.c2row[:, 0:C].indirect(T.pu[:]), ACT.Copy, ["c2row", "pu"], ["a1row"])
        act(T.hrow[:], T.ifl[:, 0:C].indirect(T.hu[:]), ACT.Copy, ["ifl", "hu"], ["hrow"])
        if rd == 0:
            act(T.thr4[:], T.i4[:], ACT.Abs, ["i4", "nb"], ["thr4"], scale=BIG, bias=T.nb[:, 0:1])
            act(T.kap[:], T.kap[:], ACT.Copy, ["kap"], ["kap"], scale=4.0 / W)
            act(T.nb[:, 2:4], pmf, ACT.Identity, ["pqf"], ["beta"], bias=8.0 * W)
            act(T.diag4[:], T.thr4[:], ACT.Relu, ["thr4"], ["diag4"], scale=-1.0, bias=1.0)
        for i in range(2):
            act(T.xh[:, 2 * C * i:2 * C * (i + 1)], T[X][:, 2 * C * i:2 * C * (i + 1)], ACT.Copy, xk, ["xh%d" % i], scale=0.5)
        cp(T[lc][:, a:b].bitcast(dt.uint32), T[bq][:, 0:128].bitcast(dt.uint32).indirect(T.ido[:]), [bq, "ido"], [lc], "lc")
        cp(T[lp][:, a:b], T[bp][:, 0:128].indirect(T.ido[:]), [bq, "ido"], [lp], "lp")
        ts(T.ru[:], T.rank[:], 0.5, (H - 1) / 2, A.mult, A.add, ["rank0", "rank1"], ["ru"])
        if rd == 0:
            quant("eq", "ep", "et", 0, 512, ["et%d" % i for i in range(4)], ["eq"])
        cp(T.hs[:, H * rd:H * (rd + 1)].indirect(T.ru[:]), T.hrow[:], ["ru", "hrow"], ["hs%d" % rd], "hs")
        if rd == 0:
            tt(T.am[:], T.c2row[:], T.diag4[:], A.mult, ["c2row", "diag4"], ["am"])
        else:
            dma("Y", "hl", T.hl[:], T.hs[0:128:16, :], ["hs0", "hs1"])
        tt(T.an[:], T.a1row[:], T.diag4[:], A.mult, ["a1row", "diag4"], ["an"])
        if rd == 0:
            scan(T.c2s[:], T.keep4[:], T.am[:], A.mult, A.add, ["keep4", "am"], ["c2s"])
        scan(T.asc[:], T.keep4[:], T.an[:], A.mult, A.add, ["keep4", "an"], ["asc"])
        if rd == 0:
            ts(T.a0u[:], T.c2s[:, 3:C:4], 4.0, pe, A.mult, A.add, ["c2s", "pqf"], ["a0u"])
        ts(T.a1u[:], T.asc[:, 3:C:4], 4.0, pe, A.mult, A.add, ["asc", "pqf"], ["a1u"])
        tt(T.da[:, 0:PS[1] // 4], T.asc[:, 3:PS[1]:4], T.c2s[:, 3:PS[1]:4], A.subtract, ["asc", "c2s"], ["da"])

        phase[0] = "s%d" % rd
        for i in range(4):
            mm(4 + i, "eq", "ep", 128 * i, lc, lp, 0, NH, True, True, ["eq", lc, lp],
               ("arr%d" % rd, 2 * engines * len(peers)), "lp")
        for i in range(4):
            scaled("SV"[i % 2], T.ft[:, i:4 * NH:4], T["pb%d" % (4 + i)][:, 0:NH], 1.0, ["ft%d" % i], [4 + i])
        fk = ["ft%d" % i for i in range(4)]

        def fparts(k, a, b):
            off = "a%du" % k
            return [(0, 1, T.ft[:, 0:4 * NH].indirect(T[off][:, a // 4:b // 4]), fk + [off])]

        def chosen(h, a, b):
            c, d = a // 4, b // 4
            if h == 0:
                tt(T.at[:, c:d], T.msc[:, a + 3:b:4], T.da[:, c:d], A.mult, ["msc0", "da"], ["at0"])
                tt(T.at[:, c:d], T.at[:, c:d], T.c2s[:, a + 3:b:4], A.add, ["at0", "c2s"], ["at0"])
                ts(T.au[:, c:d], T.at[:, c:d], 4.0, pe, A.mult, A.add, ["at0", "pqf"], ["au0"])
                win, keys = T.ft[:, 0:4 * NH], fk
            else:
                ts(T.au[:, c:d], T.msc[:, a + 3:b:4], -4.0 * W, T.nb[:, 2:3], A.mult, A.add, ["msc%d" % h, "beta"], ["au%d" % h])
                win, keys = T.pre[:, 8 * a:8 * b], ["pre0%d0" % h, "pre1%d0" % h]
            act(T.fm[:, 4 * a:4 * b], win.indirect(T.au[:, c:d]), ACT.Copy, keys + ["au%d" % h], ["fm%d" % h], scale=0.5)
            tt(T.mt[:, 4 * a:4 * b], T.fm[:, 4 * a:4 * b], T.xh[:, 4 * a:4 * b], A.add, ["xh0", "xh1", "fm%d" % h], ["mt%d" % h])

        fence(shared)
        compare(PS, X, xk, X, xk, fparts, "thr4", lambda h: ("kap", A.min, 4.0) if h else ("keep4", A.mult, 0.0), chosen)

        xk = []
        for h, (a, b) in enumerate(pieces(PS)):
            quant("mq", "mp", "mt", a, b, ["mt%d" % h], ["mq%d" % h])
            for i in range(4):
                mm(BANKS[4 * h + i], "wq", "wp", 128 * i, "mq", "mp", a, b, True, True, ["wq", "wp", "mq%d" % h])
            ks = ["%s%d%d" % (Xn, h, i) for i in range(4)]
            for i in range(4):
                bank = BANKS[4 * h + i]
                scaled(EVAC[4 * h + i], T[Xn][:, 4 * a + i:4 * b:4], T["pb%d" % bank][:, 0:b - a], 0.03125, ks[i:i + 1], [bank],
                       "xn%d%d" % (h, i))
            xk = xk + ks
            if rd < R - 1 and a < xa:
                e = min(b, xa)
                cp(T.xd[:, 4 * a:4 * e], T[Xn][:, 4 * a:4 * e], ks, ["xd%d" % h])
            if rd == R - 1:
                bank = YB[h]
                quant("xq", "xp", Xn, a, b, ks, ["xq%d" % h])
                mm(bank, "vq", "vp", 0, "xq", "xp", a, b, True, True, ["vq", "xq%d" % h])
                dma("Y", "oc%d" % h, T.oc[:, 4 * a:4 * b], T.xq[:, a:b].bitcast(dt.uint8), ["xq%d" % h])
                scaled("V" if b == C else "S", T.yt[:, a:b], T["pb%d" % bank][:, 0:b - a], 1.0, ["yt%d" % h], [bank])
                dma("Y", "y%d" % h, T.y[:, a:b], T.yt[:, a:b], ["yt%d" % h])
    for k in range(4):
        dma("S", "os%d" % k, T.osc[4 * k:4 * k + 4, :], T.xp[32 * k:32 * k + 4, :], ["xq%d" % h for h in range(len(PS) - 1)])
    issue(planned())
